import numpy as np, ml_dtypes
CORES = [3,11,19,27,35,43,51,59]
N = 8
BF = ml_dtypes.bfloat16
W, P, RO, L = 2048, 2, 4, 256
Q = 0.673
def parts(rng):
    share = rng.choice(np.array([0.015, 0.025, 0.04]), (N, 8, 1, 1)) * Q
    r = np.where(rng.random((N, 8, 16, W)) < share, rng.integers(5, 16, (N, 8, 16, W)), rng.integers(0, 5, (N, 8, 16, W)))
    hot = (rng.random((N, 8, 1, W)) < 0.004 * Q) & (rng.random((N, 8, 16, W)) < 0.7)
    r = np.where(hot, 15, r)
    return r, rng.integers(0, 256, (N, 8, 16, W)), rng.integers(0, W, (N, 8, 16, W)), rng.integers(0, W, (N, 8, 16, L))
def pack(r, x, k, s):
    return {"rec": np.ascontiguousarray(r.reshape(N, 128, W)).astype(np.float32).astype(BF), "wealth": np.ascontiguousarray(x.reshape(N, 128, W)).astype(np.float32).astype(BF),
            "kin": np.ascontiguousarray(k.reshape(N, 128, W)).astype(np.int32), "slips": np.ascontiguousarray(s.reshape(N, 128, L)).astype(np.int32)}
def setup_inputs(rng):
    r, x, k, s = parts(rng)
    return pack(r, x, k, s)
def setup_inputs_spread(rng):
    e = np.exp2(4.3 + 3.9 * rng.random((N, 8, 16, 1))) / Q
    r = np.minimum((16 * rng.random((N, 8, 16, W)) ** e).astype(np.int64), 15)
    x = np.minimum((np.exp2(8 * rng.random((N, 8, 1, W))) * rng.random((N, 8, 16, W))).astype(np.int64), 255)
    k = np.minimum((W * rng.random((N, 8, 16, W)) ** 2).astype(np.int64), W - 1)
    s = np.minimum((W * rng.random((N, 8, 16, L)) ** (1 + rng.random((N, 8, 1, L)))).astype(np.int64), W - 1)
    return pack(r, x, k, s)
def setup_inputs_ends(rng):
    r = 15 * (rng.random((N, 8, 16, W)) < 0.02 * Q)
    r = np.where(rng.random((N, 8, 1, W)) < 0.004 * Q, 15, r)
    w = rng.random((N, 8, 1, W)); x = 255 * np.where(w < 0.4, 0, np.where(w < 0.7, 1, rng.integers(0, 2, (N, 8, 16, W))))
    u = rng.random((N, 8, 16, W))
    k = np.where(u < 0.36, 0, np.where(u < 0.72, W - 1, np.where(u < 0.78, W - 2, rng.integers(0, W, (N, 8, 16, W)))))
    for first, places in ((1, ((2, W - 2), (15, W - 1))), (3, ((4, W - 1), (9, 5), (12, 5))), (6, ((4, 5), (9, W - 1)))):
        c = np.zeros((16, 1), np.int64)
        for m, v in places: c[m, 0] = v
        k[:, :, :, first::8] = c; x[:, :, :, first::8] = 0
    m = (np.arange(W) & 4) == 4
    k[:, 7] = np.where(m & (k[:, 7] == W - 1), 0, k[:, 7])
    a, b = W - 600, W - 344
    k[:, :, :, a:b] = 0; r[:, :, :, a:b] = 0; x[:, :, :, a:b] = 0
    k[:, :, :, W - 40:W - 24] = 0; r[:, :, :, W - 40:W - 24] = 0; x[:, :, :, W - 40:W - 24] = 0; k[:, :, 15, W - 32:W - 24] = W - 1
    r[:, :, :, 0] = 0; r[:, :, :, W - 1] = 15 * (rng.random((N, 8, 16)) < rng.choice(np.array([0.05, 0.15, 0.3]), (N, 8, 1))); r[:, 7, :, W - 1] = 15
    r[:, :, :, W - 2] = 0; r[:, :, :, 5] = 0
    x[:, :, :, 0] = 0; x[:, :, :, W - 1] = 255; x[:, :, :, 5] = 255; x[:, :, :, W - 2] = 255; x[:, :, 15, W - 2] = 254
    u = rng.random((N, 8, 16, L)); s = np.where(u < 0.35, 0, np.where(u < 0.7, W - 1, rng.integers(1, W - 600, (N, 8, 16, L))))
    s[:, :, :, 112:128] = W - 1
    for q in range(2):
        for g in range(8): s[q, g, :, 240:] = a + rng.permutation(256).reshape(16, 16)
    p = np.arange(16); s[N - 1, 7, :, 255] = np.where((p & 1) == 0, W - 40 + (p >> 1), W - 32 + (p >> 1))
    return pack(r, x, k, s)
def setup_inputs_corners(rng):
    r, x, k, s = parts(rng); own = np.arange(W); lane = np.arange(L)
    k[:, :4] = own
    n = rng.choice(np.array([0, 1, 3, 7, 8, 9, 11, 12, 13, 16]), (1, 4, 1, W)); order = np.argsort(rng.random((1, 4, 16, W)), axis=2)
    high = np.where(rng.random((N, 4, 16, W)) < 0.7, 15, rng.integers(6, 16, (N, 4, 16, W)))
    low = np.where(rng.random((N, 4, 16, W)) < 0.15, 5, rng.integers(0, 5, (N, 4, 16, W)))
    high[:, 1] = 6; low[:, 1] = 5; high[:, 2] = 6 + (own & 7); low[:, 2] = 5 + (own & 7)
    r[:, :4] = np.where(order < n, high, low)
    s[:, :2] = lane + 256 * rng.integers(0, W // 256, (N, 2, 16, L))
    s[:, 4] = np.repeat(rng.integers(0, W, (N, 1, 16)), 16, axis=2)
    for q in range(N):
        if (q & 1) == 0: s[q, 5] = rng.integers(0, W)
        else: s[q, 5] = lane + 256 * rng.integers(0, W // 256, (16, L))
    k[:, 6] = rng.choice(np.array([0, W - 1, W // 2]), (N, 1, W))
    z = rng.integers(0, 3, (N, 16, W)); k[:, 7] = np.where(z == 0, 0, np.where(z == 1, W - 1, own))
    r[:, 6:, :, [0, W - 1, W // 2]] = np.where(rng.random((N, 2, 16, 3)) < 0.2, 15, rng.integers(0, 5, (N, 2, 16, 3)))
    s[:, 7] = np.where(rng.random((N, 16, L)) < 0.1, rng.choice(np.array([0, W - 1]), (N, 16, L)), s[:, 7])
    x[:, 1] = 255; x[:, 2] = 255 * rng.integers(0, 2, (N, 1, W))
    return pack(r, x, k, s)
def setup_inputs_alike(rng):
    r, x, k, s = parts(rng)
    pool = np.repeat(rng.integers(0, W, (N, 8, 16, 6)), 16, axis=2)
    few = np.take_along_axis(pool, rng.integers(0, 6, (N, 8, L, 16)), 3).transpose(0, 1, 3, 2)
    s[:, ::2] = few[:, ::2]
    s[:, 1::4, :, 1::2] = np.roll(s[:, 1::4, :, 0::2], 5, axis=2)
    s[:, 3] = W - 1 - rng.integers(0, 40, (N, 16, L))
    k[:, 1::2, 8:] = k[:, 1::2, :8]
    x = np.take_along_axis(rng.choice(np.array([0, 128, 255]), (N, 8, 16, 5)), rng.integers(0, 5, (N, 8, 1, W)), 3)
    return pack(r, x, k, s)
def setup_inputs_full(rng):
    r, x, k, s = parts(rng); own = np.arange(W); lane = np.arange(L); bag = (own >> 4) & 15
    z = 2 * rng.integers(0, 8, N) + 1
    r[:, :3] = rng.integers(0, 5, (N, 3, 16, W))
    even = own[(own & 16) == 0]; r[:, 1, bag[even], even] = 15; k[:, 1] = k[:, 1] | 16
    hot = np.repeat((bag[None, :] == z[:, None])[:, None, :], 8, axis=1)
    hot[:, :2, :256] = False; hot[:, 2, :256:2] = False
    r = np.where(hot[:, :, None, :], 15, r)
    named = np.take_along_axis(hot, k.reshape(N, 8, 16 * W), 2).reshape(N, 8, 16, W); k = np.where(named, k ^ 32, k)
    s[:, :3] = lane + 256 * rng.integers(0, W // 256, (N, 3, 16, L))
    inbag = (lane >> 4)[None, :] == z[:, None]
    first = np.arange(16)[:, None] == ((5 * (lane & 15)) & 15)[None, :]
    s = np.where(inbag[:, None, None, :], lane + 256 * np.where(first, 0, rng.integers(1, W // 256, (N, 8, 16, L))), s)
    return pack(r, x, k, s)
def check_inputs(d):
    bad = []
    for k, lo, hi in (("rec", 0, 15), ("wealth", 0, 255), ("kin", 0, W - 1), ("slips", 0, W - 1)):
        v = np.asarray(d[k]).astype(np.float64)
        if not (np.min(v) >= lo and np.max(v) <= hi): bad.append("range of " + k)
        elif np.any(v != np.floor(v)): bad.append("whole numbers of " + k)
    return bad
def reference(rec, wealth, kin, slips):
    R = rec.astype(np.float32).astype(np.int64).reshape(N, 8, 16, W); X = wealth.astype(np.float32).astype(np.int64).reshape(N, 8, 16, W)
    K = kin.astype(np.int64).reshape(N, 8, 16, W); S = slips.astype(np.int64).reshape(N, 8, 16, L)
    lane = np.arange(L); b = lane >> 4; j = lane & 15; a = np.zeros((N, 16), np.int64)
    lower = lane[None, :] < lane[:, None]
    def picks(tab, ks):
        return np.take_along_axis(tab, ks.reshape(8, 1, 16 * L), 2).reshape(8, 16, 16, L)
    for t in range(RO):
        T = 8 + t; later = []
        for r in range(N):
            o = (a[r][b] + 5 * j + t) & 15
            c = S[r][:, o, lane]
            ci = c[:, None, :]
            counts = ~np.any((c[:, :, None] == c[:, None, :]) & lower[None], axis=2)
            kc = np.take_along_axis(K[r], ci, 2)
            M = np.maximum(np.take_along_axis(R[r], ci, 2), np.max(picks(R[r], kc), axis=2))
            for u in range(P):
                q = (r + 1 + (P * t + u) % (N - 1)) % N
                M = np.maximum(M, np.max(picks(R[q], np.take_along_axis(K[q], ci, 2)), axis=2))
            f = np.sum(M >= T - 2, axis=1)
            bar = (M[:, b, lane] >= T - 3) | (f >= 8)
            barred = counts & bar; inst = counts & ~bar
            torn = inst | (barred & (f >= 12))
            nxt = np.zeros((8, L), bool); nxt[:, :L - 16] = torn[:, 16:]
            moved = barred & (f < 12) & ((f & 1) == 1) & nxt
            sc = np.sum(np.maximum(picks(X[r], kc) - np.take_along_axis(X[r], ci, 2)[:, :, None, :], 0), axis=1)
            best = np.take_along_axis(kc, np.argmax(sc, axis=1)[:, None, :], 1)[:, 0]
            new = np.where(torn | moved, best, c)
            new[:, 16:] = np.where(moved[:, :L - 16], c[:, :L - 16], new[:, 16:])
            later.append((o, c, inst, new))
        for r in range(N):
            o, c, inst, new = later[r]
            S[r][:, o, lane] = new
            gi, li = np.nonzero(inst)
            R[r][gi, b[li], c[gi, li]] = T
            K[r][gi, t, c[gi, li]] = c[gi, li ^ 1]
            a[r] = np.sum(inst.reshape(8, 16, 16), axis=(0, 2))
    return {"yr": R.reshape(N, 128, W).astype(np.float32).astype(BF), "ys": S.reshape(N, 128, L).astype(np.float32)}

@@ -1,0 +1,558 @@
+import math
+from concourse.bass import DstId, RemoteDMATransfer
+from concourse.mybir import dt, AluOpType as Op, ActivationFunctionType as Fn
+
+NR, RO, W, L = 8, 4, 2048, 256
+WX = W + L
+NCH, CH = 4, 64
+V_ASK = (0, 1)
+OWN_LAST = (3,)
+
+SCRATCH = {}
+
+
+def _s(name, cols, dtype="float32", where="sbuf"):
+    SCRATCH[name] = (where, [128, cols], dtype)
+
+
+for _n in ("E", "R"):
+    _s(_n, WX, "bfloat16")
+_s("X", W, "bfloat16")
+_s("K", WX, "int32")
+_s("SN", L, "int32")
+_s("IDX", W)
+for _n in ("GO", "GA0", "GA1", "Y", "XR"):
+    _s(_n, 16 * L, "bfloat16")
+for _n in ("KL", "AK0", "AK1"):
+    _s(_n, L, "uint16")
+_s("EQ", 2176, "bfloat16")
+LOG = {}
+
+
+def _many(base, names, cols, dtype="float32"):
+    _s(base, cols * len(names), dtype)
+    for i, n in enumerate(names):
+        LOG[n] = (base, cols * i, cols)
+
+
+_TT = range(RO)
+_TK = [(t, k) for t in range(RO) for k in range(2)]
+_many("CLB", ["CL%d" % t for t in _TT], 16, "uint16")
+_many("RQB", ["RQ%d%d" % x for x in _TK], 16, "uint16")
+_many("RSB", ["RS%d%d" % x for x in _TK], L, "bfloat16")
+_many("ASB", ["AS%d%d" % x for x in _TK], L, "bfloat16")
+_many("BMB", ["BM%d" % t for t in _TT], L)
+_many("BTB", ["BT%d" % t for t in _TT], L, "bfloat16")
+_many("TBF", ["TB%d" % t for t in _TT], L, "bfloat16")
+_many("ISB", ["IST%d" % t for t in _TT], 1)
+_many("NOB2", ["NOT%d" % t for t in _TT], 1)
+_many("DGB", ["DN%d" % t for t in range(3)] + ["DI%d" % t for t in range(3)], 128, "float16")
+_many("CSB", ["CST%d" % t for t in _TT], 2, "bfloat16")
+_many("PLB", ["PL%d" % t for t in _TT], 2)
+for _n in ("CREP", "KCF", "CSW", "LH", "SF"):
+    _s(_n, L, "float16")
+for _n in ("KV", "RM", "NI", "DK", "BK", "MS", "CS", "LH2", "XS", "RST", "JF", "BF", "DG", "NOB", "OB"):
+    _s(_n, L)
+for _n in ("RCE", "NVR", "MK0", "MK1", "NTH", "CK"):
+    _s(_n, L, "bfloat16")
+for _n in ("UT", "VT", "NT"):
+    _s(_n, L + 32, "bfloat16")
+_s("D", L, "int32")
+_s("D15", L, "int32")
+_s("CB", 128, "int32")
+for _n in ("IDF", "SH", "SHW", "PSW"):
+    _s(_n, 128)
+for _n in ("IDH", "IDS"):
+    _s(_n, 128, "float16")
+for _n in ("IDB", "BD", "W1", "W2", "O128", "IOS"):
+    _s(_n, 128, "bfloat16")
+_s("GF", 8)
+_s("GH", 8, "float16")
+_s("G8", 8, "int32")
+for _n in ("GBH", "GB4", "GB16", "GB32"):
+    _s(_n, 8, "bfloat16")
+_s("PC", 2, "int32")
+_s("PM", 2, "int32")
+_s("SMI", 8, "int32")
+_s("PMF", 2)
+_s("PGF", 1)
+_s("SG", 1)
+_s("P15", 1, "bfloat16")
+_s("EXI", 16, "int32")
+_s("EXP", 16, "uint16")
+_s("SW", 16, "uint16")
+_s("SL", 16, "uint16")
+for _n in ("LIX", "LWB", "LW", "CWF", "CC", "DD", "SLM", "BKF", "DL", "DL1", "P2", "ED"):
+    _s(_n, 16)
+_s("D12", 32)
+_s("RMV", 32)
+_s("P1", 32)
+_s("RR", 2)
+_s("EQP", 2)
+_s("C48", 48, "bfloat16")
+_s("I48", 48, "bfloat16")
+for _n in ("FI", "Q1", "Q2"):
+    _s(_n, 48, "int32")
+for _n in ("TBB", "TORN", "OBB", "BO"):
+    _s(_n, 48)
+for _n in ("pZ", "pZ2", "pA", "pK", "pS", "pD", "pF", "pM"):
+    _s(_n, 512, "float32", "psum")
+
+SEMAPHORES = ["sv", "sa", "sp", "sq", "loc", "ldS", "ldK", "ldR", "ldX", "stR", "stS"]
+SEMAPHORES += ["rq%d%d" % (t, k) for t in range(RO) for k in range(2)] + ["rs%d%d" % (t, k) for t in range(RO) for k in range(2)]
+
+
+def rank_program(g, core, T, topo):
+    rank = T.rank_of(core)
+    if rank is None:
+        return
+    V, A, PE = g.vector, g.scalar, g.tensor
+    eng = {"v": V, "a": A, "p": PE, "q": g, "s": g.sync}
+    own = {"v": "sv", "a": "sa", "p": "sp", "q": "sq"}
+    cnt = {"v": 0, "a": 0, "p": 0, "q": 0}
+    known = {q: {} for q in eng}
+    snap = {}
+    res = {}
+
+    def need(q, tok):
+        s, n = tok
+        if known[q].get(s, 0) >= n:
+            return
+        eng[q].wait_ge(T.sem[s], n)
+        known[q][s] = n
+        for s2, n2 in snap.get(tok, {}).items():
+            if known[q].get(s2, 0) < n2:
+                known[q][s2] = n2
+
+    def entry(k):
+        if k not in res:
+            res[k] = {"w": None, "r": {}, "lw": {}}
+        return res[k]
+
+    def deps(q, reads, writes):
+        d = []
+        for k in reads:
+            e = entry(k)
+            if k[0] == "p":
+                d += [tok for q2, tok in e["lw"].items() if not (q2 == q == "p")]
+                d += [tok for q2, tok in e["r"].items() if q2 != q]
+            elif e["w"]:
+                d.append(e["w"])
+        for k in writes:
+            e = entry(k)
+            if k[0] == "p":
+                for m in ("lw", "r"):
+                    d += [tok for q2, tok in e[m].items() if not (q2 == q == "p")]
+            else:
+                if e["w"]:
+                    d.append(e["w"])
+                d += list(e["r"].values())
+        best = {}
+        for s, n in d:
+            best[s] = max(best.get(s, 0), n)
+        for s in best:
+            need(q, (s, best[s]))
+
+    def op(q, reads, writes, fn):
+        deps(q, reads, writes)
+        ins = fn()
+        cnt[q] += 1
+        tok = (own[q], cnt[q])
+        ins.then_inc(T.sem[own[q]], 1)
+        snap[tok] = dict(known[q])
+        for k in reads:
+            entry(k)["r"][q] = tok
+        for k in writes:
+            e = entry(k)
+            if k[0] == "p":
+                e["lw"][q] = tok
+            else:
+                e["w"] = tok
+                e["r"] = {}
+        return tok
+
+    def landed(k, sem, n):
+        entry(k)["w"] = (sem, n)
+
+    def ts(o, i, s1, s2, op0, op1=None, rd=()):
+        (on, oa), (inn, ia) = o, i
+        if op1 is None:
+            f = lambda: V.tensor_scalar(oa, ia, s1, None, op0)
+        else:
+            f = lambda: V.tensor_scalar(oa, ia, s1, s2, op0, op1)
+        return op("v", [inn] + list(rd), [on], f)
+
+    def tt(o, i0, i1, o0, rd=()):
+        return op("v", [i0[0], i1[0]] + list(rd), [o[0]], lambda: V.tensor_tensor(o[1], i0[1], i1[1], o0))
+
+    def cp(o, i, rd=()):
+        return op("v", [i[0]] + list(rd), [o[0]], lambda: V.tensor_copy(o[1], i[1]))
+
+    def act(o, i, fn=Fn.Copy, rd=(), **kw):
+        return op("a", [i[0]] + list(rd), [o[0]], lambda: A.activation(o[1], i[1], fn, **kw))
+
+    def mms(bank, parts, rd):
+        def f():
+            last = None
+            for (oa, l, r, st, sp) in parts:
+                last = PE.matmul(oa, l, r, st, sp)
+            return last
+        return op("p", rd, [bank], f)
+
+    def ap(name, lo=0, hi=None):
+        base, o, n = LOG.get(name, (name, 0, SCRATCH[name][1][1] if name in SCRATCH else 0))
+        return T[base][:, o + lo:o + (n if hi is None else hi)]
+
+    def b(name, lo=0, hi=None):
+        return (name, ap(name, lo, hi))
+
+    def iota(name, pattern, base, cm, imp=False):
+        kw = {"allow_small_or_imprecise_dtypes": True} if imp else {}
+        return op("q", [], [name], lambda: g.iota(T[name][:], pattern, base, cm, **kw))
+
+    def fill(name, val):
+        return op("v", [], [name], lambda: V.memset(ap(name), val))
+
+    g.sync.dma_start(T.SN[:], T.slips[:]).then_inc(T.sem.ldS, 16)
+    A.dma_start(T.R[:, 0:W], T.rec[:]).then_inc(T.sem.ldR, 16)
+    g.sync.dma_start(T.K[:, 0:W], T.kin[:]).then_inc(T.sem.ldK, 16)
+    A.dma_start(T.X[:], T.wealth[:]).then_inc(T.sem.ldX, 16)
+    landed("SN", "ldS", 16)
+    landed("R", "ldR", 16)
+    landed("K", "ldK", 16)
+    landed("X", "ldX", 16)
+
+    iota("PC", [[0, 2]], 0, 1)
+    iota("D", [[1, L]], 0, -1)
+    iota("JF", [[0, 16], [1, 16]], 0, 0, True)
+    iota("EXI", [[1, 16]], 0, 0)
+    iota("G8", [[1, 8]], 0, 0)
+    iota("CB", [[1, 8], [0, 16]], 0, 0)
+    iota("BF", [[1, 16], [0, 16]], 0, 0, True)
+    iota("LIX", [[128, 2], [0, 8]], W, 1, True)
+    iota("LWB", [[16, 16]], W, 0, True)
+    iota("IDX", [[1, W]], 0, 0, True)
+    ts(b("PM"), b("PC"), 15, None, Op.bitwise_and)
+    ts(b("SMI", 0, 1), b("PC", 0, 1), 4, None, Op.arith_shift_right)
+    cp(b("PMF"), b("PM"))
+    cp(b("PGF"), b("SMI", 0, 1))
+    ln2 = math.log(2.0)
+    act(b("P15"), b("PMF", 0, 1), Fn.Exp, scale=-ln2, bias=15.0 * ln2)
+    act(b("NTH"), b("JF"), Fn.Exp, scale=-ln2, bias=16.0 * ln2)
+    for nm in ("IDF", "IDB", "IDH"):
+        ts(b(nm), b("D", 0, 128), 0.0, None, Op.is_equal)
+    for t in range(RO):
+        ts(b("CST%d" % t), b("PMF"), 5.0, t - 7.5, Op.mult, Op.add)
+    ts(b("IOS"), b("JF", 0, 128), -7.5, None, Op.add)
+    cp(b("EXP"), b("EXI"))
+    ts(b("D15"), b("D"), 15, None, Op.bitwise_and)
+    ts(b("GF"), b("G8"), T.PGF[:, 0:1], None, Op.is_equal, rd=["PGF"])
+    ts(b("DG"), b("D15"), 0.0, None, Op.is_equal)
+    ts(b("RST"), b("JF"), 1.0, None, Op.min)
+    cp(b("GH"), b("GF"))
+    for t in range(RO - 1):
+        ts(b("IST%d" % t), b("PMF", 0, 1), float(t), None, Op.is_equal)
+        ts(b("NOT%d" % t), b("PMF", 0, 1), float(t), None, Op.not_equal)
+    ts(b("BD"), b("CB"), T.PGF[:, 0:1], None, Op.is_equal, rd=["PGF"])
+    for nm, f in (("GBH", 0.5), ("GB4", 4.0), ("GB16", 16.0), ("GB32", 32.0)):
+        ts(b(nm), b("GF"), f, None, Op.mult)
+    ts(b("IDS"), b("IDF"), 1.0 / 4096.0, None, Op.mult)
+    ts(b("SMI", 1, 2), b("PC", 0, 1), 1, None, Op.bitwise_and)
+    fill("O128", 1.0 / 128.0)
+    ts(b("SG"), b("SMI", 1, 2), -2.0, 1.0, Op.mult, Op.add)
+    fill("C48", 12.0)
+    ts(b("PSW"), b("D", 0, 128), T.SG[:, 0:1], None, Op.is_equal, rd=["SG"])
+    cp(b("SF"), b("SN"))
+    S = ("pS", T.pS[:, 256:512])
+    mms("pS", [(T.pS[:, 256 + 128 * h:384 + 128 * h], T.SF[:, 128 * h:128 * h + 128], T.IDH[:], True, True) for h in range(2)], ["SF", "IDH"])
+
+    MAG = 1.5 * 2.0 ** 27
+    LOC = {"n": 0}
+
+    def place(t):
+        mk = "MK%d" % (t % 2)
+        ts(b("RR"), ("pF", T.pF[:, 64:66]), MAG, -MAG, Op.add, Op.add)
+        for h in range(2):
+            ts((mk, T[mk][:, 128 * h:128 * h + 128]), b("IOS"), T.RR[:, h:h + 1], T.pF[:, 64 + h:65 + h], Op.add, Op.is_equal, rd=["RR", "pF"])
+
+    def sel1(t):
+        tt(b("MS"), S, b("MK%d" % (t % 2)), Op.mult)
+
+    def sel2(t):
+        op("v", ["RST", "MS"], ["CS"], lambda: V.tensor_tensor_scan(T.CS[:], T.RST[:], T.MS[:], 0.0, Op.mult, Op.add))
+        tt(b("PL%d" % t), ("pF", T.pF[:, 64:66]), b("RR"), Op.subtract)
+
+    def expand(out, src):
+        op("v", [src, "EXP", "DG"], [out], lambda: V.tensor_tensor(T[out][:], T[src][:].indirect(T.EXP[:]), T.DG[:], Op.mult))
+
+    def wrap(t):
+        mms("pM", [(T.pM[:, 16 + 8 * h:24 + 8 * h], T.LH[:, 128 * h:128 * h + 128], T.GH[:], True, True) for h in range(2)], ["LH", "GH"])
+
+    def send_list(t):
+        trs = []
+        for k in range(2):
+            dst = T.cores[(rank + 1 + ((2 * t + k) % 7)) % NR]
+            es = topo.engines(core, dst)
+            half = len(es) // 2
+            m = 0
+            for e in es[k * half:(k + 1) * half]:
+                m |= 1 << e
+            rid, pid, _x = topo.addr(dst)
+            trs.append(RemoteDMATransfer(dst_ids=[DstId(rid=rid, pnc=pid)], dma_engine_mask=m, remote_sem=T.sem["rq%d%d" % (t, k)],
+                                         src=ap("CL%d" % t), dst=ap("RQ%d%d" % (t, k))))
+            a = T.cores[(rank - 1 - ((2 * t + k) % 7)) % NR]
+            landed("RQ%d%d" % (t, k), "rq%d%d" % (t, k), len(topo.engines(a, core)) // 2)
+            LOC["n"] += half
+        deps("q", ["CL%d" % t], [])
+        g.remote_dma_fused(trs, local_sem=T.sem.loc)
+
+    def send_sums(t, k):
+        asker = T.cores[(rank - 1 - ((2 * t + k) % 7)) % NR]
+        rid, pid, _x = topo.addr(asker)
+        deps("q", ["AS%d%d" % (t, k)], [])
+        g.remote_dma(ap("RS%d%d" % (t, k)), ap("AS%d%d" % (t, k)), T.sem["rs%d%d" % (t, k)], T.sem.loc, pid, rid, topo.mask(core, asker))
+        LOC["n"] += len(topo.engines(core, asker))
+        q = T.cores[(rank + 1 + ((2 * t + k) % 7)) % NR]
+        landed("RS%d%d" % (t, k), "rs%d%d" % (t, k), len(topo.engines(q, core)))
+
+    mms("pF", [(T.pF[:, 64:66], T.IDB[:], ap("CST0"), True, True)], ["IDB", "CST0"])
+    place(0)
+    sel1(0)
+    sel2(0)
+    cp(b("CC"), ("CS", T.CS[:, 15::16]))
+    expand("LH", "CC")
+    wrap(0)
+    cp(b("CL0"), ("pM", T.pM[:, 16:32]))
+    send_list(0)
+
+    act(("E", T.E[:, 0:W]), ("R", T.R[:, 0:W]), Fn.Exp, scale=6.0 * ln2)
+    for t in range(RO - 1):
+        act(b("DN%d" % t), b("IDF"), Fn.Identity, rd=["NOT%d" % t], scale=ap("NOT%d" % t))
+        act(b("DI%d" % t), b("IDF"), Fn.Identity, rd=["IST%d" % t], scale=ap("IST%d" % t))
+    ts(b("SH"), b("D", 0, 128), 16.0, None, Op.is_equal)
+    ts(b("SHW"), b("D", 0, 128), -112.0, None, Op.is_equal)
+    ts(b("CK"), b("JF"), -1.0, 15.0, Op.mult, Op.add)
+    for nm, x in (("UT", -1.0), ("VT", 0.0), ("NT", 1.0)):
+        fill(nm, x)
+    ts(b("LW"), b("LWB"), T.PMF[:, 0:1], None, Op.add, rd=["PMF"])
+    ts(b("NTH"), b("NTH"), -1.0, None, Op.mult)
+    ts(b("W2"), b("BD"), T.P15[:, 0:1], None, Op.mult, rd=["P15"])
+    ts(b("W1"), b("BD"), 65536.0, None, Op.mult)
+    ts(b("NOB"), b("BF"), T.PMF[:, 0:1], None, Op.not_equal, rd=["PMF"])
+    ts(b("OB"), b("BF"), T.PMF[:, 0:1], None, Op.is_equal, rd=["PMF"])
+    for t in range(RO):
+        ts(b("BM%d" % t), b("NOB"), 1e29, 64.0 ** (5 + t), Op.mult, Op.add)
+        if t < RO - 1:
+            ts(b("BT%d" % t), b("OB"), 64.0 ** (8 + t), None, Op.mult)
+        ts(b("TB%d" % t), b("OB"), float(8 + t), None, Op.mult)
+
+    def rec_piece(q, G, lst, c):
+        o, off = T[G][:, 1024 * c:1024 * c + 1024], T[lst][:, CH * c:CH * c + CH]
+        key = "%s.%d" % (G, c)
+        if q == "a":
+            op("a", ["E", lst], [key], lambda: A.activation(o, T.E[:, 0:W].indirect(off), Fn.Copy))
+        else:
+            op("v", ["E", lst], [key], lambda: V.tensor_copy(o, T.E[:, 0:W].indirect(off)))
+
+    def rec_sum(bank, col, G, c, whole):
+        parts = []
+        for m in range(16):
+            parts.append((T[bank][:, col:col + CH], T.IDB[:], T[G][:, 1024 * c + m:1024 * c + 1024:16], whole and m == 0, whole and m == 15))
+        mms(bank, parts, ["%s.%d" % (G, c), "IDB"])
+
+    def own_sum(c):
+        rec_sum("pZ2" if c >= NCH // 2 else "pZ", CH * (c % (NCH // 2)), "GO", c, False)
+
+    def both(src, first, fin):
+        for h, z in ((0, "pZ"), (1, "pZ2")):
+            mms(z, [(T[z][:, 0:128], T.IDB[:], ap(src, 128 * h, 128 * h + 128), first, fin)], ["IDB", src])
+
+    def kin_gather(out, lst):
+        op("v", ["K", lst], [out], lambda: V.tensor_copy(T[out][:], T.K[:, 0:W].indirect(ap(lst))))
+
+    def scatter_R():
+        op("v", ["NVR", "SL"], ["R"], lambda: V.tensor_copy(T.R[:].indirect(T.SL[:]), T.NVR[:]))
+
+    def update_S(t):
+        mk = "MK%d" % (t % 2)
+        op("v", ["DL", "EXP", mk], ["XS"], lambda: V.tensor_tensor(T.XS[:], T.DL[:].indirect(T.EXP[:]), T[mk][:], Op.mult))
+        tt(S, S, b("XS"), Op.add)
+
+    def fparts(tile, w, which, fin=False):
+        return [(T.pF[:, 16 * (s + 1) + 8 * h:16 * (s + 1) + 8 * h + 8], T[tile][:, 16 + 128 * h + 16 * s:144 + 128 * h + 16 * s], T[w][:], False, fin and n == len(which) - 1)
+                for n, (h, s) in enumerate(which)]
+
+    LOW, HIGH, MIXED = [(0, -1), (0, 0)], [(1, 0), (1, 1)], [(0, 1), (1, -1)]
+
+    def compare_lanes():
+        o = 0
+        for bb in range(16):
+            n = L - 16 * bb
+            ts(("EQ.%d" % bb, T.EQ[:, o:o + n]), ("CREP", T.CREP[:, 16 * bb:L]), T.CWF[:, bb:bb + 1], None, Op.is_equal, rd=["CWF"])
+            o += n
+
+    def count_lanes(lo, hi):
+        if lo == 0:
+            mms("pD", [(T.pD[:, 0:L], T.IDB[:], T.NTH[:], True, False)], ["IDB", "NTH"])
+        for bb in range(lo, hi):
+            n = L - 16 * bb
+            o = sum(L - 16 * x for x in range(bb))
+            parts = [(T.pD[:, 16 * bb:16 * bb + 16], T.W2[:], T.EQ[:, o:o + 16], False, bb == 15)]
+            if bb < 15:
+                parts.append((T.pD[:, 16 * bb + 16:L], T.W1[:], T.EQ[:, o + 16:o + n], False, False))
+            mms("pD", parts, ["EQ.%d" % bb, "W1", "W2"])
+
+    def best_half(h):
+        sl = slice(2048 * h, 2048 * h + 2048)
+        op("v", ["X", "KL", "XR"], ["Y.%d" % h], lambda: V.tensor_tensor(T.Y[:, sl], T.X[:].indirect(T.KL[:, 128 * h:128 * h + 128]), T.XR[:, sl], Op.max))
+
+    def best_sum(h):
+        parts = []
+        for m in range(16):
+            parts.append((T.pK[:, 128 * h + m:128 * h + 128:16], T.Y[:, 2048 * h + m:2048 * h + 2048:16], T.GB16[:], False, h == 1 and m == 15))
+        mms("pK", parts, ["Y.%d" % h, "GB16"])
+
+    kin_gather("KL", "CL0")
+    for t in range(RO):
+        last = t == RO - 1
+        cl = "CL%d" % t
+        act(b("CWF"), ("pM", T.pM[:, 16:32]))
+        op("a", ["X", cl], ["XR"], lambda: A.activation(T.XR[:, 0::16], T.X[:].indirect(ap(cl)), Fn.Copy))
+        op("a", ["IDX", cl], ["CREP"], lambda: A.activation(T.CREP[:], T.IDX[:].indirect(ap(cl)), Fn.Copy))
+        op("a", ["E", cl], ["RCE"], lambda: A.activation(T.RCE[:], T.E[:, 0:W].indirect(ap(cl)), Fn.Copy))
+        for c in range(NCH):
+            if c not in OWN_LAST:
+                rec_piece("a", "GO", "KL", c)
+        mms("pM", [(T.pM[:, 64:80], T.SH[:], T.CC[:], True, False), (T.pM[:, 72:80], T.SHW[:], T.CC[:, 0:8], False, True)], ["SH", "SHW", "CC"])
+        if not last:
+            mms("pM", [(T.pM[:, 32:48], T.PSW[:], T.CWF[:], True, True)], ["PSW", "CWF"])
+        both("RCE", True, False)
+        for c in range(NCH):
+            if c not in OWN_LAST:
+                own_sum(c)
+        for st in (8, 4, 2, 1):
+            cp(("XR", T.XR[:, st::2 * st]), ("XR", T.XR[:, 0::2 * st]))
+        cp(b("KCF"), b("KL"))
+        tt(b("DD"), b("CC"), b("LIX"), Op.subtract)
+        for k in range(2):
+            kin_gather("AK%d" % k, "RQ%d%d" % (t, k))
+        if t:
+            scatter_R()
+            update_S(t - 1)
+        mms("pS", [(T.pS[:, 128 * h:128 * h + 128], T.KCF[:, 128 * h:128 * h + 128], T.IDS[:], True, True) for h in range(2)], ["KCF", "IDS"])
+        for c in V_ASK:
+            rec_piece("v", "GA1", "AK1", c)
+        for c in range(NCH):
+            rec_piece("a", "GA0", "AK0", c)
+        for c in V_ASK:
+            rec_sum("pA", L + CH * c, "GA1", c, True)
+        compare_lanes()
+        if not last:
+            cp(b("SW"), ("pM", T.pM[:, 32:48]))
+        best_half(0)
+        for c in range(NCH - 1):
+            rec_sum("pA", CH * c, "GA0", c, True)
+        count_lanes(0, 8)
+        rec_sum("pA", CH * (NCH - 1), "GA0", NCH - 1, True)
+        mms("pK", [(T.pK[:, 0:L], T.O128[:], T.CK[:], True, False)], ["O128", "CK"])
+        rest = [c for c in range(NCH) if c not in V_ASK]
+        for n, c in enumerate(rest):
+            rec_piece("a", "GA1", "AK1", c)
+            if n == 0:
+                act(b("AS%d0" % t), ("pA", T.pA[:, 0:L]))
+                send_sums(t, 0)
+                count_lanes(8, 16)
+            rec_sum("pA", L + CH * c, "GA1", c, True)
+        if not last:
+            op("a", ["IDX", "SW"], ["CSW"], lambda: A.activation(T.CSW[:], T.IDX[:].indirect(T.SW[:]), Fn.Copy))
+        act(b("AS%d1" % t), ("pA", T.pA[:, L:2 * L]))
+        send_sums(t, 1)
+        for c in OWN_LAST:
+            rec_piece("a", "GO", "KL", c)
+        best_half(1)
+        best_sum(0)
+        best_sum(1)
+        ts(("NT", T.NT[:, 16:16 + L]), ("pD", T.pD[:, 0:L]), 0.0, None, Op.is_ge)
+        if not last:
+            mms("pM", [(T.pM[:, 128:128 + L], ap("DN%d" % t), T.KCF[:], True, False), (T.pM[:, 128:128 + L], ap("DI%d" % t), T.CSW[:], False, True)],
+                ["DN%d" % t, "DI%d" % t, "KCF", "CSW"])
+            act(b("KV"), ("pM", T.pM[:, 128:128 + L]))
+        for c in OWN_LAST:
+            own_sum(c)
+        op("v", ["R", cl, "TB%d" % t], ["NVR"], lambda: V.tensor_tensor(T.NVR[:], T.R[:, 0:W].indirect(ap(cl)), ap("TB%d" % t), Op.max))
+        mms("pF", [(T.pF[:, 0:48], T.IDB[:], T.C48[:], True, False)] + fparts("NT", "GB4", LOW + HIGH + MIXED), ["IDB", "C48", "NT", "GB4"])
+        op("v", ["RST", "pK"], ["RM"], lambda: V.tensor_tensor_scan(T.RM[:], T.RST[:], T.pK[:, 0:L], 0.0, Op.mult, Op.max))
+        tt(b("NI"), ("pK", T.pK[:, 0:L]), b("RM"), Op.not_equal)
+        tt(b("DK"), ("pS", T.pS[:, 0:L]), b("NI"), Op.subtract)
+        op("v", ["NI", "DK"], ["BK"], lambda: V.tensor_tensor_scan(T.BK[:], T.NI[:], T.DK[:], 0.0, Op.mult, Op.max))
+        ts(b("BKF"), ("BK", T.BK[:, 15::16]), 4096.0, None, Op.mult)
+        tt(("D12", T.D12[:, 0:16]), ("pM", T.pM[:, 64:80]), b("BKF"), Op.subtract)
+        tt(("D12", T.D12[:, 16:32]), b("BKF"), b("CC"), Op.subtract)
+        both("RS%d0" % t, False, False)
+        both("RS%d1" % t, False, True)
+        for h, z in ((0, "pZ"), (1, "pZ2")):
+            z2, h2 = ("pZ2", 1) if h == 0 else ("pZ", 0)
+            tt(("VT.%d" % h, T.VT[:, 16 + 128 * h:144 + 128 * h]), (z, T[z][:, 0:128]), b("BM%d" % t, 128 * h, 128 * h + 128), Op.is_ge, rd=["VT"])
+            act(("UT.%d" % h2, T.UT[:, 16 + 128 * h2:144 + 128 * h2]), (z2, T[z2][:, 0:128]), Fn.Sign, rd=["UT"], bias=-0.9 * 64.0 ** (6 + t))
+        mms("pF", fparts("VT", "GB32", LOW), ["VT", "VT.0", "GB32"])
+        mms("pF", fparts("UT", "GBH", HIGH), ["UT", "UT.1", "GBH"])
+        mms("pF", fparts("VT", "GB32", HIGH + MIXED), ["VT", "VT.0", "VT.1", "GB32"])
+        mms("pF", fparts("UT", "GBH", LOW + MIXED, True), ["UT", "UT.0", "UT.1", "GBH"])
+        F = ("pF", T.pF[:, 0:48])
+        ts(b("I48"), F, 12.0, None, Op.is_lt)
+        cp(b("FI"), F)
+        if not last:
+            nt = "CST%d" % (t + 1)
+            mms("pF", [(T.pF[:, 64:66], T.IDB[:], ap(nt), True, False)] +
+                [(T.pF[:, 64:66], T.BD[:], T.I48[:, 16 + q:32:8], False, q == 7) for q in range(8)], ["IDB", nt, "BD", "I48"])
+        tt(b("SLM"), ("I48", T.I48[:, 16:32]), b("DD"), Op.mult)
+        ts(b("Q1"), b("FI"), 80, None, Op.bitwise_and)
+        ts(b("Q2"), b("FI"), 81, None, Op.bitwise_and)
+        expand("LH2", "SLM")
+        mms("pM", [(T.pM[:, 48:64], T.IDF[:], T.LW[:], True, False)] +
+            [(T.pM[:, 48 + 8 * h:56 + 8 * h], T.LH2[:, 128 * h:128 * h + 128], T.GF[:], False, h == 1) for h in range(2)], ["IDF", "LW", "LH2", "GF"])
+        ts(b("TBB"), b("Q1"), 16.0, None, Op.is_equal)
+        ts(b("OBB"), b("Q2"), 1.0, None, Op.is_equal)
+        if not last:
+            place(t + 1)
+        tt(b("TORN"), b("TBB"), b("I48"), Op.max)
+        tt(b("BO"), b("OBB"), b("I48"), Op.is_gt)
+        if not last:
+            sel1(t + 1)
+        tt(b("RMV"), ("BO", T.BO[:, 0:32]), ("TORN", T.TORN[:, 16:48]), Op.mult)
+        tt(b("P2"), ("TORN", T.TORN[:, 16:32]), ("D12", T.D12[:, 16:32]), Op.mult)
+        tt(b("P1"), b("RMV"), b("D12"), Op.mult)
+        if not last:
+            sel2(t + 1)
+        tt(b("DL1"), ("P1", T.P1[:, 0:16]), ("P1", T.P1[:, 16:32]), Op.add)
+        if not last:
+            tt(b("EQP"), b("PL%d" % (t + 1)), b("PL%d" % t), Op.is_equal)
+        tt(b("DL"), b("DL1"), b("P2"), Op.add)
+        cp(b("SL"), ("pM", T.pM[:, 48:64]))
+        if last:
+            scatter_R()
+            deps("a", ["R"], [])
+            A.dma_start(T.yr[:], T.R[:, 0:W]).then_inc(T.sem.stR, 16)
+            update_S(t)
+            cp(b("SF"), S)
+            mms("pK", [(T.pK[:, 128 * h:128 * h + 128], T.SF[:, 128 * h:128 * h + 128], T.IDH[:], True, True) for h in range(2)], ["SF", "IDH"])
+            cp(b("XS"), ("pK", T.pK[:, 0:L]))
+            deps("s", ["XS"], [])
+            g.sync.dma_start(T.ys[:], T.XS[:]).then_inc(T.sem.stS, 16)
+            break
+        for h in range(2):
+            ts(("ED.%d" % h, T.ED[:, 8 * h:8 * h + 8]), ("DL", T.DL[:, 8 * h:8 * h + 8]), T.EQP[:, h:h + 1], None, Op.mult, rd=["EQP"])
+        tt(b("CC"), ("CS", T.CS[:, 15::16]), b("ED"), Op.add, rd=["ED.0", "ED.1"])
+        expand("LH", "CC")
+        wrap(t + 1)
+        op("v", ["RCE", "BT%d" % t, "SL"], ["E"], lambda: V.tensor_tensor(T.E[:].indirect(T.SL[:]), T.RCE[:], ap("BT%d" % t), Op.add))
+        cp(b("CL%d" % (t + 1)), ("pM", T.pM[:, 16:32]))
+        send_list(t + 1)
+        op("v", ["KV", "SL"], ["K"], lambda: V.tensor_copy(T.K[:].indirect(T.SL[:]), T.KV[:]))
+        kin_gather("KL", "CL%d" % (t + 1))
+
+    g.wait_ge(T.sem.loc, LOC["n"])
+    A.wait_ge(T.sem.stR, 16)
+    g.sync.wait_ge(T.sem.stS, 16)
+    for q in ("v", "a", "p", "q"):
+        g.wait_ge(T.sem[own[q]], cnt[q])

@@ -3,10 +3,14 @@ from concourse.bass import DstId, RemoteDMATransfer
 from concourse.mybir import dt, AluOpType as Op, ActivationFunctionType as Fn
 
 NR, RO, W, L = 8, 4, 2048, 256
-WX = W + L
-NCH, CH = 4, 64
-V_ASK = (0, 1)
-OWN_LAST = (3,)
+TOP, STEP = 100.0, 0.8
+WX = W + 3 * L
+CH = 64
+VX = 192
+CMP1 = 8
+XA, XA0 = 2, 2
+B1 = 2
+OWN_FIRST = 1
 
 SCRATCH = {}
 
@@ -15,8 +19,7 @@ def _s(name, cols, dtype="float32", where="sbuf"):
     SCRATCH[name] = (where, [128, cols], dtype)
 
 
-for _n in ("E", "R"):
-    _s(_n, WX, "bfloat16")
+_s("R", WX, "bfloat16")
 _s("X", W, "bfloat16")
 _s("K", WX, "int32")
 _s("SN", L, "int32")
@@ -26,6 +29,7 @@ for _n in ("GO", "GA0", "GA1", "Y", "XR"):
 for _n in ("KL", "AK0", "AK1"):
     _s(_n, L, "uint16")
 _s("EQ", 2176, "bfloat16")
+_s("SZ", 3 * L, "float16")
 LOG = {}
 
 
@@ -41,65 +45,57 @@ _many("CLB", ["CL%d" % t for t in _TT], 16, "uint16")
 _many("RQB", ["RQ%d%d" % x for x in _TK], 16, "uint16")
 _many("RSB", ["RS%d%d" % x for x in _TK], L, "bfloat16")
 _many("ASB", ["AS%d%d" % x for x in _TK], L, "bfloat16")
-_many("BMB", ["BM%d" % t for t in _TT], L)
-_many("BTB", ["BT%d" % t for t in _TT], L, "bfloat16")
 _many("TBF", ["TB%d" % t for t in _TT], L, "bfloat16")
-_many("ISB", ["IST%d" % t for t in _TT], 1)
-_many("NOB2", ["NOT%d" % t for t in _TT], 1)
 _many("DGB", ["DN%d" % t for t in range(3)] + ["DI%d" % t for t in range(3)], 128, "float16")
-_many("CSB", ["CST%d" % t for t in _TT], 2, "bfloat16")
-_many("PLB", ["PL%d" % t for t in _TT], 2)
-for _n in ("CREP", "KCF", "CSW", "LH", "SF"):
+_many("OFB", ["OFF%d" % t for t in _TT], 2, "uint16")
+for _n in ("CREP", "KCF", "LH", "SF", "SM", "TR"):
     _s(_n, L, "float16")
-for _n in ("KV", "RM", "NI", "DK", "BK", "MS", "CS", "LH2", "XS", "RST", "JF", "BF", "DG", "NOB", "OB"):
+for _n in ("KV", "RM", "NI", "DK", "BK", "XS", "SP", "HI", "GN"):
     _s(_n, L)
-for _n in ("RCE", "NVR", "MK0", "MK1", "NTH", "CK"):
+for _n in ("RCE", "NVR", "MK0", "NTH", "CK", "OB", "BM", "RST", "JF", "BF", "DG", "D"):
     _s(_n, L, "bfloat16")
-for _n in ("UT", "VT", "NT"):
-    _s(_n, L + 32, "bfloat16")
-_s("D", L, "int32")
-_s("D15", L, "int32")
-_s("CB", 128, "int32")
-for _n in ("IDF", "SH", "SHW", "PSW"):
-    _s(_n, 128)
-for _n in ("IDH", "IDS"):
+for _n in ("UV", "NT"):
+    _s(_n, 2 * L, "bfloat16")
+_s("ROT", L, "float16")
+for _n in ("IDH", "IDS", "IDN", "PERM"):
     _s(_n, 128, "float16")
-for _n in ("IDB", "BD", "W1", "W2", "O128", "IOS"):
+for _n in ("IDB", "BDN", "CB"):
     _s(_n, 128, "bfloat16")
-_s("GF", 8)
-_s("GH", 8, "float16")
-_s("G8", 8, "int32")
-for _n in ("GBH", "GB4", "GB16", "GB32"):
+_s("ZH", 144, "float16")
+_s("ZB", 144, "bfloat16")
+_s("XZ", 240, "bfloat16")
+for _n in ("G8", "PB", "ISN"):
+    _s(_n, 8)
+for _n in ("GHP", "GHN"):
+    _s(_n, 8, "float16")
+for _n in ("GB16", "CST"):
     _s(_n, 8, "bfloat16")
-_s("PC", 2, "int32")
-_s("PM", 2, "int32")
-_s("SMI", 8, "int32")
+for _n in ("PC", "PM"):
+    _s(_n, 2, "int32")
+_s("PG", 1, "int32")
 _s("PMF", 2)
-_s("PGF", 1)
-_s("SG", 1)
-_s("P15", 1, "bfloat16")
-_s("EXI", 16, "int32")
-_s("EXP", 16, "uint16")
-_s("SW", 16, "uint16")
-_s("SL", 16, "uint16")
-for _n in ("LIX", "LWB", "LW", "CWF", "CC", "DD", "SLM", "BKF", "DL", "DL1", "P2", "ED"):
+for _n in ("PGF", "ZC", "WB", "RC"):
+    _s(_n, 1)
+_s("N16", 2, "bfloat16")
+for _n in ("EXP", "SL", "NU"):
+    _s(_n, 16, "uint16")
+for _n in ("LWB", "RND", "NEG", "NEW", "EXI", "WT"):
     _s(_n, 16)
-_s("D12", 32)
-_s("RMV", 32)
-_s("P1", 32)
+for _n in ("ODD", "TORN", "CAND"):
+    _s(_n, 16, "bfloat16")
+_s("TH", 32, "bfloat16")
+_s("MB", 64, "bfloat16")
+_s("C32", 32, "bfloat16")
+_s("C3", 48, "float16")
+_s("CH", 32, "float16")
+_s("PP", 64)
+_s("QQ", 32)
 _s("RR", 2)
-_s("EQP", 2)
-_s("C48", 48, "bfloat16")
-_s("I48", 48, "bfloat16")
-for _n in ("FI", "Q1", "Q2"):
-    _s(_n, 48, "int32")
-for _n in ("TBB", "TORN", "OBB", "BO"):
-    _s(_n, 48)
 for _n in ("pZ", "pZ2", "pA", "pK", "pS", "pD", "pF", "pM"):
     _s(_n, 512, "float32", "psum")
 
 SEMAPHORES = ["sv", "sa", "sp", "sq", "loc", "ldS", "ldK", "ldR", "ldX", "stR", "stS"]
-SEMAPHORES += ["rq%d%d" % (t, k) for t in range(RO) for k in range(2)] + ["rs%d%d" % (t, k) for t in range(RO) for k in range(2)]
+SEMAPHORES += ["rq%d%d" % (t, k) for t in range(RO) for k in range(2)] + ["rs%d%d" % (t, k) for t in range(RO) for k in range(3)]
 
 
 def rank_program(g, core, T, topo):
@@ -188,6 +184,9 @@ def rank_program(g, core, T, topo):
     def cp(o, i, rd=()):
         return op("v", [i[0]] + list(rd), [o[0]], lambda: V.tensor_copy(o[1], i[1]))
 
+    def scan(o, d0, d1):
+        return op("v", [d0[0], d1[0]], [o[0]], lambda: V.tensor_tensor_scan(o[1], d0[1], d1[1], 0.0, Op.mult, Op.max))
+
     def act(o, i, fn=Fn.Copy, rd=(), **kw):
         return op("a", [i[0]] + list(rd), [o[0]], lambda: A.activation(o[1], i[1], fn, **kw))
 
@@ -203,90 +202,32 @@ def rank_program(g, core, T, topo):
         base, o, n = LOG.get(name, (name, 0, SCRATCH[name][1][1] if name in SCRATCH else 0))
         return T[base][:, o + lo:o + (n if hi is None else hi)]
 
-    def b(name, lo=0, hi=None):
-        return (name, ap(name, lo, hi))
+    def b(name, lo=0, hi=None, key=None):
+        return (key or name, ap(name, lo, hi))
 
-    def iota(name, pattern, base, cm, imp=False):
-        kw = {"allow_small_or_imprecise_dtypes": True} if imp else {}
+    def by(name, lst, hi=None):
+        return (name, ap(name, 0, hi).indirect(lst))
+
+    def col(name, k=0):
+        return T[name][:, k:k + 1]
+
+    def iota(name, pattern, base, cm):
+        kw = {} if SCRATCH[name][2] == "int32" else {"allow_small_or_imprecise_dtypes": True}
         return op("q", [], [name], lambda: g.iota(T[name][:], pattern, base, cm, **kw))
 
-    def fill(name, val):
-        return op("v", [], [name], lambda: V.memset(ap(name), val))
+    def fill(o, val):
+        return op("v", [], [o[0]], lambda: V.memset(o[1], val))
 
     g.sync.dma_start(T.SN[:], T.slips[:]).then_inc(T.sem.ldS, 16)
-    A.dma_start(T.R[:, 0:W], T.rec[:]).then_inc(T.sem.ldR, 16)
     g.sync.dma_start(T.K[:, 0:W], T.kin[:]).then_inc(T.sem.ldK, 16)
-    A.dma_start(T.X[:], T.wealth[:]).then_inc(T.sem.ldX, 16)
+    g.sync.dma_start(T.R[:, 0:W], T.rec[:]).then_inc(T.sem.ldR, 16)
+    g.sync.dma_start(T.X[:], T.wealth[:]).then_inc(T.sem.ldX, 16)
     landed("SN", "ldS", 16)
     landed("R", "ldR", 16)
     landed("K", "ldK", 16)
     landed("X", "ldX", 16)
 
-    iota("PC", [[0, 2]], 0, 1)
-    iota("D", [[1, L]], 0, -1)
-    iota("JF", [[0, 16], [1, 16]], 0, 0, True)
-    iota("EXI", [[1, 16]], 0, 0)
-    iota("G8", [[1, 8]], 0, 0)
-    iota("CB", [[1, 8], [0, 16]], 0, 0)
-    iota("BF", [[1, 16], [0, 16]], 0, 0, True)
-    iota("LIX", [[128, 2], [0, 8]], W, 1, True)
-    iota("LWB", [[16, 16]], W, 0, True)
-    iota("IDX", [[1, W]], 0, 0, True)
-    ts(b("PM"), b("PC"), 15, None, Op.bitwise_and)
-    ts(b("SMI", 0, 1), b("PC", 0, 1), 4, None, Op.arith_shift_right)
-    cp(b("PMF"), b("PM"))
-    cp(b("PGF"), b("SMI", 0, 1))
-    ln2 = math.log(2.0)
-    act(b("P15"), b("PMF", 0, 1), Fn.Exp, scale=-ln2, bias=15.0 * ln2)
-    act(b("NTH"), b("JF"), Fn.Exp, scale=-ln2, bias=16.0 * ln2)
-    for nm in ("IDF", "IDB", "IDH"):
-        ts(b(nm), b("D", 0, 128), 0.0, None, Op.is_equal)
-    for t in range(RO):
-        ts(b("CST%d" % t), b("PMF"), 5.0, t - 7.5, Op.mult, Op.add)
-    ts(b("IOS"), b("JF", 0, 128), -7.5, None, Op.add)
-    cp(b("EXP"), b("EXI"))
-    ts(b("D15"), b("D"), 15, None, Op.bitwise_and)
-    ts(b("GF"), b("G8"), T.PGF[:, 0:1], None, Op.is_equal, rd=["PGF"])
-    ts(b("DG"), b("D15"), 0.0, None, Op.is_equal)
-    ts(b("RST"), b("JF"), 1.0, None, Op.min)
-    cp(b("GH"), b("GF"))
-    for t in range(RO - 1):
-        ts(b("IST%d" % t), b("PMF", 0, 1), float(t), None, Op.is_equal)
-        ts(b("NOT%d" % t), b("PMF", 0, 1), float(t), None, Op.not_equal)
-    ts(b("BD"), b("CB"), T.PGF[:, 0:1], None, Op.is_equal, rd=["PGF"])
-    for nm, f in (("GBH", 0.5), ("GB4", 4.0), ("GB16", 16.0), ("GB32", 32.0)):
-        ts(b(nm), b("GF"), f, None, Op.mult)
-    ts(b("IDS"), b("IDF"), 1.0 / 4096.0, None, Op.mult)
-    ts(b("SMI", 1, 2), b("PC", 0, 1), 1, None, Op.bitwise_and)
-    fill("O128", 1.0 / 128.0)
-    ts(b("SG"), b("SMI", 1, 2), -2.0, 1.0, Op.mult, Op.add)
-    fill("C48", 12.0)
-    ts(b("PSW"), b("D", 0, 128), T.SG[:, 0:1], None, Op.is_equal, rd=["SG"])
-    cp(b("SF"), b("SN"))
-    S = ("pS", T.pS[:, 256:512])
-    mms("pS", [(T.pS[:, 256 + 128 * h:384 + 128 * h], T.SF[:, 128 * h:128 * h + 128], T.IDH[:], True, True) for h in range(2)], ["SF", "IDH"])
-
-    MAG = 1.5 * 2.0 ** 27
     LOC = {"n": 0}
-
-    def place(t):
-        mk = "MK%d" % (t % 2)
-        ts(b("RR"), ("pF", T.pF[:, 64:66]), MAG, -MAG, Op.add, Op.add)
-        for h in range(2):
-            ts((mk, T[mk][:, 128 * h:128 * h + 128]), b("IOS"), T.RR[:, h:h + 1], T.pF[:, 64 + h:65 + h], Op.add, Op.is_equal, rd=["RR", "pF"])
-
-    def sel1(t):
-        tt(b("MS"), S, b("MK%d" % (t % 2)), Op.mult)
-
-    def sel2(t):
-        op("v", ["RST", "MS"], ["CS"], lambda: V.tensor_tensor_scan(T.CS[:], T.RST[:], T.MS[:], 0.0, Op.mult, Op.add))
-        tt(b("PL%d" % t), ("pF", T.pF[:, 64:66]), b("RR"), Op.subtract)
-
-    def expand(out, src):
-        op("v", [src, "EXP", "DG"], [out], lambda: V.tensor_tensor(T[out][:], T[src][:].indirect(T.EXP[:]), T.DG[:], Op.mult))
-
-    def wrap(t):
-        mms("pM", [(T.pM[:, 16 + 8 * h:24 + 8 * h], T.LH[:, 128 * h:128 * h + 128], T.GH[:], True, True) for h in range(2)], ["LH", "GH"])
 
     def send_list(t):
         trs = []
@@ -306,105 +247,143 @@ def rank_program(g, core, T, topo):
         deps("q", ["CL%d" % t], [])
         g.remote_dma_fused(trs, local_sem=T.sem.loc)
 
-    def send_sums(t, k):
+    def send_sums(t, k, lo, hi, n):
         asker = T.cores[(rank - 1 - ((2 * t + k) % 7)) % NR]
         rid, pid, _x = topo.addr(asker)
-        deps("q", ["AS%d%d" % (t, k)], [])
-        g.remote_dma(ap("RS%d%d" % (t, k)), ap("AS%d%d" % (t, k)), T.sem["rs%d%d" % (t, k)], T.sem.loc, pid, rid, topo.mask(core, asker))
+        act(b("AS%d%d" % (t, k), lo, hi, "AS%d%d" % (t, n)), ("pA", T.pA[:, L * k + lo:L * k + hi]))
+        deps("q", ["AS%d%d" % (t, n)], [])
+        g.remote_dma(ap("RS%d%d" % (t, k), lo, hi), ap("AS%d%d" % (t, k), lo, hi), T.sem["rs%d%d" % (t, n)], T.sem.loc, pid, rid, topo.mask(core, asker))
         LOC["n"] += len(topo.engines(core, asker))
         q = T.cores[(rank + 1 + ((2 * t + k) % 7)) % NR]
-        landed("RS%d%d" % (t, k), "rs%d%d" % (t, k), len(topo.engines(q, core)))
+        landed("RS%d%d" % (t, n), "rs%d%d" % (t, n), len(topo.engines(q, core)))
 
-    mms("pF", [(T.pF[:, 64:66], T.IDB[:], ap("CST0"), True, True)], ["IDB", "CST0"])
-    place(0)
-    sel1(0)
-    sel2(0)
-    cp(b("CC"), ("CS", T.CS[:, 15::16]))
-    expand("LH", "CC")
-    wrap(0)
-    cp(b("CL0"), ("pM", T.pM[:, 16:32]))
-    send_list(0)
-
-    act(("E", T.E[:, 0:W]), ("R", T.R[:, 0:W]), Fn.Exp, scale=6.0 * ln2)
-    for t in range(RO - 1):
-        act(b("DN%d" % t), b("IDF"), Fn.Identity, rd=["NOT%d" % t], scale=ap("NOT%d" % t))
-        act(b("DI%d" % t), b("IDF"), Fn.Identity, rd=["IST%d" % t], scale=ap("IST%d" % t))
-    ts(b("SH"), b("D", 0, 128), 16.0, None, Op.is_equal)
-    ts(b("SHW"), b("D", 0, 128), -112.0, None, Op.is_equal)
-    ts(b("CK"), b("JF"), -1.0, 15.0, Op.mult, Op.add)
-    for nm, x in (("UT", -1.0), ("VT", 0.0), ("NT", 1.0)):
-        fill(nm, x)
-    ts(b("LW"), b("LWB"), T.PMF[:, 0:1], None, Op.add, rd=["PMF"])
-    ts(b("NTH"), b("NTH"), -1.0, None, Op.mult)
-    ts(b("W2"), b("BD"), T.P15[:, 0:1], None, Op.mult, rd=["P15"])
-    ts(b("W1"), b("BD"), 65536.0, None, Op.mult)
-    ts(b("NOB"), b("BF"), T.PMF[:, 0:1], None, Op.not_equal, rd=["PMF"])
-    ts(b("OB"), b("BF"), T.PMF[:, 0:1], None, Op.is_equal, rd=["PMF"])
-    for t in range(RO):
-        ts(b("BM%d" % t), b("NOB"), 1e29, 64.0 ** (5 + t), Op.mult, Op.add)
-        if t < RO - 1:
-            ts(b("BT%d" % t), b("OB"), 64.0 ** (8 + t), None, Op.mult)
-        ts(b("TB%d" % t), b("OB"), float(8 + t), None, Op.mult)
-
-    def rec_piece(q, G, lst, c):
-        o, off = T[G][:, 1024 * c:1024 * c + 1024], T[lst][:, CH * c:CH * c + CH]
-        key = "%s.%d" % (G, c)
-        if q == "a":
-            op("a", ["E", lst], [key], lambda: A.activation(o, T.E[:, 0:W].indirect(off), Fn.Copy))
-        else:
-            op("v", ["E", lst], [key], lambda: V.tensor_copy(o, T.E[:, 0:W].indirect(off)))
-
-    def rec_sum(bank, col, G, c, whole):
-        parts = []
-        for m in range(16):
-            parts.append((T[bank][:, col:col + CH], T.IDB[:], T[G][:, 1024 * c + m:1024 * c + 1024:16], whole and m == 0, whole and m == 15))
-        mms(bank, parts, ["%s.%d" % (G, c), "IDB"])
-
-    def own_sum(c):
-        rec_sum("pZ2" if c >= NCH // 2 else "pZ", CH * (c % (NCH // 2)), "GO", c, False)
-
-    def both(src, first, fin):
-        for h, z in ((0, "pZ"), (1, "pZ2")):
-            mms(z, [(T[z][:, 0:128], T.IDB[:], ap(src, 128 * h, 128 * h + 128), first, fin)], ["IDB", src])
+    def wrapped(out, z, src, n, start, fin):
+        return [(out, T[z][:, 15 - j:143 - j], T[src][:, j:16 * n:16], start and j == 0, fin and j == 15) for j in range(16)]
 
     def kin_gather(out, lst):
-        op("v", ["K", lst], [out], lambda: V.tensor_copy(T[out][:], T.K[:, 0:W].indirect(ap(lst))))
+        cp(b(out), by("K", ap(lst), W), rd=[lst])
 
-    def scatter_R():
-        op("v", ["NVR", "SL"], ["R"], lambda: V.tensor_copy(T.R[:].indirect(T.SL[:]), T.NVR[:]))
+    H = ("pS", T.pS[:, L:2 * L])
 
-    def update_S(t):
-        mk = "MK%d" % (t % 2)
-        op("v", ["DL", "EXP", mk], ["XS"], lambda: V.tensor_tensor(T.XS[:], T.DL[:].indirect(T.EXP[:]), T[mk][:], Op.mult))
-        tt(S, S, b("XS"), Op.add)
+    def turn(rows):
+        parts = []
+        for p in range(4):
+            for x in range(16):
+                for e in range(2):
+                    lo = L - L * e + x
+                    parts.append((T.pS[32 * p:32 * p + 32, L + x:2 * L:16], T.SZ[:, lo:lo + 2 * L - x:16], rows(2 * p + e), e == 0, e == 1))
+        mms("pS", parts, ["SZ", "SZ0", "IDH"])
 
-    def fparts(tile, w, which, fin=False):
-        return [(T.pF[:, 16 * (s + 1) + 8 * h:16 * (s + 1) + 8 * h + 8], T[tile][:, 16 + 128 * h + 16 * s:144 + 128 * h + 16 * s], T[w][:], False, fin and n == len(which) - 1)
-                for n, (h, s) in enumerate(which)]
+    def rot(j):
+        return T.ROT[:, 8 * (5 * j % 16):8 * (5 * j % 16) + 128]
 
-    LOW, HIGH, MIXED = [(0, -1), (0, 0)], [(1, 0), (1, 1)], [(0, 1), (1, -1)]
+    iota("PC", [[0, 2]], 0, 1)
+    iota("PM", [[0, 2]], 0, 13)
+    iota("JF", [[0, 16], [1, 16]], 0, 0)
+    iota("D", [[1, L]], 0, -1)
+    iota("PB", [[L, 8]], 0, 1)
+    iota("EXI", [[16, 16]], 15, 0)
+    iota("G8", [[1, 8]], 0, 0)
+    iota("CB", [[1, 8], [0, 16]], 0, 0)
+    ts(b("PG"), b("PC", 0, 1), 4, None, Op.arith_shift_right)
+    ts(b("PM", 1, 2), b("PM", 1, 2), 15, None, Op.bitwise_and)
+    ts(b("PM", 0, 1), b("PC", 0, 1), 15, None, Op.bitwise_and)
+    cp(b("PGF"), b("PG"))
+    cp(b("PMF"), b("PM"))
+    ts(b("ZC"), b("PMF", 0, 1), -1.0, 15.0, Op.mult, Op.add)
+    ts(b("MK0"), b("JF"), col("PMF", 1), None, Op.is_equal, rd=["PMF"])
+    ts(b("ZH"), b("D", 0, 144), col("ZC"), None, Op.is_equal, rd=["ZC"])
+    ln2 = math.log(2.0)
+    ts(b("WB"), b("PMF", 0, 1), -STEP * ln2, (TOP + 15 * STEP) * ln2, Op.mult, Op.add)
+    for nm in ("IDB", "IDH"):
+        ts(b(nm), b("D", 0, 128), 0.0, None, Op.is_equal)
+    ts(b("ISN", 0, 4, "IS"), b("JF", 0, 4), col("PMF"), None, Op.is_equal, rd=["PMF"])
+    ts(b("ISN", 4, 8, "NS"), b("JF", 0, 4), col("PMF"), None, Op.not_equal, rd=["PMF"])
+    ts(b("CH", 0, 2, "CH0"), b("PMF"), 0.0, None, Op.mult)
+    tt(b("SM"), b("SN"), b("MK0"), Op.mult)
+    mms("pM", wrapped(T.pM[:, 0:16], "ZH", "SM", 16, True, True), ["ZH", "SM"])
+    ts(b("OFF0"), b("PMF"), col("PMF"), None, Op.min)
+    cp(b("CL0"), ("pM", T.pM[:, 0:16]))
+    send_list(0)
 
-    def compare_lanes():
-        o = 0
-        for bb in range(16):
-            n = L - 16 * bb
-            ts(("EQ.%d" % bb, T.EQ[:, o:o + n]), ("CREP", T.CREP[:, 16 * bb:L]), T.CWF[:, bb:bb + 1], None, Op.is_equal, rd=["CWF"])
-            o += n
+    iota("BF", [[1, 16], [0, 16]], 0, 0)
+    iota("LWB", [[32, 16]], W, 2)
+    act(b("WT"), b("EXI"), Fn.Exp, rd=["WB"], scale=-STEP * ln2, bias=col("WB"))
+    for k in range(W // L):
+        act(b("IDX", L * k, L * k + L), b("D"), Fn.Identity, rd=["PB"], bias=col("PB", k))
+        if k == 0:
+            act(b("NTH"), b("IDX", 0, L), Fn.Exp, scale=-STEP * ln2, bias=TOP * ln2 + math.log(2.55))
+    cp(b("SF"), b("SN"))
+    ts(b("RC"), b("PGF"), -15.0, None, Op.mult)
+    ts(b("RC"), b("PMF", 0, 1), 7.0, col("RC"), Op.mult, Op.add, rd=["RC"])
+    for lo in (0, 128):
+        ts(b("ROT", lo, lo + 128), b("D", 0, 128), col("RC"), None, Op.is_equal, rd=["RC"])
+    mms("pS", [(T.pS[:, L + 16 * j:L + 16 * j + 16], rot(j), T.SF[:, j::16], True, True) for j in range(16)], ["ROT", "SF"])
+    mms("pK", [(T.pK[:, 0:128], rot(0), T.IDH[:], True, True)], ["ROT", "IDH"])
+    for lo in (0, 2 * L):
+        ts(b("SZ", lo, lo + L, "SZ0"), b("MK0"), 0.0, None, Op.mult)
+    ts(b("ZB"), b("ZH"), 1.0 / 32.0, None, Op.mult)
+    ts(b("IDS"), b("IDH"), 1.0 / 4096.0, None, Op.mult)
+    ts(b("IDN"), b("IDH"), -1.0, None, Op.mult)
+    ts(b("DG"), b("JF"), col("PMF"), None, Op.is_equal, rd=["PMF"])
+    ts(b("RST"), b("JF"), 1.0, None, Op.min)
+    ts(b("CK"), b("JF"), -1.0, 15.0, Op.mult, Op.add)
+    ts(b("CST"), b("EXI", 0, 8), col("PMF"), -142.5, Op.add, Op.add, rd=["PMF"])
+    for nm, x in (("XZ", 0.0), ("MB", 0.0), ("N16", -16.0), ("NEG", -1.0)):
+        fill(b(nm), x)
+    fill(b("C32", 0, 16, "C32.0"), 0.75)
+    fill(b("C32", 16, 32, "C32.1"), 19.75 / 16.0)
+    ts(b("BDN"), b("CB"), col("PGF"), -1.0, Op.is_equal, Op.mult, rd=["PGF"])
+    for nm, f in (("GB16", 16.0), ("GHP", 4096.0), ("GHN", -4096.0)):
+        ts(b(nm), b("G8"), col("PGF"), f, Op.is_equal, Op.mult, rd=["PGF"])
+    cp(b("EXP"), b("EXI"))
+    ts(b("C3"), b("MK0", 0, 48), 0.0, None, Op.mult)
+    cp(b("SZ", L, 2 * L), H)
+    turn(lambda q: T.IDH[:, q::8])
+    kin_gather("KL", "CL0")
+    act(b("PERM"), ("pK", T.pK[:, 0:128]))
+    ts(b("OB"), b("BF"), col("PMF"), None, Op.is_equal, rd=["PMF"])
+    cp(b("C3", 16, 32), b("LWB"))
+    ts(b("BM"), b("OB"), -1e29, 1e29, Op.mult, Op.add)
+    for t in range(RO):
+        ts(b("TB%d" % t), b("OB"), float(8 + t), None, Op.mult)
+
+    def rec_piece(q, G, lst, lo, hi, t):
+        o, i = ("%s.%d" % (G, lo), T[G][:, 16 * lo:16 * hi]), by("R", T[lst][:, lo:hi], W)
+        if q == "a":
+            act(o, i, Fn.Relu, rd=[lst], bias=1.0 / 128.0 - (5 + t))
+        else:
+            ts(o, i, 1.0 / 128.0 - (5 + t), 0.0, Op.add, Op.max, rd=[lst])
+
+    def rec_sum(bank, c0, G, lo, hi, whole):
+        parts = [(T[bank][:, c0:c0 + hi - lo], T.IDB[:], T[G][:, 16 * lo + m:16 * hi:16], whole and m == 0, whole and m == 15) for m in range(16)]
+        mms(bank, parts, ["%s.%d" % (G, lo), "IDB"])
+
+    def own_sum(c):
+        rec_sum("pZ2" if CH * c >= 128 else "pZ", CH * c % 128, "GO", CH * c, CH * c + CH, False)
+
+    def add_sums(src, key, lo, hi, first, fin):
+        z = "pZ2" if lo >= 128 else "pZ"
+        mms(z, [(T[z][:, lo % 128:lo % 128 + hi - lo], T.IDB[:], ap(src, lo, hi), first, fin)], ["IDB", key])
+
+    def scatter(tab, src):
+        op("v", [src, "SL"], [tab], lambda: V.tensor_copy(T[tab][:].indirect(T.SL[:]), T[src][:]))
+
+    def compare_lanes(lo, hi):
+        for bb in range(lo, hi):
+            n, o = L - 16 * bb, sum(L - 16 * x for x in range(bb))
+            ts(("EQ.%d" % bb, T.EQ[:, o:o + n]), ("CREP", T.CREP[:, 16 * bb:L]), col("PP", 48 + bb), col("WT", bb), Op.is_equal, Op.mult, rd=["CW", "WT"])
 
     def count_lanes(lo, hi):
         if lo == 0:
             mms("pD", [(T.pD[:, 0:L], T.IDB[:], T.NTH[:], True, False)], ["IDB", "NTH"])
         for bb in range(lo, hi):
-            n = L - 16 * bb
-            o = sum(L - 16 * x for x in range(bb))
-            parts = [(T.pD[:, 16 * bb:16 * bb + 16], T.W2[:], T.EQ[:, o:o + 16], False, bb == 15)]
-            if bb < 15:
-                parts.append((T.pD[:, 16 * bb + 16:L], T.W1[:], T.EQ[:, o + 16:o + n], False, False))
-            mms("pD", parts, ["EQ.%d" % bb, "W1", "W2"])
+            n, o = L - 16 * bb, sum(L - 16 * x for x in range(bb))
+            mms("pD", [(T.pD[:, 16 * bb:L], T.BDN[:], T.EQ[:, o:o + n], False, bb == 15)], ["EQ.%d" % bb, "BDN"])
 
     def best_half(h):
         sl = slice(2048 * h, 2048 * h + 2048)
-        op("v", ["X", "KL", "XR"], ["Y.%d" % h], lambda: V.tensor_tensor(T.Y[:, sl], T.X[:].indirect(T.KL[:, 128 * h:128 * h + 128]), T.XR[:, sl], Op.max))
+        tt(("Y.%d" % h, T.Y[:, sl]), by("X", T.KL[:, 128 * h:128 * h + 128]), ("XR", T.XR[:, sl]), Op.max, rd=["KL"])
 
     def best_sum(h):
         parts = []
@@ -412,144 +391,166 @@ def rank_program(g, core, T, topo):
             parts.append((T.pK[:, 128 * h + m:128 * h + 128:16], T.Y[:, 2048 * h + m:2048 * h + 2048:16], T.GB16[:], False, h == 1 and m == 15))
         mms("pK", parts, ["Y.%d" % h, "GB16"])
 
-    kin_gather("KL", "CL0")
+    MAG = 1.5 * 2.0 ** 31
+    EVEN = 1.5 * 2.0 ** 20
+    CW = ("CW", T.PP[:, 48:64])
+    NOWN = L // CH
+
     for t in range(RO):
         last = t == RO - 1
         cl = "CL%d" % t
-        act(b("CWF"), ("pM", T.pM[:, 16:32]))
-        op("a", ["X", cl], ["XR"], lambda: A.activation(T.XR[:, 0::16], T.X[:].indirect(ap(cl)), Fn.Copy))
-        op("a", ["IDX", cl], ["CREP"], lambda: A.activation(T.CREP[:], T.IDX[:].indirect(ap(cl)), Fn.Copy))
-        op("a", ["E", cl], ["RCE"], lambda: A.activation(T.RCE[:], T.E[:, 0:W].indirect(ap(cl)), Fn.Copy))
-        for c in range(NCH):
-            if c not in OWN_LAST:
-                rec_piece("a", "GO", "KL", c)
-        mms("pM", [(T.pM[:, 64:80], T.SH[:], T.CC[:], True, False), (T.pM[:, 72:80], T.SHW[:], T.CC[:, 0:8], False, True)], ["SH", "SHW", "CC"])
-        if not last:
-            mms("pM", [(T.pM[:, 32:48], T.PSW[:], T.CWF[:], True, True)], ["PSW", "CWF"])
-        both("RCE", True, False)
-        for c in range(NCH):
-            if c not in OWN_LAST:
-                own_sum(c)
-        for st in (8, 4, 2, 1):
-            cp(("XR", T.XR[:, st::2 * st]), ("XR", T.XR[:, 0::2 * st]))
+        off = ap("OFF%d" % t, 0, 1)
+
+        def wealth(na):
+            act(("XR", T.XR[:, 0::16]), by("X", ap(cl)), rd=[cl])
+            for n, st in enumerate((8, 4, 2, 1)):
+                if n < na:
+                    act(("XR", T.XR[:, st::2 * st]), ("XR", T.XR[:, 0::2 * st]))
+                else:
+                    op("q", ["XR"], ["XR"], lambda: g.affine_select(T.XR[:, st::2 * st], T.XR[:, 0::2 * st], [[0, 8 * L // st]], Op.is_ge, 0.0, 0, 0))
+
+        drawn = ("pM", T.pM[:, 0:16]) if t == 0 else by("SP", off)
+        act(CW, drawn, rd=["OFF%d" % t])
+        act(b("CH", 2, 18), drawn, rd=["OFF%d" % t])
+        act(b("CREP"), by("IDX", ap(cl)), rd=[cl])
+        if t:
+            wealth(XA)
+        else:
+            for x in range(RO - 1):
+                act(b("DN%d" % x), b("IDB"), Fn.Identity, rd=["NS"], scale=col("ISN", 4 + x))
+                act(b("DI%d" % x), b("IDB"), Fn.Identity, rd=["IS"], scale=col("ISN", x))
+            act(b("SP"), H)
+        act(b("RCE"), by("R", ap(cl), W), Fn.Relu, rd=[cl], bias=1.0 / 128.0 - (5 + t))
+        for c in range(OWN_FIRST):
+            rec_piece("a", "GO", "KL", CH * c, CH * c + CH, t)
+        if t == 0:
+            wealth(XA0)
+        for lo in (0, 128):
+            add_sums("RCE", "RCE", lo, lo + 128, True, False)
         cp(b("KCF"), b("KL"))
-        tt(b("DD"), b("CC"), b("LIX"), Op.subtract)
+        if last:
+            op("v", ["NEG", "OFF%d" % t], ["SP"], lambda: V.tensor_copy(T.SP[:].indirect(off), T.NEG[:]))
+            cp(b("SZ", L, 2 * L), b("SP"))
+            turn(lambda q: T.IDH[:, 16 * q:16 * q + 16])
+        compare_lanes(0, CMP1)
+        count_lanes(0, CMP1)
+        for c in range(OWN_FIRST):
+            own_sum(c)
         for k in range(2):
             kin_gather("AK%d" % k, "RQ%d%d" % (t, k))
-        if t:
-            scatter_R()
-            update_S(t - 1)
+        compare_lanes(CMP1, 16)
+        count_lanes(CMP1, 16)
+        vp = [(0, CH), (CH, VX)] if VX < 3 * CH else [(0, CH), (CH, 2 * CH), (2 * CH, VX)]
+        rec_piece("a", "GA0", "AK0", VX, L, t)
+        act(b("NT", L, 2 * L, "NT.1"), ("pD", T.pD[:, 0:L]), Fn.Sign, scale=-1.0)
+        for lo, hi in vp:
+            rec_piece("v", "GA0", "AK0", lo, hi, t)
+        rec_sum("pA", VX, "GA0", VX, L, True)
+        for c in range(NOWN):
+            rec_piece("a", "GA1", "AK1", CH * c, CH * c + CH, t)
+            if c == NOWN - 1:
+                send_sums(t, 1, 0, L - CH, 1)
+            if c < len(vp):
+                rec_sum("pA", vp[c][0], "GA0", vp[c][0], vp[c][1], True)
+            if c == len(vp):
+                send_sums(t, 0, 0, L, 0)
+            rec_sum("pA", L + CH * c, "GA1", CH * c, CH * c + CH, True)
+        act(b("NT", 0, L, "NT.0"), b("NT", L, 2 * L, "NT.1"), Fn.Identity, scale=-2.0 ** 21, bias=-2.0 ** 21)
+        send_sums(t, 1, L - CH, L, 2)
+        if last:
+            act(b("TR"), H)
+            mms("pS", [(T.pS[:, L + j:2 * L:16], rot(-j), T.TR[:, 16 * j:16 * j + 16], True, True) for j in range(16)], ["ROT", "TR"])
         mms("pS", [(T.pS[:, 128 * h:128 * h + 128], T.KCF[:, 128 * h:128 * h + 128], T.IDS[:], True, True) for h in range(2)], ["KCF", "IDS"])
-        for c in V_ASK:
-            rec_piece("v", "GA1", "AK1", c)
-        for c in range(NCH):
-            rec_piece("a", "GA0", "AK0", c)
-        for c in V_ASK:
-            rec_sum("pA", L + CH * c, "GA1", c, True)
-        compare_lanes()
         if not last:
-            cp(b("SW"), ("pM", T.pM[:, 32:48]))
+            mms("pM", [(T.pM[:, 128:128 + L], ap("DN%d" % t), T.KCF[:], True, False)] +
+                [(T.pM[:, 128 + e:128 + L:2], ap("DI%d" % t), T.CREP[:, 1 - e::2], False, e == 1) for e in range(2)],
+                ["DN%d" % t, "DI%d" % t, "KCF", "CREP"])
+        mms("pF", [(T.pF[:, 0:32], T.IDB[:], T.C32[:], True, False)] + wrapped(T.pF[:, 0:32], "ZB", "NT", 32, False, False),
+            ["IDB", "C32.0", "C32.1", "ZB", "NT.0", "NT.1"])
+        mms("pK", [(T.pK[:, 0:L], T.IDB[:], T.CK[:], True, False)], ["IDB", "CK"])
         best_half(0)
-        for c in range(NCH - 1):
-            rec_sum("pA", CH * c, "GA0", c, True)
-        count_lanes(0, 8)
-        rec_sum("pA", CH * (NCH - 1), "GA0", NCH - 1, True)
-        mms("pK", [(T.pK[:, 0:L], T.O128[:], T.CK[:], True, False)], ["O128", "CK"])
-        rest = [c for c in range(NCH) if c not in V_ASK]
-        for n, c in enumerate(rest):
-            rec_piece("a", "GA1", "AK1", c)
-            if n == 0:
-                act(b("AS%d0" % t), ("pA", T.pA[:, 0:L]))
-                send_sums(t, 0)
-                count_lanes(8, 16)
-            rec_sum("pA", L + CH * c, "GA1", c, True)
-        if not last:
-            op("a", ["IDX", "SW"], ["CSW"], lambda: A.activation(T.CSW[:], T.IDX[:].indirect(T.SW[:]), Fn.Copy))
-        act(b("AS%d1" % t), ("pA", T.pA[:, L:2 * L]))
-        send_sums(t, 1)
-        for c in OWN_LAST:
-            rec_piece("a", "GO", "KL", c)
         best_half(1)
         best_sum(0)
-        best_sum(1)
-        ts(("NT", T.NT[:, 16:16 + L]), ("pD", T.pD[:, 0:L]), 0.0, None, Op.is_ge)
-        if not last:
-            mms("pM", [(T.pM[:, 128:128 + L], ap("DN%d" % t), T.KCF[:], True, False), (T.pM[:, 128:128 + L], ap("DI%d" % t), T.CSW[:], False, True)],
-                ["DN%d" % t, "DI%d" % t, "KCF", "CSW"])
-            act(b("KV"), ("pM", T.pM[:, 128:128 + L]))
-        for c in OWN_LAST:
+        for c in range(OWN_FIRST, NOWN):
+            rec_piece("a", "GO", "KL", CH * c, CH * c + CH, t)
+            if c == OWN_FIRST:
+                if last:
+                    act(b("SF"), H)
+                    mms("pS", [(H[1], T.PERM[:], T.SF[:], True, True)], ["PERM", "SF"])
+                else:
+                    act(b("KV"), ("pM", T.pM[:, 128:128 + L]))
+            if c == B1:
+                best_sum(1)
+            if c == NOWN - 1:
+                add_sums("RS%d0" % t, "RS%d0" % t, 0, 128, False, False)
+                add_sums("RS%d1" % t, "RS%d1" % t, 0, 128, False, True)
+                add_sums("RS%d0" % t, "RS%d0" % t, 128, L, False, False)
+                add_sums("RS%d1" % t, "RS%d1" % t, 128, L - CH, False, False)
             own_sum(c)
-        op("v", ["R", cl, "TB%d" % t], ["NVR"], lambda: V.tensor_tensor(T.NVR[:], T.R[:, 0:W].indirect(ap(cl)), ap("TB%d" % t), Op.max))
-        mms("pF", [(T.pF[:, 0:48], T.IDB[:], T.C48[:], True, False)] + fparts("NT", "GB4", LOW + HIGH + MIXED), ["IDB", "C48", "NT", "GB4"])
-        op("v", ["RST", "pK"], ["RM"], lambda: V.tensor_tensor_scan(T.RM[:], T.RST[:], T.pK[:, 0:L], 0.0, Op.mult, Op.max))
+        tt(b("NVR"), by("R", ap(cl), W), b("TB%d" % t), Op.max, rd=[cl])
+        if last:
+            ts(b("HI"), H, 0.0, 4096.0, Op.is_lt, Op.mult)
+        add_sums("RS%d1" % t, "RS%d2" % t, L - CH, L, False, True)
+        for h, z in ((0, "pZ"), (1, "pZ2")):
+            act(b("UV", 128 * h, 128 * h + 128, "U.%d" % h), (z, T[z][:, 0:128]), Fn.Sign, bias=-0.7)
+        scan(b("RM"), b("RST"), ("pK", T.pK[:, 0:L]))
         tt(b("NI"), ("pK", T.pK[:, 0:L]), b("RM"), Op.not_equal)
         tt(b("DK"), ("pS", T.pS[:, 0:L]), b("NI"), Op.subtract)
-        op("v", ["NI", "DK"], ["BK"], lambda: V.tensor_tensor_scan(T.BK[:], T.NI[:], T.DK[:], 0.0, Op.mult, Op.max))
-        ts(b("BKF"), ("BK", T.BK[:, 15::16]), 4096.0, None, Op.mult)
-        tt(("D12", T.D12[:, 0:16]), ("pM", T.pM[:, 64:80]), b("BKF"), Op.subtract)
-        tt(("D12", T.D12[:, 16:32]), b("BKF"), b("CC"), Op.subtract)
-        both("RS%d0" % t, False, False)
-        both("RS%d1" % t, False, True)
+        scan(b("BK"), b("NI"), b("DK"))
+        tt(b("LH"), by("BK", T.EXP[:]), b("DG"), Op.mult, rd=["EXP"])
+        mms("pM", [(T.pM[:, 16:64], T.IDH[:], T.C3[:], True, False)] +
+            [(T.pM[:, lo:lo + 16], T.IDN[:], T.CH[:, 2:18], False, False) for lo in (16, 32)] + [(T.pM[:, 48:64], T.IDH[:], T.CH[:, 1:17], False, False)] +
+            [(T.pM[:, lo + 8 * h:lo + 8 * h + 8], T.LH[:, 128 * h:128 * h + 128], T[w][:], False, lo == 48 and h == 1) for lo, w in ((16, "GHP"), (48, "GHN")) for h in range(2)],
+            ["IDH", "IDN", "C3", "CH", "CH0", "LH", "GHP", "GHN"])
         for h, z in ((0, "pZ"), (1, "pZ2")):
-            z2, h2 = ("pZ2", 1) if h == 0 else ("pZ", 0)
-            tt(("VT.%d" % h, T.VT[:, 16 + 128 * h:144 + 128 * h]), (z, T[z][:, 0:128]), b("BM%d" % t, 128 * h, 128 * h + 128), Op.is_ge, rd=["VT"])
-            act(("UT.%d" % h2, T.UT[:, 16 + 128 * h2:144 + 128 * h2]), (z2, T[z2][:, 0:128]), Fn.Sign, rd=["UT"], bias=-0.9 * 64.0 ** (6 + t))
-        mms("pF", fparts("VT", "GB32", LOW), ["VT", "VT.0", "GB32"])
-        mms("pF", fparts("UT", "GBH", HIGH), ["UT", "UT.1", "GBH"])
-        mms("pF", fparts("VT", "GB32", HIGH + MIXED), ["VT", "VT.0", "VT.1", "GB32"])
-        mms("pF", fparts("UT", "GBH", LOW + MIXED, True), ["UT", "UT.0", "UT.1", "GBH"])
-        F = ("pF", T.pF[:, 0:48])
-        ts(b("I48"), F, 12.0, None, Op.is_lt)
-        cp(b("FI"), F)
+            tt(b("UV", L + 128 * h, L + 128 * h + 128, "V.%d" % h), (z, T[z][:, 0:128]), b("BM", 128 * h, 128 * h + 128), Op.is_gt)
+        mms("pF", wrapped(T.pF[:, 0:32], "ZB", "UV", 32, False, True), ["ZB", "U.0", "U.1", "V.0", "V.1"])
+        F0 = ("pF", T.pF[:, 0:16])
+        NA = b("XZ", 112, 128)
+        ts(b("TH"), ("pF", T.pF[:, 0:32]), 0.75, None, Op.is_ge)
+        ts(b("RND"), F0, EVEN, -EVEN, Op.add, Op.add)
+        tt(NA, b("TH", 0, 16), b("TH", 16, 32), Op.max)
         if not last:
-            nt = "CST%d" % (t + 1)
-            mms("pF", [(T.pF[:, 64:66], T.IDB[:], ap(nt), True, False)] +
-                [(T.pF[:, 64:66], T.BD[:], T.I48[:, 16 + q:32:8], False, q == 7) for q in range(8)], ["IDB", nt, "BD", "I48"])
-        tt(b("SLM"), ("I48", T.I48[:, 16:32]), b("DD"), Op.mult)
-        ts(b("Q1"), b("FI"), 80, None, Op.bitwise_and)
-        ts(b("Q2"), b("FI"), 81, None, Op.bitwise_and)
-        expand("LH2", "SLM")
-        mms("pM", [(T.pM[:, 48:64], T.IDF[:], T.LW[:], True, False)] +
-            [(T.pM[:, 48 + 8 * h:56 + 8 * h], T.LH2[:, 128 * h:128 * h + 128], T.GF[:], False, h == 1) for h in range(2)], ["IDF", "LW", "LH2", "GF"])
-        ts(b("TBB"), b("Q1"), 16.0, None, Op.is_equal)
-        ts(b("OBB"), b("Q2"), 1.0, None, Op.is_equal)
-        if not last:
-            place(t + 1)
-        tt(b("TORN"), b("TBB"), b("I48"), Op.max)
-        tt(b("BO"), b("OBB"), b("I48"), Op.is_gt)
-        if not last:
-            sel1(t + 1)
-        tt(b("RMV"), ("BO", T.BO[:, 0:32]), ("TORN", T.TORN[:, 16:48]), Op.mult)
-        tt(b("P2"), ("TORN", T.TORN[:, 16:32]), ("D12", T.D12[:, 16:32]), Op.mult)
-        tt(b("P1"), b("RMV"), b("D12"), Op.mult)
-        if not last:
-            sel2(t + 1)
-        tt(b("DL1"), ("P1", T.P1[:, 0:16]), ("P1", T.P1[:, 16:32]), Op.add)
-        if not last:
-            tt(b("EQP"), b("PL%d" % (t + 1)), b("PL%d" % t), Op.is_equal)
-        tt(b("DL"), b("DL1"), b("P2"), Op.add)
-        cp(b("SL"), ("pM", T.pM[:, 48:64]))
+            mms("pD", [(T.pD[:, L:L + 2], T.IDB[:], T.CST[:, t + 1:t + 3], True, False)] +
+                [(T.pD[:, L:L + 2], T.XZ[:, 112 - 16 * q:240 - 16 * q], T.N16[:], False, q == 7) for q in range(8)], ["IDB", "CST", "XZ", "N16"])
+        tt(b("ODD"), F0, b("RND"), Op.not_equal)
+        tt(b("TORN"), F0, NA, Op.is_ge)
         if last:
-            scatter_R()
+            tt(b("PP", 16, 32, "PP.1"), NA, ("pM", T.pM[:, 32:48]), Op.mult)
+        else:
+            tt(b("MB", 16, 32, "MB.1"), b("TH", 0, 16), b("TH", 16, 32), Op.max, rd=["MB"])
+        tt(b("CAND"), b("ODD"), b("TORN"), Op.is_gt)
+        if last:
+            tt(b("QQ", 16, 32, "QQ.1"), b("PP", 16, 32, "PP.1"), CW, Op.add)
+        else:
+            ts(b("RR"), ("pD", T.pD[:, L:L + 2]), MAG, -MAG, Op.add, Op.add)
+        tt(b("MB", 33, 48, "MB.2"), b("CAND", 0, 15), b("TORN", 1, 16), Op.mult, rd=["MB"])
+        if last:
+            cp(b("SL"), b("QQ", 16, 32, "QQ.1"))
+        else:
+            ts(b("OFF%d" % (t + 1)), ("pD", T.pD[:, L:L + 2]), col("RR"), 127.5, Op.subtract, Op.add, rd=["RR"])
+        tt(b("MB", 0, 16, "MB.0"), b("TORN"), b("MB", 33, 49, "MB.2"), Op.add)
+        if last:
+            scatter("R", "NVR")
             deps("a", ["R"], [])
             A.dma_start(T.yr[:], T.R[:, 0:W]).then_inc(T.sem.stR, 16)
-            update_S(t)
-            cp(b("SF"), S)
-            mms("pK", [(T.pK[:, 128 * h:128 * h + 128], T.SF[:, 128 * h:128 * h + 128], T.IDH[:], True, True) for h in range(2)], ["SF", "IDH"])
-            cp(b("XS"), ("pK", T.pK[:, 0:L]))
+        tt(b("PP", 0, 48), b("MB", 0, 48, "MB.0"), ("pM", T.pM[:, 16:64]), Op.mult, rd=["MB.1", "MB.2", "QQ.1"])
+        tt(b("QQ"), b("PP", 0, 32), b("PP", 32, 64), Op.add, rd=["CW", "SL"])
+        if last:
+            tt(b("NEW"), b("QQ", 0, 16), CW, Op.add)
+            cp(b("NU"), b("NEW"))
+            tt(b("GN"), by("IDX", T.NU[:]), b("HI"), Op.min, rd=["NU"])
+            tt(b("XS"), b("GN"), H, Op.max)
             deps("s", ["XS"], [])
             g.sync.dma_start(T.ys[:], T.XS[:]).then_inc(T.sem.stS, 16)
             break
-        for h in range(2):
-            ts(("ED.%d" % h, T.ED[:, 8 * h:8 * h + 8]), ("DL", T.DL[:, 8 * h:8 * h + 8]), T.EQP[:, h:h + 1], None, Op.mult, rd=["EQP"])
-        tt(b("CC"), ("CS", T.CS[:, 15::16]), b("ED"), Op.add, rd=["ED.0", "ED.1"])
-        expand("LH", "CC")
-        wrap(t + 1)
-        op("v", ["RCE", "BT%d" % t, "SL"], ["E"], lambda: V.tensor_tensor(T.E[:].indirect(T.SL[:]), T.RCE[:], ap("BT%d" % t), Op.add))
-        cp(b("CL%d" % (t + 1)), ("pM", T.pM[:, 16:32]))
+        op("v", ["QQ", "CW", "OFF%d" % t], ["SP"], lambda: V.tensor_tensor(T.SP[:].indirect(off), T.QQ[:, 0:16], CW[1], Op.add))
+        cp(b("SL"), b("QQ", 16, 32))
+        cp(b("CL%d" % (t + 1)), by("SP", ap("OFF%d" % (t + 1), 0, 1)), rd=["OFF%d" % (t + 1)])
         send_list(t + 1)
-        op("v", ["KV", "SL"], ["K"], lambda: V.tensor_copy(T.K[:].indirect(T.SL[:]), T.KV[:]))
+        scatter("K", "KV")
         kin_gather("KL", "CL%d" % (t + 1))
+        scatter("R", "NVR")
 
     g.wait_ge(T.sem.loc, LOC["n"])
     A.wait_ge(T.sem.stR, 16)

@@ -6,11 +6,19 @@ NR, RO, W, L = 8, 4, 2048, 256
 TOP, STEP = 100.0, 0.8
 WX = W + 3 * L
 CH = 64
-VX = 192
-CMP1 = 8
-XA, XA0 = 2, 2
-B1 = 2
-OWN_FIRST = 1
+VX = 224
+CMP1 = 16
+XA, XA0 = 1, 0
+B1 = 3
+KOFF = 64.0
+LOW_EARLY = 0
+CREP_FIRST = 0
+ORDER = "nvr rm ni vt bk lh th rnd na odd torn cand slf moved sl rr tm off"
+ORDER_LAST = "nvr rm ni vt bk lh th rnd na odd torn slf cand sl moved tm"
+OWN_V0 = 0
+XV0 = (1, 1)
+OWN_FIRST0 = 1
+OWN_FIRST = 2
 
 SCRATCH = {}
 
@@ -21,7 +29,8 @@ def _s(name, cols, dtype="float32", where="sbuf"):
 
 _s("R", WX, "bfloat16")
 _s("X", W, "bfloat16")
-_s("K", WX, "int32")
+_s("KI", W, "int32")
+_s("K", WX)
 _s("SN", L, "int32")
 _s("IDX", W)
 for _n in ("GO", "GA0", "GA1", "Y", "XR"):
@@ -50,31 +59,31 @@ _many("DGB", ["DN%d" % t for t in range(3)] + ["DI%d" % t for t in range(3)], 12
 _many("OFB", ["OFF%d" % t for t in _TT], 2, "uint16")
 for _n in ("CREP", "KCF", "LH", "SF", "SM", "TR"):
     _s(_n, L, "float16")
-for _n in ("KV", "RM", "NI", "DK", "BK", "XS", "SP", "HI", "GN"):
+for _n in ("KV", "RM", "BK", "XS", "SP", "HI", "GN"):
     _s(_n, L)
-for _n in ("RCE", "NVR", "MK0", "NTH", "CK", "OB", "BM", "RST", "JF", "BF", "DG", "D"):
+for _n in ("RCE", "NVR", "MK0", "NTH", "CK", "OB", "BM", "RST", "JF", "BF", "DG", "D", "NT", "NI"):
     _s(_n, L, "bfloat16")
-for _n in ("UV", "NT"):
-    _s(_n, 2 * L, "bfloat16")
+_s("UV", 2 * L, "bfloat16")
 _s("ROT", L, "float16")
-for _n in ("IDH", "IDS", "IDN", "PERM"):
+for _n in ("IDH", "IDS", "PERM", "BDH"):
     _s(_n, 128, "float16")
-for _n in ("IDB", "BDN", "CB"):
+for _n in ("IDB", "BDN", "CB", "IDN", "IDL", "IDP"):
     _s(_n, 128, "bfloat16")
 _s("ZH", 144, "float16")
 _s("ZB", 144, "bfloat16")
-_s("XZ", 240, "bfloat16")
-for _n in ("G8", "PB", "ISN"):
+_s("XZ", 48, "bfloat16")
+_s("DW", 16, "bfloat16")
+_s("WB", 2)
+for _n in ("G8", "ISN"):
     _s(_n, 8)
-for _n in ("GHP", "GHN"):
-    _s(_n, 8, "float16")
+_s("GHN", 8, "float16")
 for _n in ("GB16", "CST"):
     _s(_n, 8, "bfloat16")
 for _n in ("PC", "PM"):
     _s(_n, 2, "int32")
 _s("PG", 1, "int32")
 _s("PMF", 2)
-for _n in ("PGF", "ZC", "WB", "RC"):
+for _n in ("PGF", "ZC", "RC"):
     _s(_n, 1)
 _s("N16", 2, "bfloat16")
 for _n in ("EXP", "SL", "NU"):
@@ -84,17 +93,18 @@ for _n in ("LWB", "RND", "NEG", "NEW", "EXI", "WT"):
 for _n in ("ODD", "TORN", "CAND"):
     _s(_n, 16, "bfloat16")
 _s("TH", 32, "bfloat16")
-_s("MB", 64, "bfloat16")
+_s("MB", 34, "bfloat16")
 _s("C32", 32, "bfloat16")
-_s("C3", 48, "float16")
-_s("CH", 32, "float16")
-_s("PP", 64)
-_s("QQ", 32)
+_s("C3", 16, "float16")
+_s("CH", 34, "float16")
+_s("PP", 32)
+for _n in ("QQ", "CW", "PD", "SLF"):
+    _s(_n, 16)
 _s("RR", 2)
 for _n in ("pZ", "pZ2", "pA", "pK", "pS", "pD", "pF", "pM"):
     _s(_n, 512, "float32", "psum")
 
-SEMAPHORES = ["sv", "sa", "sp", "sq", "loc", "ldS", "ldK", "ldR", "ldX", "stR", "stS"]
+SEMAPHORES = ["sv", "sa", "sp", "sq", "loc", "ldS", "ldK0", "ldK1", "ldR", "ldX", "stR", "stS"]
 SEMAPHORES += ["rq%d%d" % (t, k) for t in range(RO) for k in range(2)] + ["rs%d%d" % (t, k) for t in range(RO) for k in range(3)]
 
 
@@ -184,8 +194,8 @@ def rank_program(g, core, T, topo):
     def cp(o, i, rd=()):
         return op("v", [i[0]] + list(rd), [o[0]], lambda: V.tensor_copy(o[1], i[1]))
 
-    def scan(o, d0, d1):
-        return op("v", [d0[0], d1[0]], [o[0]], lambda: V.tensor_tensor_scan(o[1], d0[1], d1[1], 0.0, Op.mult, Op.max))
+    def scan(o, d0, d1, op0):
+        return op("v", [d0[0], d1[0]], [o[0]], lambda: V.tensor_tensor_scan(o[1], d0[1], d1[1], 0.0, op0, Op.max))
 
     def act(o, i, fn=Fn.Copy, rd=(), **kw):
         return op("a", [i[0]] + list(rd), [o[0]], lambda: A.activation(o[1], i[1], fn, **kw))
@@ -219,12 +229,13 @@ def rank_program(g, core, T, topo):
         return op("v", [], [o[0]], lambda: V.memset(o[1], val))
 
     g.sync.dma_start(T.SN[:], T.slips[:]).then_inc(T.sem.ldS, 16)
-    g.sync.dma_start(T.K[:, 0:W], T.kin[:]).then_inc(T.sem.ldK, 16)
+    for h in range(2):
+        g.sync.dma_start(T.KI[:, W // 2 * h:W // 2 * (h + 1)], T.kin[:, W // 2 * h:W // 2 * (h + 1)]).then_inc(T.sem["ldK%d" % h], 16)
+        landed("KI.%d" % h, "ldK%d" % h, 16)
     g.sync.dma_start(T.R[:, 0:W], T.rec[:]).then_inc(T.sem.ldR, 16)
     g.sync.dma_start(T.X[:], T.wealth[:]).then_inc(T.sem.ldX, 16)
     landed("SN", "ldS", 16)
     landed("R", "ldR", 16)
-    landed("K", "ldK", 16)
     landed("X", "ldX", 16)
 
     LOC = {"n": 0}
@@ -250,7 +261,7 @@ def rank_program(g, core, T, topo):
     def send_sums(t, k, lo, hi, n):
         asker = T.cores[(rank - 1 - ((2 * t + k) % 7)) % NR]
         rid, pid, _x = topo.addr(asker)
-        act(b("AS%d%d" % (t, k), lo, hi, "AS%d%d" % (t, n)), ("pA", T.pA[:, L * k + lo:L * k + hi]))
+        act(b("AS%d%d" % (t, k), lo, hi, "AS%d%d" % (t, n)), (("pA", "pK")[k], T[("pA", "pK")[k]][:, L * k + lo:L * k + hi]))
         deps("q", ["AS%d%d" % (t, n)], [])
         g.remote_dma(ap("RS%d%d" % (t, k), lo, hi), ap("AS%d%d" % (t, k), lo, hi), T.sem["rs%d%d" % (t, n)], T.sem.loc, pid, rid, topo.mask(core, asker))
         LOC["n"] += len(topo.engines(core, asker))
@@ -261,7 +272,7 @@ def rank_program(g, core, T, topo):
         return [(out, T[z][:, 15 - j:143 - j], T[src][:, j:16 * n:16], start and j == 0, fin and j == 15) for j in range(16)]
 
     def kin_gather(out, lst):
-        cp(b(out), by("K", ap(lst), W), rd=[lst])
+        ts(b(out), by("K", ap(lst), W), 0.25 - KOFF, None, Op.add, rd=[lst])
 
     H = ("pS", T.pS[:, L:2 * L])
 
@@ -281,10 +292,11 @@ def rank_program(g, core, T, topo):
     iota("PM", [[0, 2]], 0, 13)
     iota("JF", [[0, 16], [1, 16]], 0, 0)
     iota("D", [[1, L]], 0, -1)
-    iota("PB", [[L, 8]], 0, 1)
     iota("EXI", [[16, 16]], 15, 0)
-    iota("G8", [[1, 8]], 0, 0)
     iota("CB", [[1, 8], [0, 16]], 0, 0)
+    iota("G8", [[1, 8]], 0, 0)
+    iota("LWB", [[16, 16]], W, 1)
+    iota("BF", [[1, 16], [0, 16]], 0, 0)
     ts(b("PG"), b("PC", 0, 1), 4, None, Op.arith_shift_right)
     ts(b("PM", 1, 2), b("PM", 1, 2), 15, None, Op.bitwise_and)
     ts(b("PM", 0, 1), b("PC", 0, 1), 15, None, Op.bitwise_and)
@@ -292,61 +304,65 @@ def rank_program(g, core, T, topo):
     cp(b("PMF"), b("PM"))
     ts(b("ZC"), b("PMF", 0, 1), -1.0, 15.0, Op.mult, Op.add)
     ts(b("MK0"), b("JF"), col("PMF", 1), None, Op.is_equal, rd=["PMF"])
-    ts(b("ZH"), b("D", 0, 144), col("ZC"), None, Op.is_equal, rd=["ZC"])
     ln2 = math.log(2.0)
-    ts(b("WB"), b("PMF", 0, 1), -STEP * ln2, (TOP + 15 * STEP) * ln2, Op.mult, Op.add)
-    for nm in ("IDB", "IDH"):
-        ts(b(nm), b("D", 0, 128), 0.0, None, Op.is_equal)
-    ts(b("ISN", 0, 4, "IS"), b("JF", 0, 4), col("PMF"), None, Op.is_equal, rd=["PMF"])
-    ts(b("ISN", 4, 8, "NS"), b("JF", 0, 4), col("PMF"), None, Op.not_equal, rd=["PMF"])
-    ts(b("CH", 0, 2, "CH0"), b("PMF"), 0.0, None, Op.mult)
+    ts(b("WB", 0, 1, "WB.0"), b("PMF", 0, 1), -STEP * ln2, (TOP + 15 * STEP) * ln2, Op.mult, Op.add)
+    ts(b("WB", 1, 2, "WB.1"), b("PC", 0, 1), -STEP * ln2, TOP * ln2 + math.log(2.55), Op.mult, Op.add)
+    ts(b("RC"), b("PGF"), -15.0, None, Op.mult)
+    ts(b("ZH"), b("D", 0, 144), col("ZC"), None, Op.is_equal, rd=["ZC"])
+    ts(b("RC"), b("PMF", 0, 1), 7.0, col("RC"), Op.mult, Op.add, rd=["RC"])
+    ts(b("IDH"), b("D", 0, 128), 0.0, None, Op.is_equal)
     tt(b("SM"), b("SN"), b("MK0"), Op.mult)
     mms("pM", wrapped(T.pM[:, 0:16], "ZH", "SM", 16, True, True), ["ZH", "SM"])
-    ts(b("OFF0"), b("PMF"), col("PMF"), None, Op.min)
+    ts(b("BDH"), b("CB"), col("PGF"), None, Op.is_equal, rd=["PGF"])
+    for lo in (0, 128):
+        ts(b("ROT", lo, lo + 128), b("D", 0, 128), col("RC"), None, Op.is_equal, rd=["RC"])
     cp(b("CL0"), ("pM", T.pM[:, 0:16]))
     send_list(0)
 
-    iota("BF", [[1, 16], [0, 16]], 0, 0)
-    iota("LWB", [[32, 16]], W, 2)
-    act(b("WT"), b("EXI"), Fn.Exp, rd=["WB"], scale=-STEP * ln2, bias=col("WB"))
-    for k in range(W // L):
-        act(b("IDX", L * k, L * k + L), b("D"), Fn.Identity, rd=["PB"], bias=col("PB", k))
-        if k == 0:
-            act(b("NTH"), b("IDX", 0, L), Fn.Exp, scale=-STEP * ln2, bias=TOP * ln2 + math.log(2.55))
-    cp(b("SF"), b("SN"))
-    ts(b("RC"), b("PGF"), -15.0, None, Op.mult)
-    ts(b("RC"), b("PMF", 0, 1), 7.0, col("RC"), Op.mult, Op.add, rd=["RC"])
-    for lo in (0, 128):
-        ts(b("ROT", lo, lo + 128), b("D", 0, 128), col("RC"), None, Op.is_equal, rd=["RC"])
+    def own_constants(t):
+        act(b("TB%d" % t), b("OB"), Fn.Identity, scale=float(8 + t))
+        if t < RO - 1:
+            act(b("DN%d" % t), b("IDB"), Fn.Identity, rd=["NS"], scale=col("ISN", 4 + t))
+            act(b("DI%d" % t), b("IDB"), Fn.Identity, rd=["IS"], scale=col("ISN", t))
+
+    iota("CK", [[0, 16], [-1, 16]], 15, 0)
+    for nm, x in (("MB", 0), ("N16", -16), ("NEG", -1), ("XZ", 0)):
+        iota(nm, [[0, SCRATCH[nm][1][1]]], x, 0)
+    act(b("WT"), b("EXI"), Fn.Exp, rd=["WB.0"], scale=-STEP * ln2, bias=col("WB"))
+    act(b("NTH"), b("D"), Fn.Exp, rd=["WB.1"], scale=-STEP * ln2, bias=col("WB", 1))
+    act(b("SF"), b("SN"))
+    mms("pK", [(T.pK[:, 0:L], T.BDH[:], T.SM[:], True, True)], ["BDH", "SM"])
     mms("pS", [(T.pS[:, L + 16 * j:L + 16 * j + 16], rot(j), T.SF[:, j::16], True, True) for j in range(16)], ["ROT", "SF"])
-    mms("pK", [(T.pK[:, 0:128], rot(0), T.IDH[:], True, True)], ["ROT", "IDH"])
+    act(b("CW"), ("pM", T.pM[:, 0:16]))
+    act(b("CREP"), ("pK", T.pK[:, 0:L]))
+    act(b("SZ", L, 2 * L), H)
+    act(b("K", 0, W // 2), b("KI", 0, W // 2, "KI.0"), Fn.Identity, bias=KOFF)
     for lo in (0, 2 * L):
         ts(b("SZ", lo, lo + L, "SZ0"), b("MK0"), 0.0, None, Op.mult)
-    ts(b("ZB"), b("ZH"), 1.0 / 32.0, None, Op.mult)
-    ts(b("IDS"), b("IDH"), 1.0 / 4096.0, None, Op.mult)
-    ts(b("IDN"), b("IDH"), -1.0, None, Op.mult)
-    ts(b("DG"), b("JF"), col("PMF"), None, Op.is_equal, rd=["PMF"])
-    ts(b("RST"), b("JF"), 1.0, None, Op.min)
-    ts(b("CK"), b("JF"), -1.0, 15.0, Op.mult, Op.add)
-    ts(b("CST"), b("EXI", 0, 8), col("PMF"), -142.5, Op.add, Op.add, rd=["PMF"])
-    for nm, x in (("XZ", 0.0), ("MB", 0.0), ("N16", -16.0), ("NEG", -1.0)):
-        fill(b(nm), x)
-    fill(b("C32", 0, 16, "C32.0"), 0.75)
-    fill(b("C32", 16, 32, "C32.1"), 19.75 / 16.0)
-    ts(b("BDN"), b("CB"), col("PGF"), -1.0, Op.is_equal, Op.mult, rd=["PGF"])
-    for nm, f in (("GB16", 16.0), ("GHP", 4096.0), ("GHN", -4096.0)):
-        ts(b(nm), b("G8"), col("PGF"), f, Op.is_equal, Op.mult, rd=["PGF"])
-    cp(b("EXP"), b("EXI"))
-    ts(b("C3"), b("MK0", 0, 48), 0.0, None, Op.mult)
-    cp(b("SZ", L, 2 * L), H)
     turn(lambda q: T.IDH[:, q::8])
-    kin_gather("KL", "CL0")
-    act(b("PERM"), ("pK", T.pK[:, 0:128]))
+    ts(b("IDB"), b("IDH"), 1.0, None, Op.mult)
+    ts(b("BDN"), b("BDH"), -1.0, None, Op.mult)
+    ts(b("ISN", 0, 4, "IS"), b("JF", 0, 4), col("PMF"), None, Op.is_equal, rd=["PMF"])
+    ts(b("ISN", 4, 8, "NS"), b("JF", 0, 4), col("PMF"), None, Op.not_equal, rd=["PMF"])
     ts(b("OB"), b("BF"), col("PMF"), None, Op.is_equal, rd=["PMF"])
-    cp(b("C3", 16, 32), b("LWB"))
-    ts(b("BM"), b("OB"), -1e29, 1e29, Op.mult, Op.add)
-    for t in range(RO):
-        ts(b("TB%d" % t), b("OB"), float(8 + t), None, Op.mult)
+    act(b("CH", 2, 18), b("CW"))
+    own_constants(0)
+
+    def more_constants():
+        ts(b("IDS"), b("IDH"), 1.0 / 4096.0, None, Op.mult)
+        ts(b("CH", 0, 2, "CH0"), b("PMF"), 0.0, None, Op.mult)
+        ts(b("OFF0"), b("PMF"), col("PMF"), None, Op.min)
+        for nm, src, f in (("ZB", "ZH", 1.0 / 32.0), ("IDN", "IDH", -1.0), ("IDL", "IDH", -2.0 ** 21), ("IDP", "IDH", 4096.0)):
+            ts(b(nm), b(src), f, None, Op.mult)
+        ts(b("DG"), b("JF"), col("PMF"), None, Op.is_equal, rd=["PMF"])
+        ts(b("RST"), b("JF"), 1.0, None, Op.min)
+        ts(b("CST"), b("EXI", 0, 8), col("PMF"), -142.5, Op.add, Op.add, rd=["PMF"])
+        fill(b("C32", 0, 16, "C32.0"), 0.75)
+        fill(b("C32", 16, 32, "C32.1"), 11.75 / 16.0)
+        for nm, f in (("GB16", 16.0), ("GHN", -4096.0)):
+            ts(b(nm), b("G8"), col("PGF"), f, Op.is_equal, Op.mult, rd=["PGF"])
+        cp(b("EXP"), b("EXI"))
+        ts(b("BM"), b("OB"), -1e29, 1e29, Op.mult, Op.add)
 
     def rec_piece(q, G, lst, lo, hi, t):
         o, i = ("%s.%d" % (G, lo), T[G][:, 16 * lo:16 * hi]), by("R", T[lst][:, lo:hi], W)
@@ -355,9 +371,9 @@ def rank_program(g, core, T, topo):
         else:
             ts(o, i, 1.0 / 128.0 - (5 + t), 0.0, Op.add, Op.max, rd=[lst])
 
-    def rec_sum(bank, c0, G, lo, hi, whole):
+    def rec_sum(bank, c0, G, lo, hi, whole, rd=()):
         parts = [(T[bank][:, c0:c0 + hi - lo], T.IDB[:], T[G][:, 16 * lo + m:16 * hi:16], whole and m == 0, whole and m == 15) for m in range(16)]
-        mms(bank, parts, ["%s.%d" % (G, lo), "IDB"])
+        mms(bank, parts, ["%s.%d" % (G, lo), "IDB"] + list(rd))
 
     def own_sum(c):
         rec_sum("pZ2" if CH * c >= 128 else "pZ", CH * c % 128, "GO", CH * c, CH * c + CH, False)
@@ -372,7 +388,7 @@ def rank_program(g, core, T, topo):
     def compare_lanes(lo, hi):
         for bb in range(lo, hi):
             n, o = L - 16 * bb, sum(L - 16 * x for x in range(bb))
-            ts(("EQ.%d" % bb, T.EQ[:, o:o + n]), ("CREP", T.CREP[:, 16 * bb:L]), col("PP", 48 + bb), col("WT", bb), Op.is_equal, Op.mult, rd=["CW", "WT"])
+            ts(("EQ.%d" % bb, T.EQ[:, o:o + n]), ("CREP", T.CREP[:, 16 * bb:L]), col("CW", bb), col("WT", bb), Op.is_equal, Op.mult, rd=["CW", "WT"])
 
     def count_lanes(lo, hi):
         if lo == 0:
@@ -383,7 +399,7 @@ def rank_program(g, core, T, topo):
 
     def best_half(h):
         sl = slice(2048 * h, 2048 * h + 2048)
-        tt(("Y.%d" % h, T.Y[:, sl]), by("X", T.KL[:, 128 * h:128 * h + 128]), ("XR", T.XR[:, sl]), Op.max, rd=["KL"])
+        tt(("Y.%d" % h, T.Y[:, sl]), by("X", T.KL[:, 128 * h:128 * h + 128]), ("XR.%d" % h, T.XR[:, sl]), Op.max, rd=["KL"])
 
     def best_sum(h):
         parts = []
@@ -393,7 +409,7 @@ def rank_program(g, core, T, topo):
 
     MAG = 1.5 * 2.0 ** 31
     EVEN = 1.5 * 2.0 ** 20
-    CW = ("CW", T.PP[:, 48:64])
+    CW = b("CW")
     NOWN = L // CH
 
     for t in range(RO):
@@ -402,155 +418,217 @@ def rank_program(g, core, T, topo):
         off = ap("OFF%d" % t, 0, 1)
 
         def wealth(na):
-            act(("XR", T.XR[:, 0::16]), by("X", ap(cl)), rd=[cl])
-            for n, st in enumerate((8, 4, 2, 1)):
-                if n < na:
-                    act(("XR", T.XR[:, st::2 * st]), ("XR", T.XR[:, 0::2 * st]))
-                else:
-                    op("q", ["XR"], ["XR"], lambda: g.affine_select(T.XR[:, st::2 * st], T.XR[:, 0::2 * st], [[0, 8 * L // st]], Op.is_ge, 0.0, 0, 0))
+            op("a", ["X", cl], ["XR.0", "XR.1"], lambda: A.activation(T.XR[:, 0::16], T.X[:].indirect(ap(cl)), Fn.Copy))
+            for st in (8, 4, 2, 1)[:na]:
+                op("a", [], ["XR.0", "XR.1"], lambda: A.activation(T.XR[:, st::2 * st], T.XR[:, 0::2 * st], Fn.Copy))
+            for h in range(2):
+                for st in (8, 4, 2, 1)[na:4 - (XV0[h] if t == 0 else 0)]:
+                    lo, hi = 8 * L * h, 8 * L * h + 8 * L
+                    op("q", [], ["XR.%d" % h], lambda: g.affine_select(T.XR[:, lo + st:hi:2 * st], T.XR[:, lo:hi:2 * st], [[0, 4 * L // st]], Op.is_ge, 0.0, 0, 0))
 
-        drawn = ("pM", T.pM[:, 0:16]) if t == 0 else by("SP", off)
-        act(CW, drawn, rd=["OFF%d" % t])
-        act(b("CH", 2, 18), drawn, rd=["OFF%d" % t])
-        act(b("CREP"), by("IDX", ap(cl)), rd=[cl])
+        def kin_numbers():
+            mms("pS", [(T.pS[:, 0:L], T.IDH[:], T.SZ[:, 0:L], True, False)] +
+                [(T.pS[:, 128 * h:128 * h + 128], T.KCF[:, 128 * h:128 * h + 128], T.IDS[:], False, False) for h in range(2)], ["IDH", "SZ0", "KCF", "IDS"])
+
+        def kin_moves():
+            if t == RO - 2:
+                mms("pM", [(T.pM[:, 384:512], rot(0), T.IDH[:], True, True)], ["ROT", "IDH"])
+            if not last:
+                mms("pM", [(T.pM[:, 128:128 + L], ap("DN%d" % t), T.KCF[:], True, False)] +
+                    [(T.pM[:, 128 + e:128 + L:2], ap("DI%d" % t), T.CREP[:, 1 - e::2], False, e == 1) for e in range(2)],
+                    ["DN%d" % t, "DI%d" % t, "KCF", "CREP"])
+
+        first = OWN_FIRST if t else OWN_FIRST0
+        cmp1 = CMP1 if t else 16
         if t:
+            act(CW, by("SP", off), rd=["OFF%d" % t])
+            if CREP_FIRST:
+                act(b("CREP"), by("IDX", ap(cl)), rd=[cl])
             wealth(XA)
+            if not CREP_FIRST:
+                act(b("CREP"), by("IDX", ap(cl)), rd=[cl])
+            if last:
+                op("v", ["NEG", "OFF%d" % t], ["SP"], lambda: V.tensor_copy(T.SP[:].indirect(off), T.NEG[:]))
+                scatter("R", "NVR")
+                act(b("SZ", L, 2 * L), b("SP"))
+                turn(lambda q: T.IDH[:, 16 * q:16 * q + 16])
+            act(b("CH", 2, 18), CW)
+            cp(b("KCF"), b("KL"))
+            compare_lanes(0, cmp1)
         else:
-            for x in range(RO - 1):
-                act(b("DN%d" % x), b("IDB"), Fn.Identity, rd=["NS"], scale=col("ISN", 4 + x))
-                act(b("DI%d" % x), b("IDB"), Fn.Identity, rd=["IS"], scale=col("ISN", x))
-            act(b("SP"), H)
+            act(b("K", W // 2, W), b("KI", W // 2, W, "KI.1"), Fn.Identity, bias=KOFF)
+            compare_lanes(0, cmp1)
+            more_constants()
+            kin_gather("KL", "CL0")
         act(b("RCE"), by("R", ap(cl), W), Fn.Relu, rd=[cl], bias=1.0 / 128.0 - (5 + t))
-        for c in range(OWN_FIRST):
+        for c in range(first):
             rec_piece("a", "GO", "KL", CH * c, CH * c + CH, t)
-        if t == 0:
-            wealth(XA0)
         for lo in (0, 128):
             add_sums("RCE", "RCE", lo, lo + 128, True, False)
-        cp(b("KCF"), b("KL"))
-        if last:
-            op("v", ["NEG", "OFF%d" % t], ["SP"], lambda: V.tensor_copy(T.SP[:].indirect(off), T.NEG[:]))
-            cp(b("SZ", L, 2 * L), b("SP"))
-            turn(lambda q: T.IDH[:, 16 * q:16 * q + 16])
-        compare_lanes(0, CMP1)
-        count_lanes(0, CMP1)
-        for c in range(OWN_FIRST):
+        if 0 < t < RO - 1:
+            kin_moves()
+            kin_numbers()
+        count_lanes(0, cmp1)
+        for c in range(first):
             own_sum(c)
         for k in range(2):
             kin_gather("AK%d" % k, "RQ%d%d" % (t, k))
-        compare_lanes(CMP1, 16)
-        count_lanes(CMP1, 16)
-        vp = [(0, CH), (CH, VX)] if VX < 3 * CH else [(0, CH), (CH, 2 * CH), (2 * CH, VX)]
-        rec_piece("a", "GA0", "AK0", VX, L, t)
-        act(b("NT", L, 2 * L, "NT.1"), ("pD", T.pD[:, 0:L]), Fn.Sign, scale=-1.0)
+        if t == 0:
+            cp(b("KCF"), b("KL"))
+            cp(b("SP"), H)
+            kin_moves()
+            kin_numbers()
+        compare_lanes(cmp1, 16)
+        count_lanes(cmp1, 16)
+        x0, x1 = L - VX, L - VX + CH
+        vp = [(x0, x1), (x1, (x1 + L) // 4 * 2), ((x1 + L) // 4 * 2, L)]
+        rec_piece("a", "GA0", "AK0", 0, x0, t)
+        if t == 0:
+            wealth(XA0)
         for lo, hi in vp:
             rec_piece("v", "GA0", "AK0", lo, hi, t)
-        rec_sum("pA", VX, "GA0", VX, L, True)
+        if t == 0:
+            for c in range(first, first + OWN_V0):
+                rec_piece("v", "GO", "KL", CH * c, CH * c + CH, t)
         for c in range(NOWN):
             rec_piece("a", "GA1", "AK1", CH * c, CH * c + CH, t)
             if c == NOWN - 1:
                 send_sums(t, 1, 0, L - CH, 1)
-            if c < len(vp):
-                rec_sum("pA", vp[c][0], "GA0", vp[c][0], vp[c][1], True)
-            if c == len(vp):
                 send_sums(t, 0, 0, L, 0)
-            rec_sum("pA", L + CH * c, "GA1", CH * c, CH * c + CH, True)
-        act(b("NT", 0, L, "NT.0"), b("NT", L, 2 * L, "NT.1"), Fn.Identity, scale=-2.0 ** 21, bias=-2.0 ** 21)
+            if c == 0:
+                rec_sum("pA", 0, "GA0", 0, x1, True, ["GA0.%d" % x0])
+            if c == 1:
+                rec_sum("pA", vp[1][0], "GA0", vp[1][0], vp[1][1], True)
+            rec_sum("pK", L + CH * c, "GA1", CH * c, CH * c + CH, True)
+            if c == 2:
+                rec_sum("pA", vp[2][0], "GA0", vp[2][0], L, True)
+        act(b("NT"), ("pD", T.pD[:, 0:L]), Fn.Sign, scale=-1.0)
         send_sums(t, 1, L - CH, L, 2)
         if last:
             act(b("TR"), H)
+        mms("pD", wrapped(T.pD[:, L + 16:L + 32], "ZB", "NT", 16, True, True), ["ZB", "NT"])
+        if t == 0:
+            iota("IDX", [[1, W]], 0, 0)
+            for c in range(first, first + OWN_V0):
+                own_sum(c)
+            first += OWN_V0
+        if last:
             mms("pS", [(T.pS[:, L + j:2 * L:16], rot(-j), T.TR[:, 16 * j:16 * j + 16], True, True) for j in range(16)], ["ROT", "TR"])
-        mms("pS", [(T.pS[:, 128 * h:128 * h + 128], T.KCF[:, 128 * h:128 * h + 128], T.IDS[:], True, True) for h in range(2)], ["KCF", "IDS"])
-        if not last:
-            mms("pM", [(T.pM[:, 128:128 + L], ap("DN%d" % t), T.KCF[:], True, False)] +
-                [(T.pM[:, 128 + e:128 + L:2], ap("DI%d" % t), T.CREP[:, 1 - e::2], False, e == 1) for e in range(2)],
-                ["DN%d" % t, "DI%d" % t, "KCF", "CREP"])
-        mms("pF", [(T.pF[:, 0:32], T.IDB[:], T.C32[:], True, False)] + wrapped(T.pF[:, 0:32], "ZB", "NT", 32, False, False),
-            ["IDB", "C32.0", "C32.1", "ZB", "NT.0", "NT.1"])
+            kin_moves()
         mms("pK", [(T.pK[:, 0:L], T.IDB[:], T.CK[:], True, False)], ["IDB", "CK"])
-        best_half(0)
-        best_half(1)
+        for h in range(2):
+            for st in (8, 4, 2, 1)[4 - (XV0[h] if t == 0 else 0):]:
+                lo, hi = 8 * L * h, 8 * L * h + 8 * L
+                cp(("XR.%d" % h, T.XR[:, lo + st:hi:2 * st]), ("XR.%d" % h, T.XR[:, lo:hi:2 * st]))
+            best_half(h)
         best_sum(0)
-        for c in range(OWN_FIRST, NOWN):
+        for c in range(first, NOWN):
             rec_piece("a", "GO", "KL", CH * c, CH * c + CH, t)
-            if c == OWN_FIRST:
+            if c == first:
+                act(b("DW"), ("pD", T.pD[:, L + 16:L + 32]), Fn.Identity, bias=0.5)
+                mms("pF", [(T.pF[:, 0:32], T.IDB[:], T.C32[:], True, False), (T.pF[:, 0:16], T.IDL[:], T.DW[:], False, False),
+                           (T.pF[:, 16:32], T.IDB[:], T.DW[:], False, False)], ["IDB", "IDL", "C32.0", "C32.1", "DW"])
                 if last:
                     act(b("SF"), H)
                     mms("pS", [(H[1], T.PERM[:], T.SF[:], True, True)], ["PERM", "SF"])
-                else:
-                    act(b("KV"), ("pM", T.pM[:, 128:128 + L]))
             if c == B1:
                 best_sum(1)
-            if c == NOWN - 1:
-                add_sums("RS%d0" % t, "RS%d0" % t, 0, 128, False, False)
-                add_sums("RS%d1" % t, "RS%d1" % t, 0, 128, False, True)
-                add_sums("RS%d0" % t, "RS%d0" % t, 128, L, False, False)
-                add_sums("RS%d1" % t, "RS%d1" % t, 128, L - CH, False, False)
+                if last:
+                    ts(b("HI"), H, 0.0, 4096.0, Op.is_lt, Op.mult)
+                    kin_numbers()
+            if c == NOWN - 1 and LOW_EARLY:
+                add_sums("RS%d1" % t, "RS%d1" % t, 0, 128, False, False)
+                add_sums("RS%d0" % t, "RS%d0" % t, 0, 128, False, True)
             own_sum(c)
-        tt(b("NVR"), by("R", ap(cl), W), b("TB%d" % t), Op.max, rd=[cl])
-        if last:
-            ts(b("HI"), H, 0.0, 4096.0, Op.is_lt, Op.mult)
+        if not LOW_EARLY:
+            add_sums("RS%d1" % t, "RS%d1" % t, 0, 128, False, False)
+            add_sums("RS%d0" % t, "RS%d0" % t, 0, 128, False, True)
+        add_sums("RS%d0" % t, "RS%d0" % t, 128, L, False, False)
+        add_sums("RS%d1" % t, "RS%d1" % t, 128, L - CH, False, False)
         add_sums("RS%d1" % t, "RS%d2" % t, L - CH, L, False, True)
         for h, z in ((0, "pZ"), (1, "pZ2")):
             act(b("UV", 128 * h, 128 * h + 128, "U.%d" % h), (z, T[z][:, 0:128]), Fn.Sign, bias=-0.7)
-        scan(b("RM"), b("RST"), ("pK", T.pK[:, 0:L]))
-        tt(b("NI"), ("pK", T.pK[:, 0:L]), b("RM"), Op.not_equal)
-        tt(b("DK"), ("pS", T.pS[:, 0:L]), b("NI"), Op.subtract)
-        scan(b("BK"), b("NI"), b("DK"))
-        tt(b("LH"), by("BK", T.EXP[:]), b("DG"), Op.mult, rd=["EXP"])
-        mms("pM", [(T.pM[:, 16:64], T.IDH[:], T.C3[:], True, False)] +
-            [(T.pM[:, lo:lo + 16], T.IDN[:], T.CH[:, 2:18], False, False) for lo in (16, 32)] + [(T.pM[:, 48:64], T.IDH[:], T.CH[:, 1:17], False, False)] +
-            [(T.pM[:, lo + 8 * h:lo + 8 * h + 8], T.LH[:, 128 * h:128 * h + 128], T[w][:], False, lo == 48 and h == 1) for lo, w in ((16, "GHP"), (48, "GHN")) for h in range(2)],
-            ["IDH", "IDN", "C3", "CH", "CH0", "LH", "GHP", "GHN"])
-        for h, z in ((0, "pZ"), (1, "pZ2")):
-            tt(b("UV", L + 128 * h, L + 128 * h + 128, "V.%d" % h), (z, T[z][:, 0:128]), b("BM", 128 * h, 128 * h + 128), Op.is_gt)
-        mms("pF", wrapped(T.pF[:, 0:32], "ZB", "UV", 32, False, True), ["ZB", "U.0", "U.1", "V.0", "V.1"])
-        F0 = ("pF", T.pF[:, 0:16])
-        NA = b("XZ", 112, 128)
-        ts(b("TH"), ("pF", T.pF[:, 0:32]), 0.75, None, Op.is_ge)
-        ts(b("RND"), F0, EVEN, -EVEN, Op.add, Op.add)
-        tt(NA, b("TH", 0, 16), b("TH", 16, 32), Op.max)
         if not last:
-            mms("pD", [(T.pD[:, L:L + 2], T.IDB[:], T.CST[:, t + 1:t + 3], True, False)] +
-                [(T.pD[:, L:L + 2], T.XZ[:, 112 - 16 * q:240 - 16 * q], T.N16[:], False, q == 7) for q in range(8)], ["IDB", "CST", "XZ", "N16"])
-        tt(b("ODD"), F0, b("RND"), Op.not_equal)
-        tt(b("TORN"), F0, NA, Op.is_ge)
+            act(b("KV"), ("pM", T.pM[:, 128:128 + L]), Fn.Identity, bias=KOFF)
+            own_constants(t + 1)
+        if t == RO - 2:
+            act(b("PERM"), ("pM", T.pM[:, 384:512]))
+        F0 = ("pF", T.pF[:, 0:16])
+        NA = b("XZ", 16, 32)
+
+        def less_key():
+            tt(b("NI"), b("RM"), ("pK", T.pK[:, 0:L]), Op.subtract)
+            mms("pS", [(T.pS[:, 0:L], T.IDN[:], T.NI[:], False, True)], ["IDN", "NI"])
+
+        def less_best():
+            tt(b("LH"), by("BK", T.EXP[:]), b("DG"), Op.mult, rd=["EXP"])
+            mms("pM", [(T.pM[:, 16:48], T.IDH[:], T.SZ[:, 0:32], True, False), (T.pM[:, 16:32], T.IDH[:], T.CH[:, 2:18], False, False),
+                       (T.pM[:, 32:48], T.IDH[:], T.CH[:, 1:17], False, False)], ["IDH", "SZ0", "CH", "CH0"])
+            mms("pM", [(T.pM[:, lo + 8 * h:lo + 8 * h + 8], T.LH[:, 128 * h:128 * h + 128], T.GHN[:], False, lo == 32 and h == 1) for lo in (16, 32) for h in range(2)],
+                ["LH", "GHN"])
+
+        def bars():
+            for h, z in ((0, "pZ"), (1, "pZ2")):
+                tt(b("UV", L + 128 * h, L + 128 * h + 128, "V.%d" % h), (z, T[z][:, 0:128]), b("BM", 128 * h, 128 * h + 128), Op.is_gt)
+            mms("pF", wrapped(T.pF[:, 0:32], "ZB", "UV", 32, False, True), ["ZB", "U.0", "U.1", "V.0", "V.1"])
+
+        def not_installed():
+            tt(NA, b("TH", 0, 16), b("TH", 16, 32), Op.max)
+            mms("pA", [(T.pA[:, 0:16], T.IDH[:], T.CH[:, 2:18], True, False), (T.pA[:, 0:16], T.IDP[:], NA[1], False, True)], ["IDH", "CH", "IDP", "XZ"])
+            if not last:
+                mms("pD", [(T.pD[:, L:L + 2], T.IDB[:], T.CST[:, t + 1:t + 3], True, False)] +
+                    [(T.pD[32 * p:32 * p + 32, L:L + 2], T.XZ[:, 16 - 16 * e:48 - 16 * e], T.N16[:], False, e == 1) for p in range(4) for e in range(2)],
+                    ["IDB", "CST", "XZ", "N16"])
+
+        def targets():
+            cp(b("SL"), b("SLF"))
+            if last:
+                scatter("R", "NVR")
+                deps("a", ["R"], [])
+                A.dma_start(T.yr[:], T.R[:, 0:W]).then_inc(T.sem.stR, 16)
+            elif KOFF:
+                op("a", ["KV", "SL"], ["K"], lambda: A.activation(T.K[:].indirect(T.SL[:]), T.KV[:], Fn.Silu))
+
+        step = {
+            "nvr": lambda: tt(b("NVR"), by("R", ap(cl), W), b("TB%d" % t), Op.max, rd=[cl]),
+            "rm": lambda: scan(b("RM"), b("RST"), ("pK", T.pK[:, 0:L]), Op.mult),
+            "ni": less_key,
+            "bk": lambda: scan(b("BK"), b("NI"), ("pS", T.pS[:, 0:L]), Op.min),
+            "lh": less_best,
+            "vt": bars,
+            "th": lambda: ts(b("TH"), ("pF", T.pF[:, 0:32]), 0.75, None, Op.is_ge),
+            "rnd": lambda: ts(b("RND"), F0, EVEN, -EVEN, Op.add, Op.add),
+            "na": not_installed,
+            "odd": lambda: tt(b("ODD"), F0, b("RND"), Op.not_equal),
+            "torn": lambda: tt(b("TORN"), F0, NA, Op.is_ge),
+            "slf": lambda: tt(b("SLF"), ("pA", T.pA[:, 0:16]), b("LWB"), Op.min),
+            "cand": lambda: tt(b("CAND"), b("ODD"), b("TORN"), Op.is_gt),
+            "sl": targets,
+            "moved": lambda: tt(b("MB", 17, 32, "MB.1"), b("CAND", 0, 15), b("TORN", 1, 16), Op.mult, rd=["MB"]),
+            "rr": lambda: last or ts(b("RR"), ("pD", T.pD[:, L:L + 2]), MAG, -MAG, Op.add, Op.add),
+            "tm": lambda: tt(b("MB", 0, 16, "MB.0"), b("TORN"), b("MB", 17, 33, "MB.1"), Op.add),
+            "off": lambda: last or ts(b("OFF%d" % (t + 1)), ("pD", T.pD[:, L:L + 2]), col("RR"), 127.5, Op.subtract, Op.add, rd=["RR"]),
+        }
+        for name in (ORDER_LAST if last else ORDER).split():
+            step[name]()
+        tt(b("PP"), b("MB", 0, 32, "MB.0"), ("pM", T.pM[:, 16:48]), Op.mult, rd=["MB.1"])
+        tt(b("QQ"), b("PP", 16, 32), b("PP", 0, 16), Op.subtract)
         if last:
-            tt(b("PP", 16, 32, "PP.1"), NA, ("pM", T.pM[:, 32:48]), Op.mult)
-        else:
-            tt(b("MB", 16, 32, "MB.1"), b("TH", 0, 16), b("TH", 16, 32), Op.max, rd=["MB"])
-        tt(b("CAND"), b("ODD"), b("TORN"), Op.is_gt)
-        if last:
-            tt(b("QQ", 16, 32, "QQ.1"), b("PP", 16, 32, "PP.1"), CW, Op.add)
-        else:
-            ts(b("RR"), ("pD", T.pD[:, L:L + 2]), MAG, -MAG, Op.add, Op.add)
-        tt(b("MB", 33, 48, "MB.2"), b("CAND", 0, 15), b("TORN", 1, 16), Op.mult, rd=["MB"])
-        if last:
-            cp(b("SL"), b("QQ", 16, 32, "QQ.1"))
-        else:
-            ts(b("OFF%d" % (t + 1)), ("pD", T.pD[:, L:L + 2]), col("RR"), 127.5, Op.subtract, Op.add, rd=["RR"])
-        tt(b("MB", 0, 16, "MB.0"), b("TORN"), b("MB", 33, 49, "MB.2"), Op.add)
-        if last:
-            scatter("R", "NVR")
-            deps("a", ["R"], [])
-            A.dma_start(T.yr[:], T.R[:, 0:W]).then_inc(T.sem.stR, 16)
-        tt(b("PP", 0, 48), b("MB", 0, 48, "MB.0"), ("pM", T.pM[:, 16:64]), Op.mult, rd=["MB.1", "MB.2", "QQ.1"])
-        tt(b("QQ"), b("PP", 0, 32), b("PP", 32, 64), Op.add, rd=["CW", "SL"])
-        if last:
-            tt(b("NEW"), b("QQ", 0, 16), CW, Op.add)
+            tt(b("NEW"), b("QQ"), CW, Op.add)
             cp(b("NU"), b("NEW"))
             tt(b("GN"), by("IDX", T.NU[:]), b("HI"), Op.min, rd=["NU"])
             tt(b("XS"), b("GN"), H, Op.max)
             deps("s", ["XS"], [])
             g.sync.dma_start(T.ys[:], T.XS[:]).then_inc(T.sem.stS, 16)
             break
-        op("v", ["QQ", "CW", "OFF%d" % t], ["SP"], lambda: V.tensor_tensor(T.SP[:].indirect(off), T.QQ[:, 0:16], CW[1], Op.add))
-        cp(b("SL"), b("QQ", 16, 32))
+        op("v", ["QQ", "CW", "OFF%d" % t], ["SP"], lambda: V.tensor_tensor(T.SP[:].indirect(off), T.QQ[:], CW[1], Op.add))
         cp(b("CL%d" % (t + 1)), by("SP", ap("OFF%d" % (t + 1), 0, 1)), rd=["OFF%d" % (t + 1)])
         send_list(t + 1)
-        scatter("K", "KV")
+        if not KOFF:
+            scatter("K", "KV")
         kin_gather("KL", "CL%d" % (t + 1))
-        scatter("R", "NVR")
+        if t < RO - 2:
+            scatter("R", "NVR")
 
     g.wait_ge(T.sem.loc, LOC["n"])
     A.wait_ge(T.sem.stR, 16)

@@ -3,22 +3,37 @@ from concourse.bass import DstId, RemoteDMATransfer
 from concourse.mybir import dt, AluOpType as Op, ActivationFunctionType as Fn
 
 NR, RO, W, L = 8, 4, 2048, 256
-TOP, STEP = 100.0, 0.8
 WX = W + 3 * L
-CH = 64
-VX = 224
-CMP1 = 16
-XA, XA0 = 1, 0
-B1 = 3
 KOFF = 64.0
-LOW_EARLY = 0
-CREP_FIRST = 0
-ORDER = "nvr rm ni vt bk lh th rnd na odd torn cand slf moved sl rr tm off"
-ORDER_LAST = "nvr rm ni vt bk lh th rnd na odd torn slf cand sl moved tm"
-OWN_V0 = 0
-XV0 = (1, 1)
-OWN_FIRST0 = 1
-OWN_FIRST = 2
+EPS = 1.0 / 2048.0
+X0, XD = 10.0, 0.3
+BIG = 1024.0
+CELL = 8
+MOD = 129 * 256
+ZS = 192
+
+S0 = """
+idx Akl ch cmp +cmp rce0 rce1 rcm1 rcm0 Ao:0-64 mc Axr +o:0-64 Vak0 Ax0:0-256 Gx1:0-256 Gx2:0-256 Ao:64-120 Gx3:0-128 lc spc Vak1 Vkcf +o:64-120
+Ag0:0-64 +kcf Vg0:128-192 +g0:0-64 +g0:128-192 Ag0:64-128 Vg0:192-256 +g0:64-128 +g0:192-256 Ag1:0-64 Vg1:128-192 +g1:0-64 +g1:128-192 Ag1:64-128
+Ae0:0-256 s0:0-256 Vg1:192-256 +g1:64-128 nt +nt +g1:192-256 Ao:120-192 Ae1:0-256 s1:0-256 Vx3:128-256 Vy:0-128 +o:120-192 +y:0-128 Vy:128-256
+an00 an01 Ao:192-256 +o:192-256 k0 an10 u0 kv rc k1 an11 +y:128-256 rm0 ni0 v0 w1 cm v1 kx0 bm nvm rm1 bk0 dc ni1 fs rnd kx1 na naa rn2 bk1
+torn nl lh lhm odd slm wn nv sl ks rrv mv tw pm tb qq pp offv sp cl perm rcs
+"""
+S1 = """
+cw Acrep sr Axr Vkl Gx0:0-256 Gx1:0-256 Gx2:0-256 rce0 Gx3:0-128 Vkcf +kcf ch rce1 rcm0 rcm1 cmp +cmp Ao:0-88 Vak0 Aak1 +o:0-64 Vg0:128-192 Ag0:0-64
++g0:128-192 +g0:0-64 Vg0:192-256 Ag0:64-128 +g0:192-256 +g0:64-128 Vg1:128-192 Ag1:0-64 +g1:128-192 Ae0:0-256 s0:0-256 +g1:0-64 Gx3:128-256
+Vg1:192-256 Ag1:64-128 +g1:192-256 +g1:64-128 nt Ao:88-128 Vy:0-128 Ae1:0-256 s1:0-256 +nt an01 an00 Ao:128-192 +y:0-128 +o:64-192 Vy:128-224
+Ao:192-256 +y:128-224 Vy:224-256 kv an10 u0 +o:192-256 an11 +y:224-256 rm0 nvr ni0 kx0 v0 w1 v1 bm cm rm1 dc ni1 bk0 kx1 rnd fs na naa rn2 bk1 torn nl
+odd lh lhm slm wn sl ks rrv mv tw pm tb qq pp offv sp cl perm rcs
+"""
+S3 = """
+cw neg sz +sz Acrep Axr Vkl sr Gx0:0-256 Gx1:0-256 Gx2:0-256 Gx3:0-128 Vkcf ch rce1 rce0 rcm1 cmp rcm0 +cmp Ao:0-72 tr +tr +o:0-64 Vak0 Aak1 Ag0:0-64
+Vg0:128-192 sf +g0:0-64 Ag0:64-128 +sf Vg0:192-256 +g0:128-256 +g0:64-128 Ag1:0-64 Vg1:128-192 +g1:0-64 Ae0:0-256 Gx3:128-256 s0:0-256 Ag1:64-128
+Vg1:192-256 +g1:128-256 +g1:64-128 nt Ao:72-104 hi +hi Vy:0-128 Ae1:0-256 Vo:224-256 s1:0-256 +nt Ao:104-128 Ao:128-192 Vy:128-224 +y:0-128 an00
++o:64-128 nvr an01 +o:128-192 Ao:192-224 +o:192-256 an10 an11 u0 rm0 w1 v1 v0 bm cm Vy:224-256 ni0 +y:128-256 rnd fs na kx0 nl rn2 slm rm1 sl odd torn
+srl ni1 st bk0 kx1 wn bk1 mv lh lhm dc tw pm tb qq pp fin
+"""
+SEQ = [S0, S1, S1, S3]
 
 SCRATCH = {}
 
@@ -55,57 +70,54 @@ _many("RQB", ["RQ%d%d" % x for x in _TK], 16, "uint16")
 _many("RSB", ["RS%d%d" % x for x in _TK], L, "bfloat16")
 _many("ASB", ["AS%d%d" % x for x in _TK], L, "bfloat16")
 _many("TBF", ["TB%d" % t for t in _TT], L, "bfloat16")
-_many("DGB", ["DN%d" % t for t in range(3)] + ["DI%d" % t for t in range(3)], 128, "float16")
+_many("DGB", ["DN%d" % t for t in range(3)], 128, "float16")
 _many("OFB", ["OFF%d" % t for t in _TT], 2, "uint16")
-for _n in ("CREP", "KCF", "LH", "SF", "SM", "TR"):
+for _n in ("CREP", "KCF", "SF", "SM", "TR", "ROT"):
     _s(_n, L, "float16")
-for _n in ("KV", "RM", "BK", "XS", "SP", "HI", "GN"):
+for _n in ("KV", "RM", "KX", "XS", "SP", "HI", "GN"):
     _s(_n, L)
-for _n in ("RCE", "NVR", "MK0", "NTH", "CK", "OB", "BM", "RST", "JF", "BF", "DG", "D", "NT", "NI"):
+for _n in ("RCE", "RC", "NV", "MK0", "NTH", "BM", "RST", "JF", "BF", "D", "NT", "NI"):
     _s(_n, L, "bfloat16")
 _s("UV", 2 * L, "bfloat16")
-_s("ROT", L, "float16")
-for _n in ("IDH", "IDS", "PERM", "BDH"):
+for _n in ("IDH", "IDS", "PERM", "LH", "BDH"):
     _s(_n, 128, "float16")
-for _n in ("IDB", "BDN", "CB", "IDN", "IDL", "IDP"):
+for _n in ("IDB", "BDN", "IDN", "IDK"):
     _s(_n, 128, "bfloat16")
-_s("ZH", 144, "float16")
+for _n in ("ZH", "Z16"):
+    _s(_n, 144, "float16")
 _s("ZB", 144, "bfloat16")
+_s("ZG", 48, "float16")
 _s("XZ", 48, "bfloat16")
-_s("DW", 16, "bfloat16")
-_s("WB", 2)
-for _n in ("G8", "ISN"):
+_s("MB", 50, "bfloat16")
+_s("C32", 32, "bfloat16")
+_s("CH", 34, "float16")
+_s("BK", L + 8)
+for _n in ("ISN", "CSI"):
     _s(_n, 8)
-_s("GHN", 8, "float16")
 for _n in ("GB16", "CST"):
     _s(_n, 8, "bfloat16")
 for _n in ("PC", "PM"):
     _s(_n, 2, "int32")
-_s("PG", 1, "int32")
-_s("PMF", 2)
-for _n in ("PGF", "ZC", "RC"):
+for _n in ("PG", "PH", "PH2"):
+    _s(_n, 1, "int32")
+for _n in ("PMF", "WB"):
+    _s(_n, 2)
+for _n in ("PGF", "ZC", "RTC", "PHF", "PHG", "ZGC", "OBC"):
     _s(_n, 1)
-_s("N16", 2, "bfloat16")
+for _n in ("N16", "C2", "RR"):
+    _s(_n, 2, "bfloat16")
 for _n in ("EXP", "SL", "NU"):
     _s(_n, 16, "uint16")
-for _n in ("LWB", "RND", "NEG", "NEW", "EXI", "WT"):
+for _n in ("LWB", "RND", "NEG", "NEW", "WT", "WS", "QQ", "CW", "SLF", "NL", "DC", "PP", "PM1", "FS", "RN2"):
     _s(_n, 16)
-for _n in ("ODD", "TORN", "CAND"):
+for _n in ("ODD", "TORN", "TB"):
     _s(_n, 16, "bfloat16")
-_s("TH", 32, "bfloat16")
-_s("MB", 34, "bfloat16")
-_s("C32", 32, "bfloat16")
-_s("C3", 16, "float16")
-_s("CH", 34, "float16")
-_s("PP", 32)
-for _n in ("QQ", "CW", "PD", "SLF"):
-    _s(_n, 16)
-_s("RR", 2)
 for _n in ("pZ", "pZ2", "pA", "pK", "pS", "pD", "pF", "pM"):
     _s(_n, 512, "float32", "psum")
 
 SEMAPHORES = ["sv", "sa", "sp", "sq", "loc", "ldS", "ldK0", "ldK1", "ldR", "ldX", "stR", "stS"]
-SEMAPHORES += ["rq%d%d" % (t, k) for t in range(RO) for k in range(2)] + ["rs%d%d" % (t, k) for t in range(RO) for k in range(3)]
+SEMAPHORES += ["rq%d%d" % x for x in _TK]
+SEMAPHORES += ["rs%d%s_%s" % (t, w[1], w[3:].split("-")[0]) for t in _TT for w in SEQ[t].split() if w[:3] in ("s0:", "s1:")]
 
 
 def rank_program(g, core, T, topo):
@@ -135,16 +147,22 @@ def rank_program(g, core, T, topo):
             res[k] = {"w": None, "r": {}, "lw": {}}
         return res[k]
 
+    def flat(keys):
+        out = []
+        for k in keys:
+            out += k if isinstance(k, list) else [k]
+        return out
+
     def deps(q, reads, writes):
         d = []
-        for k in reads:
+        for k in flat(reads):
             e = entry(k)
             if k[0] == "p":
                 d += [tok for q2, tok in e["lw"].items() if not (q2 == q == "p")]
                 d += [tok for q2, tok in e["r"].items() if q2 != q]
             elif e["w"]:
                 d.append(e["w"])
-        for k in writes:
+        for k in flat(writes):
             e = entry(k)
             if k[0] == "p":
                 for m in ("lw", "r"):
@@ -166,9 +184,9 @@ def rank_program(g, core, T, topo):
         tok = (own[q], cnt[q])
         ins.then_inc(T.sem[own[q]], 1)
         snap[tok] = dict(known[q])
-        for k in reads:
+        for k in flat(reads):
             entry(k)["r"][q] = tok
-        for k in writes:
+        for k in flat(writes):
             e = entry(k)
             if k[0] == "p":
                 e["lw"][q] = tok
@@ -221,12 +239,18 @@ def rank_program(g, core, T, topo):
     def col(name, k=0):
         return T[name][:, k:k + 1]
 
+    def cells(name, lo, hi):
+        return ["%s.%d" % (name, c) for c in range(lo // CELL, (hi + CELL - 1) // CELL)]
+
     def iota(name, pattern, base, cm):
         kw = {} if SCRATCH[name][2] == "int32" else {"allow_small_or_imprecise_dtypes": True}
         return op("q", [], [name], lambda: g.iota(T[name][:], pattern, base, cm, **kw))
 
     def fill(o, val):
         return op("v", [], [o[0]], lambda: V.memset(o[1], val))
+
+    def copy(q):
+        return cp if q == "v" else act
 
     g.sync.dma_start(T.SN[:], T.slips[:]).then_inc(T.sem.ldS, 16)
     for h in range(2):
@@ -238,7 +262,7 @@ def rank_program(g, core, T, topo):
     landed("R", "ldR", 16)
     landed("X", "ldX", 16)
 
-    LOC = {"n": 0}
+    left = [0]
 
     def send_list(t):
         trs = []
@@ -254,27 +278,25 @@ def rank_program(g, core, T, topo):
                                          src=ap("CL%d" % t), dst=ap("RQ%d%d" % (t, k))))
             a = T.cores[(rank - 1 - ((2 * t + k) % 7)) % NR]
             landed("RQ%d%d" % (t, k), "rq%d%d" % (t, k), len(topo.engines(a, core)) // 2)
-            LOC["n"] += half
+            left[0] += half
         deps("q", ["CL%d" % t], [])
         g.remote_dma_fused(trs, local_sem=T.sem.loc)
 
-    def send_sums(t, k, lo, hi, n):
+    def send_sums(t, k, lo, hi):
         asker = T.cores[(rank - 1 - ((2 * t + k) % 7)) % NR]
         rid, pid, _x = topo.addr(asker)
-        act(b("AS%d%d" % (t, k), lo, hi, "AS%d%d" % (t, n)), (("pA", "pK")[k], T[("pA", "pK")[k]][:, L * k + lo:L * k + hi]))
-        deps("q", ["AS%d%d" % (t, n)], [])
-        g.remote_dma(ap("RS%d%d" % (t, k), lo, hi), ap("AS%d%d" % (t, k), lo, hi), T.sem["rs%d%d" % (t, n)], T.sem.loc, pid, rid, topo.mask(core, asker))
-        LOC["n"] += len(topo.engines(core, asker))
+        sem = "rs%d%d_%d" % (t, k, lo)
+        deps("q", cells("AS%d%d" % (t, k), lo, hi), [])
+        g.remote_dma(ap("RS%d%d" % (t, k), lo, hi), ap("AS%d%d" % (t, k), lo, hi), T.sem[sem], T.sem.loc, pid, rid, topo.mask(core, asker))
+        left[0] += len(topo.engines(core, asker))
         q = T.cores[(rank + 1 + ((2 * t + k) % 7)) % NR]
-        landed("RS%d%d" % (t, n), "rs%d%d" % (t, n), len(topo.engines(q, core)))
+        for c in cells("RS%d%d" % (t, k), lo, hi):
+            landed(c, sem, len(topo.engines(q, core)))
+
+    H = ("pS", T.pS[:, L:2 * L])
 
     def wrapped(out, z, src, n, start, fin):
         return [(out, T[z][:, 15 - j:143 - j], T[src][:, j:16 * n:16], start and j == 0, fin and j == 15) for j in range(16)]
-
-    def kin_gather(out, lst):
-        ts(b(out), by("K", ap(lst), W), 0.25 - KOFF, None, Op.add, rd=[lst])
-
-    H = ("pS", T.pS[:, L:2 * L])
 
     def turn(rows):
         parts = []
@@ -283,354 +305,335 @@ def rank_program(g, core, T, topo):
                 for e in range(2):
                     lo = L - L * e + x
                     parts.append((T.pS[32 * p:32 * p + 32, L + x:2 * L:16], T.SZ[:, lo:lo + 2 * L - x:16], rows(2 * p + e), e == 0, e == 1))
-        mms("pS", parts, ["SZ", "SZ0", "IDH"])
+        mms("pS", parts, ["SZ", "SZ.0", "SZ.2", "IDH"])
 
     def rot(j):
         return T.ROT[:, 8 * (5 * j % 16):8 * (5 * j % 16) + 128]
 
-    iota("PC", [[0, 2]], 0, 1)
-    iota("PM", [[0, 2]], 0, 13)
-    iota("JF", [[0, 16], [1, 16]], 0, 0)
+    ROT = ["ROT.0", "ROT.128"]
+
     iota("D", [[1, L]], 0, -1)
-    iota("EXI", [[16, 16]], 15, 0)
-    iota("CB", [[1, 8], [0, 16]], 0, 0)
-    iota("G8", [[1, 8]], 0, 0)
-    iota("LWB", [[16, 16]], W, 1)
-    iota("BF", [[1, 16], [0, 16]], 0, 0)
-    ts(b("PG"), b("PC", 0, 1), 4, None, Op.arith_shift_right)
-    ts(b("PM", 1, 2), b("PM", 1, 2), 15, None, Op.bitwise_and)
-    ts(b("PM", 0, 1), b("PC", 0, 1), 15, None, Op.bitwise_and)
-    cp(b("PGF"), b("PG"))
+    iota("JF", [[0, 16], [1, 16]], 0, 0)
+    for nm, lo, hi, x in (("C32", 0, 16, 1.0 + 3.25 / 16.0), ("MB", 0, 50, 0.0), ("C32", 16, 32, 0.7421875), ("N16", 0, 2, -16.0), ("NEG", 0, 16, -1.0),
+                          ("XZ", 0, 48, 0.0), ("C2", 0, 2, -float(MOD)), ("BK", 0, 8, 0.0)):
+        fill(b(nm, lo, hi), x)
+    ts(b("WB", 1, 2, "WB.1"), b("D", 0, 1), XD, -X0, Op.mult, Op.add)
+    act(b("XS"), b("D"), Fn.Silu, rd=["WB.1"], scale=-XD, bias=col("WB", 1))
+    ts(b("PC", 0, 1, "PC.0"), b("D", 0, 1), -1.0, None, Op.mult)
+    ts(b("PC", 1, 2, "PC.1"), b("D", 0, 1), -13.0, None, Op.mult)
+    ts(b("PM"), b("PC", 0, 2, "PC.0"), 15, None, Op.bitwise_and, rd=["PC.1"])
+    ts(b("PG"), b("PC", 0, 1, "PC.0"), 4, None, Op.arith_shift_right)
+    ts(b("ZC"), b("PM", 0, 1), -1.0, 15.0, Op.mult, Op.add)
     cp(b("PMF"), b("PM"))
-    ts(b("ZC"), b("PMF", 0, 1), -1.0, 15.0, Op.mult, Op.add)
-    ts(b("MK0"), b("JF"), col("PMF", 1), None, Op.is_equal, rd=["PMF"])
-    ln2 = math.log(2.0)
-    ts(b("WB", 0, 1, "WB.0"), b("PMF", 0, 1), -STEP * ln2, (TOP + 15 * STEP) * ln2, Op.mult, Op.add)
-    ts(b("WB", 1, 2, "WB.1"), b("PC", 0, 1), -STEP * ln2, TOP * ln2 + math.log(2.55), Op.mult, Op.add)
-    ts(b("RC"), b("PGF"), -15.0, None, Op.mult)
     ts(b("ZH"), b("D", 0, 144), col("ZC"), None, Op.is_equal, rd=["ZC"])
-    ts(b("RC"), b("PMF", 0, 1), 7.0, col("RC"), Op.mult, Op.add, rd=["RC"])
-    ts(b("IDH"), b("D", 0, 128), 0.0, None, Op.is_equal)
+    ts(b("MK0"), b("JF"), col("PMF", 1), None, Op.is_equal, rd=["PMF"])
+    ts(b("WB", 0, 1, "WB.0"), b("PMF", 0, 1), -XD, col("WB", 1), Op.mult, Op.add, rd=["WB.1"])
     tt(b("SM"), b("SN"), b("MK0"), Op.mult)
     mms("pM", wrapped(T.pM[:, 0:16], "ZH", "SM", 16, True, True), ["ZH", "SM"])
-    ts(b("BDH"), b("CB"), col("PGF"), None, Op.is_equal, rd=["PGF"])
-    for lo in (0, 128):
-        ts(b("ROT", lo, lo + 128), b("D", 0, 128), col("RC"), None, Op.is_equal, rd=["RC"])
+    tt(b("BF"), b("JF"), b("D"), Op.subtract)
+    ts(b("RTC"), b("PG"), -15.0, None, Op.mult)
+    ts(b("BDH"), b("BF", 0, 128), col("PMF"), None, Op.is_equal, rd=["PMF"])
+    ts(b("RTC"), b("PMF", 0, 1), 7.0, col("RTC"), Op.mult, Op.add, rd=["RTC"])
+    ts(b("IDH"), b("D", 0, 128), 0.0, None, Op.is_equal)
     cp(b("CL0"), ("pM", T.pM[:, 0:16]))
     send_list(0)
+    for lo in (0, 128):
+        ts(b("ROT", lo, lo + 128, "ROT.%d" % lo), b("D", 0, 128), col("RTC"), None, Op.is_equal, rd=["RTC"])
+    cp(b("PGF"), b("PG"))
 
-    def own_constants(t):
-        act(b("TB%d" % t), b("OB"), Fn.Identity, scale=float(8 + t))
-        if t < RO - 1:
-            act(b("DN%d" % t), b("IDB"), Fn.Identity, rd=["NS"], scale=col("ISN", 4 + t))
-            act(b("DI%d" % t), b("IDB"), Fn.Identity, rd=["IS"], scale=col("ISN", t))
+    def scaled(names):
+        for nm, src, f in names:
+            act(b(nm), b(src), Fn.Identity, scale=f)
 
-    iota("CK", [[0, 16], [-1, 16]], 15, 0)
-    for nm, x in (("MB", 0), ("N16", -16), ("NEG", -1), ("XZ", 0)):
-        iota(nm, [[0, SCRATCH[nm][1][1]]], x, 0)
-    act(b("WT"), b("EXI"), Fn.Exp, rd=["WB.0"], scale=-STEP * ln2, bias=col("WB"))
-    act(b("NTH"), b("D"), Fn.Exp, rd=["WB.1"], scale=-STEP * ln2, bias=col("WB", 1))
+    iota("LWB", [[16, 16]], W, 1)
+    iota("CSI", [[16, 4], [0, 2]], 16, 0)
+    for x in (0, 2):
+        ts(b("SZ", x * L, x * L + L, "SZ.%d" % x), b("MK0"), 0.0, None, Op.mult)
+    ts(b("ISN", 0, 4), b("JF", 0, 4), col("PMF"), None, Op.not_equal, rd=["PMF"])
+    ts(b("OBC"), b("PMF", 0, 1), -16.0, col("D"), Op.mult, Op.subtract, rd=["D"])
+    ts(b("ZGC"), b("PG"), -16.0, 16.0, Op.mult, Op.add)
+    act(b("WS"), ("D", T.D[:, 0::16]), Fn.Silu, rd=["WB.0"], scale=-XD, bias=col("WB"))
     act(b("SF"), b("SN"))
+    act(b("WT"), b("WS"), Fn.Square, scale=2.0 ** 60)
+    act(b("NTH"), b("XS"), Fn.Square, scale=2.0 ** 60 * math.sqrt(2.55))
+    scaled((("ZB", "ZH", -1.0), ("Z16", "ZH", 1.0 / 16.0), ("IDB", "IDH", 1.0)))
     mms("pK", [(T.pK[:, 0:L], T.BDH[:], T.SM[:], True, True)], ["BDH", "SM"])
-    mms("pS", [(T.pS[:, L + 16 * j:L + 16 * j + 16], rot(j), T.SF[:, j::16], True, True) for j in range(16)], ["ROT", "SF"])
+    mms("pS", [(T.pS[:, L + 16 * j:L + 16 * j + 16], rot(j), T.SF[:, j::16], True, True) for j in range(16)], ROT + ["SF"])
     act(b("CW"), ("pM", T.pM[:, 0:16]))
     act(b("CREP"), ("pK", T.pK[:, 0:L]))
+    scaled((("BDN", "BDH", -1.0), ("IDS", "IDH", 1.0 / 4096.0)))
     act(b("SZ", L, 2 * L), H)
-    act(b("K", 0, W // 2), b("KI", 0, W // 2, "KI.0"), Fn.Identity, bias=KOFF)
-    for lo in (0, 2 * L):
-        ts(b("SZ", lo, lo + L, "SZ0"), b("MK0"), 0.0, None, Op.mult)
     turn(lambda q: T.IDH[:, q::8])
-    ts(b("IDB"), b("IDH"), 1.0, None, Op.mult)
-    ts(b("BDN"), b("BDH"), -1.0, None, Op.mult)
-    ts(b("ISN", 0, 4, "IS"), b("JF", 0, 4), col("PMF"), None, Op.is_equal, rd=["PMF"])
-    ts(b("ISN", 4, 8, "NS"), b("JF", 0, 4), col("PMF"), None, Op.not_equal, rd=["PMF"])
-    ts(b("OB"), b("BF"), col("PMF"), None, Op.is_equal, rd=["PMF"])
-    act(b("CH", 2, 18), b("CW"))
-    own_constants(0)
+    scaled((("IDN", "IDH", -1.0), ("IDK", "IDH", BIG)))
 
     def more_constants():
-        ts(b("IDS"), b("IDH"), 1.0 / 4096.0, None, Op.mult)
+        ts(b("TB0"), b("BF"), col("OBC"), 8.0, Op.is_equal, Op.mult, rd=["OBC"])
+        ts(b("DN0"), b("IDH"), col("ISN"), None, Op.mult, rd=["ISN"])
+
+    def last_constants():
         ts(b("CH", 0, 2, "CH0"), b("PMF"), 0.0, None, Op.mult)
         ts(b("OFF0"), b("PMF"), col("PMF"), None, Op.min)
-        for nm, src, f in (("ZB", "ZH", 1.0 / 32.0), ("IDN", "IDH", -1.0), ("IDL", "IDH", -2.0 ** 21), ("IDP", "IDH", 4096.0)):
-            ts(b(nm), b(src), f, None, Op.mult)
-        ts(b("DG"), b("JF"), col("PMF"), None, Op.is_equal, rd=["PMF"])
-        ts(b("RST"), b("JF"), 1.0, None, Op.min)
-        ts(b("CST"), b("EXI", 0, 8), col("PMF"), -142.5, Op.add, Op.add, rd=["PMF"])
-        fill(b("C32", 0, 16, "C32.0"), 0.75)
-        fill(b("C32", 16, 32, "C32.1"), 11.75 / 16.0)
-        for nm, f in (("GB16", 16.0), ("GHN", -4096.0)):
-            ts(b(nm), b("G8"), col("PGF"), f, Op.is_equal, Op.mult, rd=["PGF"])
-        cp(b("EXP"), b("EXI"))
-        ts(b("BM"), b("OB"), -1e29, 1e29, Op.mult, Op.add)
+        ts(b("RST", 0, 128), b("JF", 0, 128), 1.0, None, Op.min)
+        ts(b("CST"), b("CSI"), col("PMF"), None, Op.add, rd=["PMF"])
+        ts(b("GB16"), b("JF", 0, 8), col("PGF"), 16.0, Op.is_equal, Op.mult, rd=["PGF"])
+        ts(b("PH"), b("PM", 0, 1), 8, None, Op.bitwise_and)
+        ts(b("PH2"), b("PM", 0, 1), 7, None, Op.bitwise_and)
+        ts(b("ZG"), b("D", 0, 48), col("ZGC"), -4096.0, Op.is_equal, Op.mult, rd=["ZGC"])
+        ts(b("PHF"), b("PH"), 16.0, col("D"), Op.mult, Op.subtract, rd=["D"])
+        ts(b("PHG"), b("PH2"), col("PGF"), None, Op.is_equal, rd=["PGF"])
+        ts(b("BM"), b("BF"), col("OBC"), -BIG, Op.is_equal, Op.mult, rd=["OBC"])
+        ts(b("EXP", 0, 8), ("D", T.D[:, 23:151:16]), col("PHF"), col("PHG"), Op.add, Op.mult, rd=["PHF", "PHG"])
 
-    def rec_piece(q, G, lst, lo, hi, t):
-        o, i = ("%s.%d" % (G, lo), T[G][:, 16 * lo:16 * hi]), by("R", T[lst][:, lo:hi], W)
+    def round_constants(t):
+        act(b("TB%d" % t), b("TB0"), Fn.Identity, scale=(8 + t) / 8.0)
+        if t < RO - 1:
+            act(b("DN%d" % t), b("IDH"), Fn.Identity, rd=["ISN"], scale=col("ISN", t))
+
+    EVEN = 1.5 * 2.0 ** 20
+    CW = b("CW")
+    NA = b("XZ", 16, 32)
+    F0, F1 = ("pF", T.pF[:, 0:16]), ("pF", T.pF[:, 16:32])
+    BUF = {"g0": ("GA0", "AK0"), "g1": ("GA1", "AK1"), "o": ("GO", "KL")}
+    ABANK = (("pA", 0), ("pF", L))
+    KEY = (("pK", T.pK[:, 0:128]), ("pA", T.pA[:, 0:128]))
+    PART = ((0, ZS), (ZS, L))
+    Z = (("pZ", T.pZ[:, 0:ZS]), ("pZ2", T.pZ2[:, 0:L - ZS]))
+
+    def kin_gather(q, out, lst, t):
+        src, x = ((["KI.0", "KI.1"], T.KI[:].indirect(ap(lst))), 0.25) if t == 0 else (by("K", ap(lst), W), 0.25 - KOFF)
         if q == "a":
-            act(o, i, Fn.Relu, rd=[lst], bias=1.0 / 128.0 - (5 + t))
+            act(b(out), src, Fn.Identity, rd=[lst], bias=x)
         else:
-            ts(o, i, 1.0 / 128.0 - (5 + t), 0.0, Op.add, Op.max, rd=[lst])
+            ts(b(out), src, x, None, Op.add, rd=[lst])
 
-    def rec_sum(bank, c0, G, lo, hi, whole, rd=()):
+    def rec_piece(q, kind, lo, hi, t):
+        G, lst = BUF[kind]
+        o, i = (cells(G, lo, hi), T[G][:, 16 * lo:16 * hi]), by("R", T[lst][:, lo:hi], W)
+        if q == "a":
+            act(o, i, Fn.Relu, rd=[lst], bias=EPS - (5 + t))
+        else:
+            ts(o, i, EPS - (5 + t), 0.0, Op.add, Op.max, rd=[lst])
+
+    def rec_sum(kind, lo, hi):
+        G = BUF[kind][0]
+        whole = kind != "o"
+        bank, c0 = (ABANK[int(kind[1])][0], ABANK[int(kind[1])][1] + lo) if whole else (("pZ2", lo - ZS) if lo >= ZS else ("pZ", lo))
         parts = [(T[bank][:, c0:c0 + hi - lo], T.IDB[:], T[G][:, 16 * lo + m:16 * hi:16], whole and m == 0, whole and m == 15) for m in range(16)]
-        mms(bank, parts, ["%s.%d" % (G, lo), "IDB"] + list(rd))
+        mms(bank, parts, cells(G, lo, hi) + ["IDB"])
 
-    def own_sum(c):
-        rec_sum("pZ2" if CH * c >= 128 else "pZ", CH * c % 128, "GO", CH * c, CH * c + CH, False)
-
-    def add_sums(src, key, lo, hi, first, fin):
-        z = "pZ2" if lo >= 128 else "pZ"
-        mms(z, [(T[z][:, lo % 128:lo % 128 + hi - lo], T.IDB[:], ap(src, lo, hi), first, fin)], ["IDB", key])
-
-    def scatter(tab, src):
-        op("v", [src, "SL"], [tab], lambda: V.tensor_copy(T[tab][:].indirect(T.SL[:]), T[src][:]))
-
-    def compare_lanes(lo, hi):
-        for bb in range(lo, hi):
+    def compare_lanes():
+        for bb in range(16):
             n, o = L - 16 * bb, sum(L - 16 * x for x in range(bb))
             ts(("EQ.%d" % bb, T.EQ[:, o:o + n]), ("CREP", T.CREP[:, 16 * bb:L]), col("CW", bb), col("WT", bb), Op.is_equal, Op.mult, rd=["CW", "WT"])
 
-    def count_lanes(lo, hi):
-        if lo == 0:
-            mms("pD", [(T.pD[:, 0:L], T.IDB[:], T.NTH[:], True, False)], ["IDB", "NTH"])
-        for bb in range(lo, hi):
+    def count_lanes():
+        mms("pD", [(T.pD[:, 0:L], T.IDB[:], T.NTH[:], True, False)], ["IDB", "NTH"])
+        for bb in range(16):
             n, o = L - 16 * bb, sum(L - 16 * x for x in range(bb))
             mms("pD", [(T.pD[:, 16 * bb:L], T.BDN[:], T.EQ[:, o:o + n], False, bb == 15)], ["EQ.%d" % bb, "BDN"])
 
-    def best_half(h):
-        sl = slice(2048 * h, 2048 * h + 2048)
-        tt(("Y.%d" % h, T.Y[:, sl]), by("X", T.KL[:, 128 * h:128 * h + 128]), ("XR.%d" % h, T.XR[:, sl]), Op.max, rd=["KL"])
+    def best_piece(lo, hi):
+        sl = slice(16 * lo, 16 * hi)
+        tt((cells("Y", lo, hi), T.Y[:, sl]), by("X", T.KL[:, lo:hi]), (cells("XR", lo, hi), T.XR[:, sl]), Op.max, rd=["KL"])
 
-    def best_sum(h):
-        parts = []
+    def best_sum(lo, hi):
+        bank, p0 = KEY[lo // 128][0], lo % 128
+        parts = [(T[bank][:, 0:128], T.IDN[:], T.JF[:, 0:128], True, False)] if p0 == 0 else []
         for m in range(16):
-            parts.append((T.pK[:, 128 * h + m:128 * h + 128:16], T.Y[:, 2048 * h + m:2048 * h + 2048:16], T.GB16[:], False, h == 1 and m == 15))
-        mms("pK", parts, ["Y.%d" % h, "GB16"])
+            parts.append((T[bank][p0:p0 + hi - lo, m:128:16], T.Y[:, 16 * lo + m:16 * hi:16], T.GB16[:], False, m == 15))
+        mms(bank, parts, cells("Y", lo, hi) + ["GB16", "IDN", "JF"])
 
-    MAG = 1.5 * 2.0 ** 31
-    EVEN = 1.5 * 2.0 ** 20
-    CW = b("CW")
-    NOWN = L // CH
+    def best_steps(h):
+        lo, hi = 128 * h, 128 * h + 128
+        rm, ni, kx = (b(n, lo, hi, "%s.%d" % (n, h)) for n in ("RM", "NI", "KX"))
+        return {"rm%d" % h: lambda: scan(rm, b("RST", 0, 128), KEY[h], Op.mult),
+                "ni%d" % h: lambda: tt(ni, rm, KEY[h], Op.subtract),
+                "kx%d" % h: lambda: tt(kx, ("pS", T.pS[:, lo:hi]), ni, Op.subtract),
+                "bk%d" % h: lambda: scan(b("BK", 8 + lo, 8 + hi, "BK.%d" % h), ni, kx, Op.min)}
 
-    for t in range(RO):
+    def kin_numbers():
+        mms("pS", [(T.pS[:, 128 * h:128 * h + 128], T.KCF[:, 128 * h:128 * h + 128], T.IDS[:], h == 0, h == 1) for h in range(2)], ["KCF", "IDS"])
+
+    def double(q, s, lo, hi):
+        st, keys = 8 >> s, cells("XR", lo, hi)
+        o, i = T.XR[:, 16 * lo + st:16 * hi:2 * st], T.XR[:, 16 * lo:16 * hi:2 * st]
+        if q == "q":
+            op("q", [], keys, lambda: g.affine_select(o, i, [[0, (hi - lo) << s]], Op.is_ge, 0.0, 0, 0))
+        else:
+            copy(q)((keys, o), (keys, i))
+
+    def one_round(t):
         last = t == RO - 1
         cl = "CL%d" % t
         off = ap("OFF%d" % t, 0, 1)
-
-        def wealth(na):
-            op("a", ["X", cl], ["XR.0", "XR.1"], lambda: A.activation(T.XR[:, 0::16], T.X[:].indirect(ap(cl)), Fn.Copy))
-            for st in (8, 4, 2, 1)[:na]:
-                op("a", [], ["XR.0", "XR.1"], lambda: A.activation(T.XR[:, st::2 * st], T.XR[:, 0::2 * st], Fn.Copy))
-            for h in range(2):
-                for st in (8, 4, 2, 1)[na:4 - (XV0[h] if t == 0 else 0)]:
-                    lo, hi = 8 * L * h, 8 * L * h + 8 * L
-                    op("q", [], ["XR.%d" % h], lambda: g.affine_select(T.XR[:, lo + st:hi:2 * st], T.XR[:, lo:hi:2 * st], [[0, 4 * L // st]], Op.is_ge, 0.0, 0, 0))
-
-        def kin_numbers():
-            mms("pS", [(T.pS[:, 0:L], T.IDH[:], T.SZ[:, 0:L], True, False)] +
-                [(T.pS[:, 128 * h:128 * h + 128], T.KCF[:, 128 * h:128 * h + 128], T.IDS[:], False, False) for h in range(2)], ["IDH", "SZ0", "KCF", "IDS"])
+        words = SEQ[t].split()
+        kept = ("pM", T.pM[:, 128:128 + L]) if last else H
 
         def kin_moves():
-            if t == RO - 2:
-                mms("pM", [(T.pM[:, 384:512], rot(0), T.IDH[:], True, True)], ["ROT", "IDH"])
-            if not last:
-                mms("pM", [(T.pM[:, 128:128 + L], ap("DN%d" % t), T.KCF[:], True, False)] +
-                    [(T.pM[:, 128 + e:128 + L:2], ap("DI%d" % t), T.CREP[:, 1 - e::2], False, e == 1) for e in range(2)],
-                    ["DN%d" % t, "DI%d" % t, "KCF", "CREP"])
-
-        first = OWN_FIRST if t else OWN_FIRST0
-        cmp1 = CMP1 if t else 16
-        if t:
-            act(CW, by("SP", off), rd=["OFF%d" % t])
-            if CREP_FIRST:
-                act(b("CREP"), by("IDX", ap(cl)), rd=[cl])
-            wealth(XA)
-            if not CREP_FIRST:
-                act(b("CREP"), by("IDX", ap(cl)), rd=[cl])
-            if last:
-                op("v", ["NEG", "OFF%d" % t], ["SP"], lambda: V.tensor_copy(T.SP[:].indirect(off), T.NEG[:]))
-                scatter("R", "NVR")
-                act(b("SZ", L, 2 * L), b("SP"))
-                turn(lambda q: T.IDH[:, 16 * q:16 * q + 16])
-            act(b("CH", 2, 18), CW)
-            cp(b("KCF"), b("KL"))
-            compare_lanes(0, cmp1)
-        else:
-            act(b("K", W // 2, W), b("KI", W // 2, W, "KI.1"), Fn.Identity, bias=KOFF)
-            compare_lanes(0, cmp1)
-            more_constants()
-            kin_gather("KL", "CL0")
-        act(b("RCE"), by("R", ap(cl), W), Fn.Relu, rd=[cl], bias=1.0 / 128.0 - (5 + t))
-        for c in range(first):
-            rec_piece("a", "GO", "KL", CH * c, CH * c + CH, t)
-        for lo in (0, 128):
-            add_sums("RCE", "RCE", lo, lo + 128, True, False)
-        if 0 < t < RO - 1:
-            kin_moves()
+            parts = [(T.pM[:, 128:128 + L], ap("DN%d" % t), T.KCF[:], True, False)]
+            parts += [(T.pM[:, 128 + e:128 + L:2], T.Z16[:, 15 - t:143 - t], T.CREP[:, 1 - e::2], False, e == 1) for e in range(2)]
+            mms("pM", parts, ["DN%d" % t, "Z16", "KCF", "CREP"])
             kin_numbers()
-        count_lanes(0, cmp1)
-        for c in range(first):
-            own_sum(c)
-        for k in range(2):
-            kin_gather("AK%d" % k, "RQ%d%d" % (t, k))
-        if t == 0:
-            cp(b("KCF"), b("KL"))
-            cp(b("SP"), H)
-            kin_moves()
-            kin_numbers()
-        compare_lanes(cmp1, 16)
-        count_lanes(cmp1, 16)
-        x0, x1 = L - VX, L - VX + CH
-        vp = [(x0, x1), (x1, (x1 + L) // 4 * 2), ((x1 + L) // 4 * 2, L)]
-        rec_piece("a", "GA0", "AK0", 0, x0, t)
-        if t == 0:
-            wealth(XA0)
-        for lo, hi in vp:
-            rec_piece("v", "GA0", "AK0", lo, hi, t)
-        if t == 0:
-            for c in range(first, first + OWN_V0):
-                rec_piece("v", "GO", "KL", CH * c, CH * c + CH, t)
-        for c in range(NOWN):
-            rec_piece("a", "GA1", "AK1", CH * c, CH * c + CH, t)
-            if c == NOWN - 1:
-                send_sums(t, 1, 0, L - CH, 1)
-                send_sums(t, 0, 0, L, 0)
-            if c == 0:
-                rec_sum("pA", 0, "GA0", 0, x1, True, ["GA0.%d" % x0])
-            if c == 1:
-                rec_sum("pA", vp[1][0], "GA0", vp[1][0], vp[1][1], True)
-            rec_sum("pK", L + CH * c, "GA1", CH * c, CH * c + CH, True)
-            if c == 2:
-                rec_sum("pA", vp[2][0], "GA0", vp[2][0], L, True)
-        act(b("NT"), ("pD", T.pD[:, 0:L]), Fn.Sign, scale=-1.0)
-        send_sums(t, 1, L - CH, L, 2)
-        if last:
-            act(b("TR"), H)
-        mms("pD", wrapped(T.pD[:, L + 16:L + 32], "ZB", "NT", 16, True, True), ["ZB", "NT"])
-        if t == 0:
-            iota("IDX", [[1, W]], 0, 0)
-            for c in range(first, first + OWN_V0):
-                own_sum(c)
-            first += OWN_V0
-        if last:
-            mms("pS", [(T.pS[:, L + j:2 * L:16], rot(-j), T.TR[:, 16 * j:16 * j + 16], True, True) for j in range(16)], ["ROT", "TR"])
-            kin_moves()
-        mms("pK", [(T.pK[:, 0:L], T.IDB[:], T.CK[:], True, False)], ["IDB", "CK"])
-        for h in range(2):
-            for st in (8, 4, 2, 1)[4 - (XV0[h] if t == 0 else 0):]:
-                lo, hi = 8 * L * h, 8 * L * h + 8 * L
-                cp(("XR.%d" % h, T.XR[:, lo + st:hi:2 * st]), ("XR.%d" % h, T.XR[:, lo:hi:2 * st]))
-            best_half(h)
-        best_sum(0)
-        for c in range(first, NOWN):
-            rec_piece("a", "GO", "KL", CH * c, CH * c + CH, t)
-            if c == first:
-                act(b("DW"), ("pD", T.pD[:, L + 16:L + 32]), Fn.Identity, bias=0.5)
-                mms("pF", [(T.pF[:, 0:32], T.IDB[:], T.C32[:], True, False), (T.pF[:, 0:16], T.IDL[:], T.DW[:], False, False),
-                           (T.pF[:, 16:32], T.IDB[:], T.DW[:], False, False)], ["IDB", "IDL", "C32.0", "C32.1", "DW"])
-                if last:
-                    act(b("SF"), H)
-                    mms("pS", [(H[1], T.PERM[:], T.SF[:], True, True)], ["PERM", "SF"])
-            if c == B1:
-                best_sum(1)
-                if last:
-                    ts(b("HI"), H, 0.0, 4096.0, Op.is_lt, Op.mult)
-                    kin_numbers()
-            if c == NOWN - 1 and LOW_EARLY:
-                add_sums("RS%d1" % t, "RS%d1" % t, 0, 128, False, False)
-                add_sums("RS%d0" % t, "RS%d0" % t, 0, 128, False, True)
-            own_sum(c)
-        if not LOW_EARLY:
-            add_sums("RS%d1" % t, "RS%d1" % t, 0, 128, False, False)
-            add_sums("RS%d0" % t, "RS%d0" % t, 0, 128, False, True)
-        add_sums("RS%d0" % t, "RS%d0" % t, 128, L, False, False)
-        add_sums("RS%d1" % t, "RS%d1" % t, 128, L - CH, False, False)
-        add_sums("RS%d1" % t, "RS%d2" % t, L - CH, L, False, True)
-        for h, z in ((0, "pZ"), (1, "pZ2")):
-            act(b("UV", 128 * h, 128 * h + 128, "U.%d" % h), (z, T[z][:, 0:128]), Fn.Sign, bias=-0.7)
-        if not last:
-            act(b("KV"), ("pM", T.pM[:, 128:128 + L]), Fn.Identity, bias=KOFF)
-            own_constants(t + 1)
-        if t == RO - 2:
-            act(b("PERM"), ("pM", T.pM[:, 384:512]))
-        F0 = ("pF", T.pF[:, 0:16])
-        NA = b("XZ", 16, 32)
 
-        def less_key():
-            tt(b("NI"), b("RM"), ("pK", T.pK[:, 0:L]), Op.subtract)
-            mms("pS", [(T.pS[:, 0:L], T.IDN[:], T.NI[:], False, True)], ["IDN", "NI"])
+        def new_records(u):
+            if "nvr" in SEQ[u].split():
+                op("v", ["NV", "SL"], ["R"], lambda: V.tensor_copy(T.R[:].indirect(T.SL[:]), T.NV[:]))
+            else:
+                op("v", ["NV", "TB%d" % u, "SL"], ["R"], lambda: V.tensor_tensor(T.R[:].indirect(T.SL[:]), T.NV[:], ap("TB%d" % u), Op.add))
 
-        def less_best():
-            tt(b("LH"), by("BK", T.EXP[:]), b("DG"), Op.mult, rd=["EXP"])
-            mms("pM", [(T.pM[:, 16:48], T.IDH[:], T.SZ[:, 0:32], True, False), (T.pM[:, 16:32], T.IDH[:], T.CH[:, 2:18], False, False),
-                       (T.pM[:, 32:48], T.IDH[:], T.CH[:, 1:17], False, False)], ["IDH", "SZ0", "CH", "CH0"])
-            mms("pM", [(T.pM[:, lo + 8 * h:lo + 8 * h + 8], T.LH[:, 128 * h:128 * h + 128], T.GHN[:], False, lo == 32 and h == 1) for lo in (16, 32) for h in range(2)],
-                ["LH", "GHN"])
+        def evacuate(q, k, lo, hi):
+            bank, c0 = ABANK[k]
+            copy(q)((cells("AS%d%d" % (t, k), lo, hi), ap("AS%d%d" % (t, k), lo, hi)), (bank, T[bank][:, c0 + lo:c0 + hi]))
 
-        def bars():
-            for h, z in ((0, "pZ"), (1, "pZ2")):
-                tt(b("UV", L + 128 * h, L + 128 * h + 128, "V.%d" % h), (z, T[z][:, 0:128]), b("BM", 128 * h, 128 * h + 128), Op.is_gt)
-            mms("pF", wrapped(T.pF[:, 0:32], "ZB", "UV", 32, False, True), ["ZB", "U.0", "U.1", "V.0", "V.1"])
+        def addend(w, src, h):
+            lo, hi = PART[h]
+            fin = w == [x for x in words if x in ("an0%d" % h, "an1%d" % h)][-1]
+            mms(Z[h][0], [(Z[h][1], T.IDB[:], ap(src, lo, hi), w[0] == "r", fin)], ["IDB"] + cells(src, lo, hi))
 
-        def not_installed():
-            tt(NA, b("TH", 0, 16), b("TH", 16, 32), Op.max)
-            mms("pA", [(T.pA[:, 0:16], T.IDH[:], T.CH[:, 2:18], True, False), (T.pA[:, 0:16], T.IDP[:], NA[1], False, True)], ["IDH", "CH", "IDP", "XZ"])
+        def part_steps(h):
+            lo, hi = PART[h]
+            u = b("UV", lo, hi, "U.%d" % h)
+            return {"rce%d" % h: lambda: act((cells("RCE", lo, hi), ap("RCE", lo, hi)), by("R", ap(cl, lo // 16, hi // 16), W), Fn.Relu, rd=[cl], bias=EPS - (5 + t)),
+                    "rcm%d" % h: lambda: addend("rcm", "RCE", h),
+                    "an0%d" % h: lambda: addend("an0%d" % h, "RS%d0" % t, h),
+                    "an1%d" % h: lambda: addend("an1%d" % h, "RS%d1" % t, h),
+                    "u%d" % h: lambda: act(u, Z[h], Fn.Relu, scale=-1.0 / 16.0, bias=(1.0 - BIG) / 16.0),
+                    "w%d" % h: lambda: ts(u, Z[h], 0.7 - BIG, 1.0 / 16.0, Op.is_lt, Op.mult),
+                    "v%d" % h: lambda: tt(b("UV", L + lo, L + hi, "V.%d" % h), Z[h], b("BM", lo, hi), Op.is_gt)}
+
+        def citizens():
+            mms("pM", [(T.pM[:, 16:32], T.IDH[:], T.CH[:, 2:18], True, False)], ["IDH", "CH"])
             if not last:
-                mms("pD", [(T.pD[:, L:L + 2], T.IDB[:], T.CST[:, t + 1:t + 3], True, False)] +
-                    [(T.pD[32 * p:32 * p + 32, L:L + 2], T.XZ[:, 16 - 16 * e:48 - 16 * e], T.N16[:], False, e == 1) for p in range(4) for e in range(2)],
-                    ["IDB", "CST", "XZ", "N16"])
+                mms("pD", [(T.pD[:, L:L + 2], T.IDB[:], T.CST[:, 2 * t:2 * t + 2], True, False), (T.pD[:, L:L + 2], T.IDB[:], T.C2[:], False, False)],
+                    ["IDB", "CST", "C2"])
 
-        def targets():
-            cp(b("SL"), b("SLF"))
-            if last:
-                scatter("R", "NVR")
-                deps("a", ["R"], [])
-                A.dma_start(T.yr[:], T.R[:, 0:W]).then_inc(T.sem.stR, 16)
-            elif KOFF:
-                op("a", ["KV", "SL"], ["K"], lambda: A.activation(T.K[:].indirect(T.SL[:]), T.KV[:], Fn.Silu))
+        def store_records():
+            deps("a", ["R"], [])
+            A.dma_start(T.yr[:], T.R[:, 0:W]).then_inc(T.sem.stR, 16)
 
-        step = {
-            "nvr": lambda: tt(b("NVR"), by("R", ap(cl), W), b("TB%d" % t), Op.max, rd=[cl]),
-            "rm": lambda: scan(b("RM"), b("RST"), ("pK", T.pK[:, 0:L]), Op.mult),
-            "ni": less_key,
-            "bk": lambda: scan(b("BK"), b("NI"), ("pS", T.pS[:, 0:L]), Op.min),
-            "lh": less_best,
-            "vt": bars,
-            "th": lambda: ts(b("TH"), ("pF", T.pF[:, 0:32]), 0.75, None, Op.is_ge),
-            "rnd": lambda: ts(b("RND"), F0, EVEN, -EVEN, Op.add, Op.add),
-            "na": not_installed,
-            "odd": lambda: tt(b("ODD"), F0, b("RND"), Op.not_equal),
-            "torn": lambda: tt(b("TORN"), F0, NA, Op.is_ge),
-            "slf": lambda: tt(b("SLF"), ("pA", T.pA[:, 0:16]), b("LWB"), Op.min),
-            "cand": lambda: tt(b("CAND"), b("ODD"), b("TORN"), Op.is_gt),
-            "sl": targets,
-            "moved": lambda: tt(b("MB", 17, 32, "MB.1"), b("CAND", 0, 15), b("TORN", 1, 16), Op.mult, rd=["MB"]),
-            "rr": lambda: last or ts(b("RR"), ("pD", T.pD[:, L:L + 2]), MAG, -MAG, Op.add, Op.add),
-            "tm": lambda: tt(b("MB", 0, 16, "MB.0"), b("TORN"), b("MB", 17, 33, "MB.1"), Op.add),
-            "off": lambda: last or ts(b("OFF%d" % (t + 1)), ("pD", T.pD[:, L:L + 2]), col("RR"), 127.5, Op.subtract, Op.add, rd=["RR"]),
-        }
-        for name in (ORDER_LAST if last else ORDER).split():
-            step[name]()
-        tt(b("PP"), b("MB", 0, 32, "MB.0"), ("pM", T.pM[:, 16:48]), Op.mult, rd=["MB.1"])
-        tt(b("QQ"), b("PP", 16, 32), b("PP", 0, 16), Op.subtract)
-        if last:
-            tt(b("NEW"), b("QQ"), CW, Op.add)
+        def finish():
+            tt(b("NEW"), b("QQ"), b("PP"), Op.subtract)
             cp(b("NU"), b("NEW"))
             tt(b("GN"), by("IDX", T.NU[:]), b("HI"), Op.min, rd=["NU"])
             tt(b("XS"), b("GN"), H, Op.max)
             deps("s", ["XS"], [])
             g.sync.dma_start(T.ys[:], T.XS[:]).then_inc(T.sem.stS, 16)
-            break
-        op("v", ["QQ", "CW", "OFF%d" % t], ["SP"], lambda: V.tensor_tensor(T.SP[:].indirect(off), T.QQ[:], CW[1], Op.add))
-        cp(b("CL%d" % (t + 1)), by("SP", ap("OFF%d" % (t + 1), 0, 1)), rd=["OFF%d" % (t + 1)])
-        send_list(t + 1)
-        if not KOFF:
-            scatter("K", "KV")
-        kin_gather("KL", "CL%d" % (t + 1))
-        if t < RO - 2:
-            scatter("R", "NVR")
 
-    g.wait_ge(T.sem.loc, LOC["n"])
+        def next_list():
+            cp(b("CL%d" % (t + 1)), by("SP", ap("OFF%d" % (t + 1), 0, 1)), rd=["OFF%d" % (t + 1)])
+            send_list(t + 1)
+
+        def permutation():
+            if t == RO - 2:
+                mms("pZ2", [(T.pZ2[:, L:L + 128], rot(0), T.IDH[:], True, True)], ROT + ["IDH"])
+                act(b("PERM"), ("pZ2", T.pZ2[:, L:L + 128]))
+
+        best_list = ["EXP", "BK.0", "BK.1"]
+        either = {
+            "kl": lambda q: kin_gather(q, "KL", cl, t),
+            "ak0": lambda q: kin_gather(q, "AK0", "RQ%d0" % t, t),
+            "ak1": lambda q: kin_gather(q, "AK1", "RQ%d1" % t, t),
+            "kcf": lambda q: copy(q)(b("KCF"), b("KL")),
+            "crep": lambda q: copy(q)(b("CREP"), by("IDX", ap(cl)), rd=[cl]),
+            "xr": lambda q: copy(q)((cells("XR", 0, L), T.XR[:, 0::16]), by("X", ap(cl)), rd=[cl]),
+        }
+        step = {
+            "mc": more_constants,
+            "lc": last_constants,
+            "idx": lambda: iota("IDX", [[1, W]], 0, 0),
+            "spc": lambda: cp(b("SP"), H),
+            "k0": lambda: act(b("K", 0, W // 2), b("KI", 0, W // 2, "KI.0"), Fn.Identity, bias=KOFF),
+            "k1": lambda: act(b("K", W // 2, W), b("KI", W // 2, W, "KI.1"), Fn.Identity, bias=KOFF),
+            "rcs": lambda: round_constants(t + 1),
+            "perm": permutation,
+            "sr": lambda: new_records(t - 1),
+            "cw": lambda: act(CW, by("SP", off), rd=["OFF%d" % t]),
+            "ch": lambda: act(b("CH", 2, 18), CW),
+            "+kcf": kin_moves,
+            "cmp": compare_lanes,
+            "+cmp": count_lanes,
+            "nt": lambda: act(b("NT"), ("pD", T.pD[:, 0:L]), Fn.Sign, scale=-1.0),
+            "+nt": lambda: [mms(Z[h][0], [(Z[h][1], T.IDK[:], ap("NT", *PART[h]), False, False)], ["IDK", "NT"]) for h in range(2)],
+            "bm": lambda: mms("pF", [(T.pF[:, 0:32], T.IDB[:], T.C32[:], True, False)] + wrapped(T.pF[:, 0:32], "ZB", "UV", 32, False, True),
+                              ["IDB", "C32", "ZB", "U.0", "U.1", "V.0", "V.1"]),
+            "neg": lambda: op("v", ["NEG", "OFF%d" % t], ["SP"], lambda: V.tensor_copy(T.SP[:].indirect(off), T.NEG[:])),
+            "sz": lambda: act(b("SZ", L, 2 * L), b("SP")),
+            "+sz": lambda: turn(lambda q: T.IDH[:, 16 * q:16 * q + 16]),
+            "tr": lambda: act(b("TR"), H),
+            "+tr": lambda: mms("pS", [(T.pS[:, L + j:2 * L:16], rot(-j), T.TR[:, 16 * j:16 * j + 16], True, True) for j in range(16)], ROT + ["TR"]),
+            "sf": lambda: act(b("SF"), H),
+            "+sf": lambda: mms("pS", [(H[1], T.PERM[:], T.SF[:], True, True)], ["PERM", "SF"]),
+            "hi": lambda: act(b("HI"), H, Fn.Relu, scale=-4096.0),
+            "+hi": kin_numbers,
+            "kv": lambda: act(b("KV"), ("pM", T.pM[:, 128:128 + L]), Fn.Identity, bias=KOFF),
+            "rc": lambda: act(b("RC"), by("R", ap(cl), W), rd=[cl]),
+            "nvm": lambda: mms(kept[0], [(kept[1], T.IDB[:], T.RC[:], True, False), (kept[1], T.IDN[:], ap("TB%d" % t), False, True)], ["IDB", "IDN", "RC", "TB%d" % t]),
+            "nv": lambda: act(b("NV"), kept, Fn.Relu),
+            "nvr": lambda: tt(b("NV"), by("R", ap(cl), W), b("TB%d" % t), Op.max, rd=[cl]),
+            "cm": citizens,
+            "lh": lambda: act(b("LH"), by("BK", T.EXP[:, 0:8]), rd=best_list),
+            "lhv": lambda: cp(b("LH"), by("BK", T.EXP[:, 0:8]), rd=best_list),
+            "lhm": lambda: mms("pM", [(T.pM[32 * (x // 2):32 * (x // 2) + 32, 16:32], T.ZG[:, 16 - 16 * (x % 2):48 - 16 * (x % 2)], T.LH[:, 16 * x:16 * x + 16],
+                                       False, x % 2 == 1) for x in range(8)], ["LH", "ZG"]),
+            "rnd": lambda: ts(b("RND"), F0, EVEN, -EVEN, Op.add, Op.add),
+            "na": lambda: tt(NA, b("RND"), F1, Op.is_ge),
+            "odd": lambda: tt(b("ODD"), F0, b("RND"), Op.is_gt),
+            "fs": lambda: ts(b("FS"), F1, 1.0 / 32.0, 0.012, Op.mult, Op.add),
+            "rn2": lambda: tt(b("RN2"), b("RND"), b("FS"), Op.add),
+            "torn": lambda: tt(b("TORN"), b("RN2"), NA, Op.is_ge),
+            "wn": lambda: tt(b("MB", 34, 49, "MB.2"), b("ODD", 0, 15), b("TORN", 1, 16), Op.mult, rd=["MB"]),
+            "mv": lambda: tt(b("MB", 17, 33, "MB.1"), b("MB", 34, 50, "MB.2"), b("TORN"), Op.is_gt),
+            "tw": lambda: tt(b("MB", 0, 16, "MB.0"), b("MB", 34, 50, "MB.2"), b("TORN"), Op.max),
+            "nl": lambda: tt(b("NL"), NA, b("LWB"), Op.mult),
+            "slm": lambda: tt(b("SLF"), b("NL"), CW, Op.max),
+            "sl": lambda: act(b("SL"), b("SLF")),
+            "slv": lambda: cp(b("SL"), b("SLF")),
+            "ks": lambda: op("a", ["KV", "SL"], ["K"], lambda: A.activation(T.K[:].indirect(T.SL[:]), T.KV[:], Fn.Silu)),
+            "srl": lambda: new_records(t),
+            "st": store_records,
+            "naa": lambda: mms("pD", [(T.pD[32 * p:32 * p + 32, L:L + 2], T.XZ[:, 16 - 16 * e:48 - 16 * e], T.N16[:], False, e == 1) for p in range(4) for e in range(2)],
+                               ["XZ", "N16"]),
+            "rrv": lambda: ts(b("RR", 0, 1), ("pD", T.pD[:, L:L + 1]), -1.0, 127.5, Op.mult, Op.add),
+            "offv": lambda: ts(b("OFF%d" % (t + 1), 0, 1), ("pD", T.pD[:, L + 1:L + 2]), col("RR"), None, Op.add, rd=["RR"]),
+            "off": lambda: [act(b("RR", 0, 1), ("pD", T.pD[:, L:L + 1]), Fn.Identity, scale=-1.0, bias=127.5),
+                            act(b("OFF%d" % (t + 1), 0, 1), ("pD", T.pD[:, L + 1:L + 2]), Fn.Identity, rd=["RR"], bias=col("RR"))],
+            "dc": lambda: tt(b("DC"), b("CH", 1, 17), b("CH", 2, 18), Op.subtract, rd=["CH0"]),
+            "pm": lambda: tt(b("PM1"), b("MB", 16, 32, "MB.1"), b("DC"), Op.mult),
+            "tb": lambda: tt(b("TB"), b("MB", 0, 16, "MB.0"), b("MB", 16, 32, "MB.1"), Op.subtract),
+            "qq": lambda: tt(b("QQ"), b("PM1"), CW, Op.add),
+            "pp": lambda: tt(b("PP"), b("TB"), ("pM", T.pM[:, 16:32]), Op.mult),
+            "sp": lambda: op("v", ["QQ", "PP", "OFF%d" % t], ["SP"], lambda: V.tensor_tensor(T.SP[:].indirect(off), T.QQ[:], T.PP[:], Op.subtract)),
+            "cl": next_list,
+            "fin": finish,
+        }
+        for h in range(2):
+            step.update(part_steps(h))
+            step.update(best_steps(h))
+
+        for word in words:
+            q = {"V": "v", "A": "a", "G": "q", "+": "p"}.get(word[0])
+            kind, _x, span = (word[1:] if q else word).partition(":")
+            if not span:
+                either[kind](q) if q in ("v", "a") else step[word]()
+                continue
+            lo, hi = (int(x) for x in span.split("-"))
+            if q == "p":
+                best_sum(lo, hi) if kind == "y" else rec_sum(kind, lo, hi)
+            elif kind == "y":
+                best_piece(lo, hi)
+            elif kind in BUF:
+                rec_piece(q, kind, lo, hi, t)
+            elif kind[0] == "e":
+                evacuate(q, int(kind[1]), lo, hi)
+            elif kind[0] == "s":
+                send_sums(t, int(kind[1]), lo, hi)
+            else:
+                double(q, int(kind[1]), lo, hi)
+
+    for t in range(RO):
+        one_round(t)
+
+    g.wait_ge(T.sem.loc, left[0])
     A.wait_ge(T.sem.stR, 16)
     g.sync.wait_ge(T.sem.stS, 16)
     for q in ("v", "a", "p", "q"):

@@ -1,4 +1,3 @@
-import math
 from concourse.bass import DstId, RemoteDMATransfer
 from concourse.mybir import dt, AluOpType as Op, ActivationFunctionType as Fn
 
@@ -6,32 +5,52 @@ NR, RO, W, L = 8, 4, 2048, 256
 WX = W + 3 * L
 KOFF = 64.0
 EPS = 1.0 / 2048.0
-X0, XD = 10.0, 0.3
 BIG = 1024.0
 CELL = 8
 MOD = 129 * 256
 ZS = 192
 
 S0 = """
-idx Akl ch cmp +cmp rce0 rce1 rcm1 rcm0 Ao:0-64 mc Axr +o:0-64 Vak0 Ax0:0-256 Gx1:0-256 Gx2:0-256 Ao:64-120 Gx3:0-128 lc spc Vak1 Vkcf +o:64-120
-Ag0:0-64 +kcf Vg0:128-192 +g0:0-64 +g0:128-192 Ag0:64-128 Vg0:192-256 +g0:64-128 +g0:192-256 Ag1:0-64 Vg1:128-192 +g1:0-64 +g1:128-192 Ag1:64-128
-Ae0:0-256 s0:0-256 Vg1:192-256 +g1:64-128 nt +nt +g1:192-256 Ao:120-192 Ae1:0-256 s1:0-256 Vx3:128-256 Vy:0-128 +o:120-192 +y:0-128 Vy:128-256
-an00 an01 Ao:192-256 +o:192-256 k0 an10 u0 kv rc k1 an11 +y:128-256 rm0 ni0 v0 w1 cm v1 kx0 bm nvm rm1 bk0 dc ni1 fs rnd kx1 na naa rn2 bk1
-torn nl lh lhm odd slm wn nv sl ks rrv mv tw pm tb qq pp offv sp cl perm rcs
+idx aT cmp Akl:0-256 cC aC Arce +rce +cmp Ao:0-64 Axr Ax0:0-256 Gx1:0-256 Gx2:0-256 Gx3:0-128 Vak0:0-256 ch Ao:64-128 Vak1:0-256 Ag0:0-64
++o:0-64 +o:64-128 Vg0:128-192 +g0:128-192 +g0:0-64 Ag0:64-128 Vg0:192-256 +g0:192-256 +g0:64-128 Vg1:192-256 Ag1:0-64 Ae0:0-256 s0:0-256 Gx3:128-256
++g1:192-256 +g1:0-64 Ag1:64-128 Vy:0-128 +g1:64-128 Ag2:128-192 +g2:128-192 Ae1:0-128 Ae1:192-256 Ae2:128-192 s1:0-256 +y:0-128 Akcf spc cm +kcf
+Ao:128-192 +o:128-192 an0 Vy:128-256 rm0 cD Ao:192-256 ni0 +y:128-256 +kx0 +o:192-256 an1 nvr bp0 rm1 Ak0 Ak1 kv ni1 +kx1 w v bm bp1 lh lhm rnd na odd naa
+sls torn ntorn off c1 c2 sl ks sp cl l0 l1 rcs
 """
 S1 = """
-cw Acrep sr Axr Vkl Gx0:0-256 Gx1:0-256 Gx2:0-256 rce0 Gx3:0-128 Vkcf +kcf ch rce1 rcm0 rcm1 cmp +cmp Ao:0-88 Vak0 Aak1 +o:0-64 Vg0:128-192 Ag0:0-64
-+g0:128-192 +g0:0-64 Vg0:192-256 Ag0:64-128 +g0:192-256 +g0:64-128 Vg1:128-192 Ag1:0-64 +g1:128-192 Ae0:0-256 s0:0-256 +g1:0-64 Gx3:128-256
-Vg1:192-256 Ag1:64-128 +g1:192-256 +g1:64-128 nt Ao:88-128 Vy:0-128 Ae1:0-256 s1:0-256 +nt an01 an00 Ao:128-192 +y:0-128 +o:64-192 Vy:128-224
-Ao:192-256 +y:128-224 Vy:224-256 kv an10 u0 +o:192-256 an11 +y:224-256 rm0 nvr ni0 kx0 v0 w1 v1 bm cm rm1 dc ni1 bk0 kx1 rnd fs na naa rn2 bk1 torn nl
-odd lh lhm slm wn sl ks rrv mv tw pm tb qq pp offv sp cl perm rcs
+sr cw Axr Acrep Akl:0-256 Gx0:0-256 Gx1:0-256 Gx2:0-256 Gx3:0-128 Arce +rce cmp +cmp Ao:0-64 +o:0-64 Vak0:128-256 Aak0:0-128 Vg0:128-192
+ch Ag0:0-64 +g0:128-192 +g0:0-64 Aak1:0-256 Vg0:192-256 Ag0:64-128 +g0:192-256 +g0:64-128 Vg1:192-256 Ag1:0-64 Ae0:0-256 s0:0-256 Gx3:128-256
++g1:192-256 +g1:0-64 Ag1:64-128 Vy:0-128 +g1:64-128 Ag2:128-192 +g2:128-192 Ae1:0-128 Ae1:192-256 Ae2:128-192 s1:0-256 +y:0-128 Vkcf cm +kcf
+Ao:64-128 +o:64-128 an0 Vy:128-256 rm0 Ao:128-192 ni0 +y:128-256 +kx0 +o:128-192 Vo:224-256 Ao:192-224 nvr bp0 rm1 +o:192-256 an1 kv ni1 +kx1 w v bm bp1 lh lhm
+rnd na odd naa sls torn ntorn off c1 c2 sl ks sp cl l0 l1 perm rcs
 """
 S3 = """
-cw neg sz +sz Acrep Axr Vkl sr Gx0:0-256 Gx1:0-256 Gx2:0-256 Gx3:0-128 Vkcf ch rce1 rce0 rcm1 cmp rcm0 +cmp Ao:0-72 tr +tr +o:0-64 Vak0 Aak1 Ag0:0-64
-Vg0:128-192 sf +g0:0-64 Ag0:64-128 +sf Vg0:192-256 +g0:128-256 +g0:64-128 Ag1:0-64 Vg1:128-192 +g1:0-64 Ae0:0-256 Gx3:128-256 s0:0-256 Ag1:64-128
-Vg1:192-256 +g1:128-256 +g1:64-128 nt Ao:72-104 hi +hi Vy:0-128 Ae1:0-256 Vo:224-256 s1:0-256 +nt Ao:104-128 Ao:128-192 Vy:128-224 +y:0-128 an00
-+o:64-128 nvr an01 +o:128-192 Ao:192-224 +o:192-256 an10 an11 u0 rm0 w1 v1 v0 bm cm Vy:224-256 ni0 +y:128-256 rnd fs na kx0 nl rn2 slm rm1 sl odd torn
-srl ni1 st bk0 kx1 wn bk1 mv lh lhm dc tw pm tb qq pp fin
+cw sr neg Asz +sz Axr Acrep Akl:0-256 Gx0:0-256 Gx1:0-256 Gx2:0-256 Gx3:0-128 Arce +rce cmp +cmp tr +tr Ao:0-64 +o:0-64 Vak0:128-256 Aak0:0-128 Vg0:128-192
+ch Ag0:0-64 +g0:128-192 +g0:0-64 Aak1:0-256 Vg0:192-256 Ag0:64-128 +g0:192-256 +g0:64-128 Vg1:192-256 Ag1:0-64 Ae0:0-256 s0:0-256 Gx3:128-256
++g1:192-256 +g1:0-64 Ag1:64-128 Vo:192-256 +g1:64-128 Ag2:128-192 +g2:128-192 Ae1:0-128 Ae1:192-256 Ae2:128-192 s1:0-256 Vy:0-128 Vkcf cm
+Ao:64-128 +o:64-128 +o:192-256 +y:0-128 an0 Ao:128-192 +o:128-192 an1 nvr rm0 sf +sf w v bm ni0 Vy:128-192 +kx0 hi rnd na sls sl srl st Vy:192-256
++y:128-256 bp0 odd torn ntorn rm1 ni1 +kx1 bp1 lh lhm c1 c2 fin
+"""
+S0 = """
+idx ch Akl:0-256 +ob cC cmp Ao:0-64 Arce +rce Axr Ax0:0-256 Vak0:0-256 aC0 aC Gx1:0-256 Gx2:0-256 Gx3:0-128 Ag0:0-72 Vak1:0-256 Vg0:128-192 +o:0-64
++cmp +g0:128-192 +g0:0-64 Ag0:72-128 Vg0:192-256 Vkcf +g0:192-256 +g0:64-128 Ag1:0-72 Vg1:128-192 Ae0:0-256 Gx3:128-256 s0:0-256 +g1:128-192 +g1:0-72
+spc Ag1:72-128 Vg1:192-256 cmd Vo:64-96 +g1:192-256 +g1:72-128 Ao:96-144 Vy:0-128 Ae1:0-256 s1:0-256 Ao:144-192 rc Ao:192-256 +cmd +kcf cm +y:0-128
++kn0 +o:64-192 an00 Vy:128-224 +y:128-224 an10 cn Vy:224-256 rm0 ni0 v0 w0 +y:224-256 an01 +o:192-256 an11 Ak0 kv rm1 kx0 ni1 +kx1 +nv v1 w1 bm cD bp1
+bp0 Ak1 rcs nv Vlh rnd na lhm naa ntorn sls odd torn c1 c2 sp Asl off ks cl l0 l1
+"""
+S1 = """
+Acrep cw sr Axr ch Arce Vkl:0-256 Gx0:0-256 Gx1:0-256 Gx2:0-256 Gx3:0-128 +rce +ob cmp Vak0:0-256 cmd Ao:0-96 Ag0:0-56 Aak1:0-256 Vg0:136-200
+Vg0:200-256 Vg1:176-256 Ag0:56-136 cn +cmp +g0:136-200 +g0:0-56 +g0:200-256 +cmd +g0:56-136 +o:0-64 Ag1:0-72 Ae0:0-256 Gx3:128-256 s0:0-256
+Vg1:144-176 Ag1:72-144 +g1:144-192 +g1:0-72 +g1:192-256 +g1:72-144 Ao:96-136 Vkcf Vy:0-128 Ae1:0-256 s1:0-256 Ao:136-192 +y:0-128 +kn0 +kcf cm
+Vy:128-224 Ao:192-256 +o:64-192 an00 an01 +y:128-224 an10 Vy:224-256 rm0 ni0 kx0 w0 v0 +y:224-256 +o:192-256 an11 kv rc +nv rm1 ni1 +kx1 w1 v1 bm bp0
+bp1 nv rcs Vlh rnd na lhm naa odd sls torn ntorn Asl off c2 c1 sp perm ks cl l0 l1
+"""
+S3 = """
+cw Acrep ch +ob sr neg Asz Arce Vkl:0-256 Vxr Gx0:0-256 Gx1:0-256 Gx2:0-256 Gx3:0-128 Gx3:128-256 +sz +rce Vkcf cmp cmd +cmd +cmp Ao:0-88 Aak1:0-256
+Vak0:0-256 Vg0:176-256 Vg0:112-176 Ag0:0-48 Ag0:48-112 +g0:184-256 +g0:112-184 +g0:0-72 +g0:72-112 Ag1:0-88 Ae0:0-256 s0:0-256 Vg1:168-256 Ag1:88-136
++g1:168-256 +g1:0-88 Ag1:136-168 tr +g1:88-168 +o:0-88 Vy:0-128 Ao:88-128 Ae1:0-256 s1:0-256 Ao:128-192 +y:0-128 +kn0 +tr Vy:128-224 +o:88-192 an00 sf
+Ao:192-256 +sf +y:128-224 an10 rm0 Vy:224-256 ni0 kx0 w0 +y:224-256 an01 +o:192-256 an11 rc +nv hi cm rm1 v0 ni1 +kx1 v1 w1 bm bp0 bp1 rnd nv Alh na
+lhm sls odd torn ntorn Asl c1 c2 srl st fin
 """
 SEQ = [S0, S1, S1, S3]
 
@@ -48,11 +67,10 @@ _s("KI", W, "int32")
 _s("K", WX)
 _s("SN", L, "int32")
 _s("IDX", W)
-for _n in ("GO", "GA0", "GA1", "Y", "XR"):
+for _n in ("GO", "GA0", "GA1", "Y", "XR", "EQ"):
     _s(_n, 16 * L, "bfloat16")
 for _n in ("KL", "AK0", "AK1"):
     _s(_n, L, "uint16")
-_s("EQ", 2176, "bfloat16")
 _s("SZ", 3 * L, "float16")
 LOG = {}
 
@@ -72,26 +90,29 @@ _many("ASB", ["AS%d%d" % x for x in _TK], L, "bfloat16")
 _many("TBF", ["TB%d" % t for t in _TT], L, "bfloat16")
 _many("DGB", ["DN%d" % t for t in range(3)], 128, "float16")
 _many("OFB", ["OFF%d" % t for t in _TT], 2, "uint16")
+_many("ZER", ["XZ", "WF"], 96, "bfloat16")
 for _n in ("CREP", "KCF", "SF", "SM", "TR", "ROT"):
     _s(_n, L, "float16")
-for _n in ("KV", "RM", "KX", "XS", "SP", "HI", "GN"):
+for _n in ("KV", "RM", "XS", "SP", "HI", "GN"):
     _s(_n, L)
-for _n in ("RCE", "RC", "NV", "MK0", "NTH", "BM", "RST", "JF", "BF", "D", "NT", "NI"):
+for _n in ("RCE", "RC", "UP", "NV", "MK0", "BM", "JF", "BF", "D", "NI"):
     _s(_n, L, "bfloat16")
 _s("UV", 2 * L, "bfloat16")
-for _n in ("IDH", "IDS", "PERM", "LH", "BDH"):
+for _n in ("IDH", "IDM", "IDS", "LH", "BDH", "PERM"):
     _s(_n, 128, "float16")
-for _n in ("IDB", "BDN", "IDN", "IDK"):
+for _n in ("IDB", "BDS", "IDN", "SG1", "SGN", "RST"):
     _s(_n, 128, "bfloat16")
 for _n in ("ZH", "Z16"):
     _s(_n, 144, "float16")
 _s("ZB", 144, "bfloat16")
-_s("ZG", 48, "float16")
-_s("XZ", 48, "bfloat16")
-_s("MB", 50, "bfloat16")
+for _n in ("ZG", "ZP"):
+    _s(_n, 48, "float16")
 _s("C32", 32, "bfloat16")
 _s("CH", 34, "float16")
+_s("LWB", 16, "float16")
 _s("BK", L + 8)
+_s("SC", 128)
+_s("SLF", 32)
 for _n in ("ISN", "CSI"):
     _s(_n, 8)
 for _n in ("GB16", "CST"):
@@ -100,18 +121,15 @@ for _n in ("PC", "PM"):
     _s(_n, 2, "int32")
 for _n in ("PG", "PH", "PH2"):
     _s(_n, 1, "int32")
-for _n in ("PMF", "WB"):
-    _s(_n, 2)
+_s("PMF", 2)
 for _n in ("PGF", "ZC", "RTC", "PHF", "PHG", "ZGC", "OBC"):
     _s(_n, 1)
 for _n in ("N16", "C2", "RR"):
     _s(_n, 2, "bfloat16")
 for _n in ("EXP", "SL", "NU"):
     _s(_n, 16, "uint16")
-for _n in ("LWB", "RND", "NEG", "NEW", "WT", "WS", "QQ", "CW", "SLF", "NL", "DC", "PP", "PM1", "FS", "RN2"):
+for _n in ("CW", "RND", "NEG", "NEW", "LT"):
     _s(_n, 16)
-for _n in ("ODD", "TORN", "TB"):
-    _s(_n, 16, "bfloat16")
 for _n in ("pZ", "pZ2", "pA", "pK", "pS", "pD", "pF", "pM"):
     _s(_n, 512, "float32", "psum")
 
@@ -212,8 +230,8 @@ def rank_program(g, core, T, topo):
     def cp(o, i, rd=()):
         return op("v", [i[0]] + list(rd), [o[0]], lambda: V.tensor_copy(o[1], i[1]))
 
-    def scan(o, d0, d1, op0):
-        return op("v", [d0[0], d1[0]], [o[0]], lambda: V.tensor_tensor_scan(o[1], d0[1], d1[1], 0.0, op0, Op.max))
+    def scan(o, d0, d1, op0, op1):
+        return op("v", [d0[0], d1[0]], [o[0]], lambda: V.tensor_tensor_scan(o[1], d0[1], d1[1], 0.0, op0, op1))
 
     def act(o, i, fn=Fn.Copy, rd=(), **kw):
         return op("a", [i[0]] + list(rd), [o[0]], lambda: A.activation(o[1], i[1], fn, **kw))
@@ -226,12 +244,12 @@ def rank_program(g, core, T, topo):
             return last
         return op("p", rd, [bank], f)
 
-    def ap(name, lo=0, hi=None):
+    def ap(name, lo=0, hi=None, step=None):
         base, o, n = LOG.get(name, (name, 0, SCRATCH[name][1][1] if name in SCRATCH else 0))
-        return T[base][:, o + lo:o + (n if hi is None else hi)]
+        return T[base][:, o + lo:o + (n if hi is None else hi):step]
 
-    def b(name, lo=0, hi=None, key=None):
-        return (key or name, ap(name, lo, hi))
+    def b(name, lo=0, hi=None, key=None, step=None):
+        return (key or name, ap(name, lo, hi, step))
 
     def by(name, lst, hi=None):
         return (name, ap(name, 0, hi).indirect(lst))
@@ -242,9 +260,9 @@ def rank_program(g, core, T, topo):
     def cells(name, lo, hi):
         return ["%s.%d" % (name, c) for c in range(lo // CELL, (hi + CELL - 1) // CELL)]
 
-    def iota(name, pattern, base, cm):
-        kw = {} if SCRATCH[name][2] == "int32" else {"allow_small_or_imprecise_dtypes": True}
-        return op("q", [], [name], lambda: g.iota(T[name][:], pattern, base, cm, **kw))
+    def iota(o, pattern, base, cm):
+        kw = {} if SCRATCH[o[0].split(".")[0]][2] == "int32" else {"allow_small_or_imprecise_dtypes": True}
+        return op("q", [], [o[0]], lambda: g.iota(o[1], pattern, base, cm, **kw))
 
     def fill(o, val):
         return op("v", [], [o[0]], lambda: V.memset(o[1], val))
@@ -264,36 +282,38 @@ def rank_program(g, core, T, topo):
 
     left = [0]
 
-    def send_list(t):
+    def send(t, k, way, out, src, keys, sem, lands):
+        dst, frm = (T.cores[(rank + w * (1 + (2 * t + k) % 7)) % NR] for w in (way, -way))
+        rid, pid, _x = topo.addr(dst)
+        deps("q", keys, [])
+        g.remote_dma(out, src, T.sem[sem], T.sem.loc, pid, rid, topo.mask(core, dst))
+        left[0] += len(topo.engines(core, dst))
+        for c in lands:
+            landed(c, sem, len(topo.engines(frm, core)))
+
+    def send_list(t, k):
+        send(t, k, 1, ap("RQ%d%d" % (t, k)), ap("CL%d" % t), ["CL%d" % t], "rq%d%d" % (t, k), ["RQ%d%d" % (t, k)])
+
+    def send_lists(t):
         trs = []
         for k in range(2):
-            dst = T.cores[(rank + 1 + ((2 * t + k) % 7)) % NR]
+            dst, frm = (T.cores[(rank + w * (1 + (2 * t + k) % 7)) % NR] for w in (1, -1))
             es = topo.engines(core, dst)
             half = len(es) // 2
-            m = 0
-            for e in es[k * half:(k + 1) * half]:
-                m |= 1 << e
             rid, pid, _x = topo.addr(dst)
-            trs.append(RemoteDMATransfer(dst_ids=[DstId(rid=rid, pnc=pid)], dma_engine_mask=m, remote_sem=T.sem["rq%d%d" % (t, k)],
-                                         src=ap("CL%d" % t), dst=ap("RQ%d%d" % (t, k))))
-            a = T.cores[(rank - 1 - ((2 * t + k) % 7)) % NR]
-            landed("RQ%d%d" % (t, k), "rq%d%d" % (t, k), len(topo.engines(a, core)) // 2)
+            trs.append(RemoteDMATransfer(dst_ids=[DstId(rid=rid, pnc=pid)], dma_engine_mask=sum(1 << e for e in es[k * half:(k + 1) * half]),
+                                         remote_sem=T.sem["rq%d%d" % (t, k)], src=ap("CL%d" % t), dst=ap("RQ%d%d" % (t, k))))
+            landed("RQ%d%d" % (t, k), "rq%d%d" % (t, k), len(topo.engines(frm, core)) // 2)
             left[0] += half
         deps("q", ["CL%d" % t], [])
         g.remote_dma_fused(trs, local_sem=T.sem.loc)
 
     def send_sums(t, k, lo, hi):
-        asker = T.cores[(rank - 1 - ((2 * t + k) % 7)) % NR]
-        rid, pid, _x = topo.addr(asker)
-        sem = "rs%d%d_%d" % (t, k, lo)
-        deps("q", cells("AS%d%d" % (t, k), lo, hi), [])
-        g.remote_dma(ap("RS%d%d" % (t, k), lo, hi), ap("AS%d%d" % (t, k), lo, hi), T.sem[sem], T.sem.loc, pid, rid, topo.mask(core, asker))
-        left[0] += len(topo.engines(core, asker))
-        q = T.cores[(rank + 1 + ((2 * t + k) % 7)) % NR]
-        for c in cells("RS%d%d" % (t, k), lo, hi):
-            landed(c, sem, len(topo.engines(q, core)))
+        rs, sums = "RS%d%d" % (t, k), "AS%d%d" % (t, k)
+        send(t, k, -1, ap(rs, lo, hi), ap(sums, lo, hi), cells(sums, lo, hi), "rs%d%d_%d" % (t, k, lo), cells(rs, lo, hi))
 
     H = ("pS", T.pS[:, L:2 * L])
+    CW = b("CW")
 
     def wrapped(out, z, src, n, start, fin):
         return [(out, T[z][:, 15 - j:143 - j], T[src][:, j:16 * n:16], start and j == 0, fin and j == 15) for j in range(16)]
@@ -312,77 +332,80 @@ def rank_program(g, core, T, topo):
 
     ROT = ["ROT.0", "ROT.128"]
 
-    iota("D", [[1, L]], 0, -1)
-    iota("JF", [[0, 16], [1, 16]], 0, 0)
-    for nm, lo, hi, x in (("C32", 0, 16, 1.0 + 3.25 / 16.0), ("MB", 0, 50, 0.0), ("C32", 16, 32, 0.7421875), ("N16", 0, 2, -16.0), ("NEG", 0, 16, -1.0),
-                          ("XZ", 0, 48, 0.0), ("C2", 0, 2, -float(MOD)), ("BK", 0, 8, 0.0)):
-        fill(b(nm, lo, hi), x)
-    ts(b("WB", 1, 2, "WB.1"), b("D", 0, 1), XD, -X0, Op.mult, Op.add)
-    act(b("XS"), b("D"), Fn.Silu, rd=["WB.1"], scale=-XD, bias=col("WB", 1))
-    ts(b("PC", 0, 1, "PC.0"), b("D", 0, 1), -1.0, None, Op.mult)
-    ts(b("PC", 1, 2, "PC.1"), b("D", 0, 1), -13.0, None, Op.mult)
-    ts(b("PM"), b("PC", 0, 2, "PC.0"), 15, None, Op.bitwise_and, rd=["PC.1"])
-    ts(b("PG"), b("PC", 0, 1, "PC.0"), 4, None, Op.arith_shift_right)
-    ts(b("ZC"), b("PM", 0, 1), -1.0, 15.0, Op.mult, Op.add)
-    cp(b("PMF"), b("PM"))
-    ts(b("ZH"), b("D", 0, 144), col("ZC"), None, Op.is_equal, rd=["ZC"])
-    ts(b("MK0"), b("JF"), col("PMF", 1), None, Op.is_equal, rd=["PMF"])
-    ts(b("WB", 0, 1, "WB.0"), b("PMF", 0, 1), -XD, col("WB", 1), Op.mult, Op.add, rd=["WB.1"])
-    tt(b("SM"), b("SN"), b("MK0"), Op.mult)
-    mms("pM", wrapped(T.pM[:, 0:16], "ZH", "SM", 16, True, True), ["ZH", "SM"])
-    tt(b("BF"), b("JF"), b("D"), Op.subtract)
-    ts(b("RTC"), b("PG"), -15.0, None, Op.mult)
-    ts(b("BDH"), b("BF", 0, 128), col("PMF"), None, Op.is_equal, rd=["PMF"])
-    ts(b("RTC"), b("PMF", 0, 1), 7.0, col("RTC"), Op.mult, Op.add, rd=["RTC"])
-    ts(b("IDH"), b("D", 0, 128), 0.0, None, Op.is_equal)
-    cp(b("CL0"), ("pM", T.pM[:, 0:16]))
-    send_list(0)
-    for lo in (0, 128):
-        ts(b("ROT", lo, lo + 128, "ROT.%d" % lo), b("D", 0, 128), col("RTC"), None, Op.is_equal, rd=["RTC"])
-    cp(b("PGF"), b("PG"))
-
     def scaled(names):
         for nm, src, f in names:
             act(b(nm), b(src), Fn.Identity, scale=f)
 
-    iota("LWB", [[16, 16]], W, 1)
-    iota("CSI", [[16, 4], [0, 2]], 16, 0)
-    for x in (0, 2):
-        ts(b("SZ", x * L, x * L + L, "SZ.%d" % x), b("MK0"), 0.0, None, Op.mult)
-    ts(b("ISN", 0, 4), b("JF", 0, 4), col("PMF"), None, Op.not_equal, rd=["PMF"])
-    ts(b("OBC"), b("PMF", 0, 1), -16.0, col("D"), Op.mult, Op.subtract, rd=["D"])
-    ts(b("ZGC"), b("PG"), -16.0, 16.0, Op.mult, Op.add)
-    act(b("WS"), ("D", T.D[:, 0::16]), Fn.Silu, rd=["WB.0"], scale=-XD, bias=col("WB"))
+    iota(b("PC", 0, 1, "PC.0"), [[0, 1]], 0, 1)
+    iota(b("PC", 1, 2, "PC.1"), [[0, 1]], 0, 13)
+    iota(b("D"), [[1, L]], 0, -1)
+    iota(b("JF"), [[0, 16], [1, 16]], 0, 0)
+    iota(b("CSI"), [[16, 4], [0, 2]], 16, 0)
+    op("v", [], ["XZ", "WF"], lambda: V.memset(T.ZER[:], 0.0))
+    fill(b("C32", 0, 16), 1.0 + 3.25 / 16.0)
+    ts(b("PM"), b("PC", 0, 2, "PC.0"), 15, None, Op.bitwise_and, rd=["PC.1"])
+    ts(b("PG"), b("PC", 0, 1, "PC.0"), 4, None, Op.arith_shift_right)
+    fill(b("C32", 16, 32, "C32.1"), 0.7421875)
+    ts(b("ZC"), b("PM", 0, 1), -1.0, 15.0, Op.mult, Op.add)
+    cp(b("PMF"), b("PM"))
+    ts(b("RTC"), b("PG"), -15.0, None, Op.mult)
+    act(b("LWB"), b("D", 0, L, None, 16), Fn.Silu, scale=2.0, bias=float(W + L))
+    ts(b("IDH"), b("D", 0, 128), 0.0, None, Op.is_equal)
+    ts(b("ZH"), b("D", 0, 144), col("ZC"), None, Op.is_equal, rd=["ZC"])
+    ts(b("RTC"), b("PMF", 0, 1), 7.0, col("RTC"), Op.mult, Op.add, rd=["RTC"])
+    ts(b("MK0"), b("JF"), col("PMF", 1), None, Op.is_equal, rd=["PMF"])
+    for lo in (0, 128):
+        ts(b("ROT", lo, lo + 128, "ROT.%d" % lo), b("D", 0, 128), col("RTC"), None, Op.is_equal, rd=["RTC"])
+    tt(b("SM"), b("SN"), b("MK0"), Op.mult)
+    mms("pM", wrapped(T.pM[:, 0:16], "ZH", "SM", 16, True, True), ["ZH", "SM"])
+    tt(b("BF"), b("JF"), b("D"), Op.subtract)
     act(b("SF"), b("SN"))
-    act(b("WT"), b("WS"), Fn.Square, scale=2.0 ** 60)
-    act(b("NTH"), b("XS"), Fn.Square, scale=2.0 ** 60 * math.sqrt(2.55))
-    scaled((("ZB", "ZH", -1.0), ("Z16", "ZH", 1.0 / 16.0), ("IDB", "IDH", 1.0)))
+    act(b("SG1"), b("JF", 0, 128), Fn.Sign, scale=-1.0, bias=7.5)
+    scaled((("SGN", "SG1", BIG),))
+    ts(b("BDH"), b("BF", 0, 128), col("PMF"), None, Op.is_equal, rd=["PMF"])
+    ts(b("UP"), b("JF"), col("PMF"), 4096.0, Op.is_le, Op.mult, rd=["PMF"])
+    cp(b("CL0"), ("pM", T.pM[:, 0:16]))
+    send_lists(0)
+
     mms("pK", [(T.pK[:, 0:L], T.BDH[:], T.SM[:], True, True)], ["BDH", "SM"])
     mms("pS", [(T.pS[:, L + 16 * j:L + 16 * j + 16], rot(j), T.SF[:, j::16], True, True) for j in range(16)], ROT + ["SF"])
-    act(b("CW"), ("pM", T.pM[:, 0:16]))
+    tt(b("BDS"), b("BDH"), b("SGN"), Op.mult)
+    for x in (0, 2):
+        ts(b("SZ", x * L, x * L + L, "SZ.%d" % x), b("MK0"), 0.0, None, Op.mult)
+    scaled((("IDB", "IDH", 1.0), ("IDM", "IDH", -1.0), ("IDN", "IDH", -1.0)))
+    act(CW, ("pM", T.pM[:, 0:16]))
     act(b("CREP"), ("pK", T.pK[:, 0:L]))
-    scaled((("BDN", "BDH", -1.0), ("IDS", "IDH", 1.0 / 4096.0)))
     act(b("SZ", L, 2 * L), H)
     turn(lambda q: T.IDH[:, q::8])
-    scaled((("IDN", "IDH", -1.0), ("IDK", "IDH", BIG)))
 
-    def more_constants():
+    def vector_constants():
+        ts(b("OBC"), b("PMF", 0, 1), -16.0, col("D"), Op.mult, Op.subtract, rd=["D"])
+        ts(b("ISN", 0, 4), b("JF", 0, 4), col("PMF"), None, Op.not_equal, rd=["PMF"])
+        cp(b("PGF"), b("PG"))
+        ts(b("ZGC"), b("PG"), -16.0, 16.0, Op.mult, Op.add)
         ts(b("TB0"), b("BF"), col("OBC"), 8.0, Op.is_equal, Op.mult, rd=["OBC"])
-        ts(b("DN0"), b("IDH"), col("ISN"), None, Op.mult, rd=["ISN"])
-
-    def last_constants():
-        ts(b("CH", 0, 2, "CH0"), b("PMF"), 0.0, None, Op.mult)
-        ts(b("OFF0"), b("PMF"), col("PMF"), None, Op.min)
-        ts(b("RST", 0, 128), b("JF", 0, 128), 1.0, None, Op.min)
-        ts(b("CST"), b("CSI"), col("PMF"), None, Op.add, rd=["PMF"])
+        ts(b("BM"), b("BF"), col("OBC"), BIG * BIG, Op.not_equal, Op.mult, rd=["OBC"])
         ts(b("GB16"), b("JF", 0, 8), col("PGF"), 16.0, Op.is_equal, Op.mult, rd=["PGF"])
+        ts(b("ZP"), b("D", 0, 48), col("ZGC"), 4096.0, Op.is_equal, Op.mult, rd=["ZGC"])
+
+    def late_constants():
         ts(b("PH"), b("PM", 0, 1), 8, None, Op.bitwise_and)
         ts(b("PH2"), b("PM", 0, 1), 7, None, Op.bitwise_and)
-        ts(b("ZG"), b("D", 0, 48), col("ZGC"), -4096.0, Op.is_equal, Op.mult, rd=["ZGC"])
         ts(b("PHF"), b("PH"), 16.0, col("D"), Op.mult, Op.subtract, rd=["D"])
         ts(b("PHG"), b("PH2"), col("PGF"), None, Op.is_equal, rd=["PGF"])
-        ts(b("BM"), b("BF"), col("OBC"), -BIG, Op.is_equal, Op.mult, rd=["OBC"])
         ts(b("EXP", 0, 8), ("D", T.D[:, 23:151:16]), col("PHF"), col("PHG"), Op.add, Op.mult, rd=["PHF", "PHG"])
+
+    def scalar_constants():
+        scaled((("ZG", "ZP", -1.0),))
+        act(b("DN0"), b("IDH"), Fn.Identity, rd=["ISN"], scale=col("ISN", 0))
+
+    def first_scalar_constants():
+        scaled((("IDS", "IDH", 1.0 / 4096.0), ("ZB", "ZH", -1.0), ("Z16", "ZH", 1.0 / 16.0)))
+        act(b("RST"), b("JF", 0, 128), Fn.Sign)
+        act(b("CST"), b("CSI"), Fn.Identity, rd=["PMF"], bias=col("PMF"))
+        act(b("OFF0"), b("PMF"))
+        for o, n, x in ((b("N16"), 2, -16.0), (b("C2"), 2, -float(MOD)), (b("NEG"), 16, -1.0), (b("BK", 0, 8), 8, 0.0), (b("CH", 0, 2, "CH0"), 2, 0.0)):
+            act(o, b("JF", 0, n), Fn.Identity, scale=0.0, bias=x)
 
     def round_constants(t):
         act(b("TB%d" % t), b("TB0"), Fn.Identity, scale=(8 + t) / 8.0)
@@ -390,54 +413,43 @@ def rank_program(g, core, T, topo):
             act(b("DN%d" % t), b("IDH"), Fn.Identity, rd=["ISN"], scale=col("ISN", t))
 
     EVEN = 1.5 * 2.0 ** 20
-    CW = b("CW")
-    NA = b("XZ", 16, 32)
+    NA = b("XZ", 33, 64, None, 2)
     F0, F1 = ("pF", T.pF[:, 0:16]), ("pF", T.pF[:, 16:32])
-    BUF = {"g0": ("GA0", "AK0"), "g1": ("GA1", "AK1"), "o": ("GO", "KL")}
-    ABANK = (("pA", 0), ("pF", L))
-    KEY = (("pK", T.pK[:, 0:128]), ("pA", T.pA[:, 0:128]))
-    PART = ((0, ZS), (ZS, L))
-    Z = (("pZ", T.pZ[:, 0:ZS]), ("pZ2", T.pZ2[:, 0:L - ZS]))
+    BUF = {"g0": ("GA0", "AK0"), "g1": ("GA1", "AK1"), "g2": ("GA1", "AK1"), "o": ("GO", "KL")}
+    ABANK = (("pA", 0), ("pF", L), ("pD", 0))
+    KEY = ("pK", "pA")
+    ZBANK, PART = ("pZ", "pZ2"), ((0, ZS), (ZS, L))
+    WF = ["WF", "WF.o", "WF.n", "WF.t"]
 
-    def kin_gather(q, out, lst, t):
-        src, x = ((["KI.0", "KI.1"], T.KI[:].indirect(ap(lst))), 0.25) if t == 0 else (by("K", ap(lst), W), 0.25 - KOFF)
+    def kin_gather(q, out, lst, lo, hi, t):
+        l = ap(lst, lo // 16, hi // 16)
+        src, x = ((["KI.0", "KI.1"], T.KI[:].indirect(l)), 0.25) if t == 0 else (by("K", l, W), 0.25 - KOFF)
+        o = (cells(out, lo, hi), ap(out, lo, hi))
         if q == "a":
-            act(b(out), src, Fn.Identity, rd=[lst], bias=x)
+            act(o, src, Fn.Identity, rd=[lst], bias=x)
         else:
-            ts(b(out), src, x, None, Op.add, rd=[lst])
+            ts(o, src, x, None, Op.add, rd=[lst])
+
+    def over_bar(q, o, lst, keys, t):
+        if q == "a":
+            act(o, by("R", lst, W), Fn.Relu, rd=keys, bias=EPS - (5 + t))
+        else:
+            ts(o, by("R", lst, W), EPS - (5 + t), 0.0, Op.add, Op.max, rd=keys)
 
     def rec_piece(q, kind, lo, hi, t):
         G, lst = BUF[kind]
-        o, i = (cells(G, lo, hi), T[G][:, 16 * lo:16 * hi]), by("R", T[lst][:, lo:hi], W)
-        if q == "a":
-            act(o, i, Fn.Relu, rd=[lst], bias=EPS - (5 + t))
-        else:
-            ts(o, i, EPS - (5 + t), 0.0, Op.add, Op.max, rd=[lst])
-
-    def rec_sum(kind, lo, hi):
-        G = BUF[kind][0]
-        whole = kind != "o"
-        bank, c0 = (ABANK[int(kind[1])][0], ABANK[int(kind[1])][1] + lo) if whole else (("pZ2", lo - ZS) if lo >= ZS else ("pZ", lo))
-        parts = [(T[bank][:, c0:c0 + hi - lo], T.IDB[:], T[G][:, 16 * lo + m:16 * hi:16], whole and m == 0, whole and m == 15) for m in range(16)]
-        mms(bank, parts, cells(G, lo, hi) + ["IDB"])
+        over_bar(q, (cells(G, lo, hi), T[G][:, 16 * lo:16 * hi]), T[lst][:, lo:hi], cells(lst, lo, hi), t)
 
     def compare_lanes():
-        for bb in range(16):
-            n, o = L - 16 * bb, sum(L - 16 * x for x in range(bb))
-            ts(("EQ.%d" % bb, T.EQ[:, o:o + n]), ("CREP", T.CREP[:, 16 * bb:L]), col("CW", bb), col("WT", bb), Op.is_equal, Op.mult, rd=["CW", "WT"])
-
-    def count_lanes():
-        mms("pD", [(T.pD[:, 0:L], T.IDB[:], T.NTH[:], True, False)], ["IDB", "NTH"])
-        for bb in range(16):
-            n, o = L - 16 * bb, sum(L - 16 * x for x in range(bb))
-            mms("pD", [(T.pD[:, 16 * bb:L], T.BDN[:], T.EQ[:, o:o + n], False, bb == 15)], ["EQ.%d" % bb, "BDN"])
+        for bb in range(15):
+            ts(("EQ.%d" % bb, T.EQ[:, L * bb + 16 * bb + 16:L * bb + L]), ("CREP", T.CREP[:, 16 * bb + 16:L]), col("CW", bb), None, Op.is_equal, rd=["CW"])
 
     def best_piece(lo, hi):
         sl = slice(16 * lo, 16 * hi)
-        tt((cells("Y", lo, hi), T.Y[:, sl]), by("X", T.KL[:, lo:hi]), (cells("XR", lo, hi), T.XR[:, sl]), Op.max, rd=["KL"])
+        tt((cells("Y", lo, hi), T.Y[:, sl]), by("X", T.KL[:, lo:hi]), (cells("XR", lo, hi), T.XR[:, sl]), Op.max, rd=cells("KL", lo, hi))
 
     def best_sum(lo, hi):
-        bank, p0 = KEY[lo // 128][0], lo % 128
+        bank, p0 = KEY[lo // 128], lo % 128
         parts = [(T[bank][:, 0:128], T.IDN[:], T.JF[:, 0:128], True, False)] if p0 == 0 else []
         for m in range(16):
             parts.append((T[bank][p0:p0 + hi - lo, m:128:16], T.Y[:, 16 * lo + m:16 * hi:16], T.GB16[:], False, m == 15))
@@ -445,14 +457,14 @@ def rank_program(g, core, T, topo):
 
     def best_steps(h):
         lo, hi = 128 * h, 128 * h + 128
-        rm, ni, kx = (b(n, lo, hi, "%s.%d" % (n, h)) for n in ("RM", "NI", "KX"))
-        return {"rm%d" % h: lambda: scan(rm, b("RST", 0, 128), KEY[h], Op.mult),
-                "ni%d" % h: lambda: tt(ni, rm, KEY[h], Op.subtract),
-                "kx%d" % h: lambda: tt(kx, ("pS", T.pS[:, lo:hi]), ni, Op.subtract),
-                "bk%d" % h: lambda: scan(b("BK", 8 + lo, 8 + hi, "BK.%d" % h), ni, kx, Op.min)}
-
-    def kin_numbers():
-        mms("pS", [(T.pS[:, 128 * h:128 * h + 128], T.KCF[:, 128 * h:128 * h + 128], T.IDS[:], h == 0, h == 1) for h in range(2)], ["KCF", "IDS"])
+        rm, ni = (b(n, lo, hi, "%s.%d" % (n, h)) for n in ("RM", "NI"))
+        key, kin = (KEY[h], T[KEY[h]][:, 0:128]), (KEY[h], T[KEY[h]][:, 128:L])
+        return {"rm%d" % h: lambda: scan(rm, b("RST"), key, Op.mult, Op.max),
+                "ni%d" % h: lambda: tt(ni, rm, key, Op.subtract),
+                "+kx%d" % h: lambda: mms(KEY[h], [(kin[1], T.KCF[:, lo:hi], T.IDS[:], True, False), (kin[1], T.IDN[:], ni[1], False, True)], ["KCF", "IDS", "IDN", ni[0]]),
+                "bp%d" % h: lambda: scan(b("BK", 8 + lo, 8 + hi, "BK.%d" % h), ni, kin, Op.min, Op.max),
+                "+kn%d" % h: lambda: mms(KEY[h], [(kin[1], T.KCF[:, lo:hi], T.IDS[:], True, True)], ["KCF", "IDS"]),
+                "kx%d" % h: lambda: tt(kin, kin, ni, Op.subtract)}
 
     def double(q, s, lo, hi):
         st, keys = 8 >> s, cells("XR", lo, hi)
@@ -467,15 +479,51 @@ def rank_program(g, core, T, topo):
         cl = "CL%d" % t
         off = ap("OFF%d" % t, 0, 1)
         words = SEQ[t].split()
-        kept = ("pM", T.pM[:, 128:128 + L]) if last else H
+        done = []
+
+        def into_sums(lo, hi, parts, rd, start=False, fin=False):
+            for bank, (a, z) in zip(ZBANK, PART):
+                a, z = max(a, lo), min(z, hi)
+                if a < z:
+                    ps = parts(T[bank], a, z)
+                    mms(bank, [(o, l, r, start, fin) for o, l, r in ps], rd)
+
+        def rec_sum(kind, lo, hi):
+            G = BUF[kind][0]
+            if kind == "o":
+                into_sums(lo, hi, lambda p, a, z: [(p[:, a:z], T.IDB[:], T.GO[:, 16 * a + m:16 * z:16]) for m in range(16)], cells(G, lo, hi) + ["IDB"])
+            else:
+                bank, c0 = ABANK[int(kind[1])]
+                mms(bank, [(T[bank][:, c0 + lo:c0 + hi], T.IDB[:], T[G][:, 16 * lo + m:16 * hi:16], m == 0, m == 15) for m in range(16)], cells(G, lo, hi) + ["IDB"])
+
+        def count_lanes():
+            for bb in range(15):
+                into_sums(16 * bb + 16, L, lambda p, a, z: [(p[:, a:z], T.BDS[:], T.EQ[:, L * bb + a:L * bb + z])], ["EQ.%d" % bb, "BDS"])
+
+        def own_bags():
+            parts = [(T.pD[:, 0:L], T.IDB[:], T.UP[:], True, False)] + [(T.pD[:, j:L:16], T.IDH[:], T.CH[:, 2:18], False, j == 15) for j in range(16)]
+            mms("pD", parts, ["IDB", "UP", "IDH", "CH"])
+
+        def part_steps(h):
+            lo, hi = PART[h]
+            z = (ZBANK[h], T[ZBANK[h]][:, lo:hi])
+            fin = max(words.index("an%d%d" % (k, h)) for k in range(2))
+
+            def answer(k):
+                rs = "RS%d%d" % (t, k)
+                into_sums(lo, hi, lambda p, a, z: [(p[:, a:z], T.IDB[:], ap(rs, a, z))], ["IDB"] + cells(rs, lo, hi), fin=words[fin] == "an%d%d" % (k, h))
+
+            return {"an0%d" % h: lambda: answer(0), "an1%d" % h: lambda: answer(1),
+                    "w%d" % h: lambda: ts(b("UV", lo, hi, "U.%d" % h), z, 0.7, 1.0 / 16.0, Op.is_lt, Op.mult),
+                    "v%d" % h: lambda: tt(b("UV", L + lo, L + hi, "V.%d" % h), z, b("BM", lo, hi), Op.is_gt)}
 
         def kin_moves():
             parts = [(T.pM[:, 128:128 + L], ap("DN%d" % t), T.KCF[:], True, False)]
             parts += [(T.pM[:, 128 + e:128 + L:2], T.Z16[:, 15 - t:143 - t], T.CREP[:, 1 - e::2], False, e == 1) for e in range(2)]
             mms("pM", parts, ["DN%d" % t, "Z16", "KCF", "CREP"])
-            kin_numbers()
 
-        def new_records(u):
+        def new_records():
+            u = t if done[-1] == "srl" else t - 1
             if "nvr" in SEQ[u].split():
                 op("v", ["NV", "SL"], ["R"], lambda: V.tensor_copy(T.R[:].indirect(T.SL[:]), T.NV[:]))
             else:
@@ -483,134 +531,128 @@ def rank_program(g, core, T, topo):
 
         def evacuate(q, k, lo, hi):
             bank, c0 = ABANK[k]
-            copy(q)((cells("AS%d%d" % (t, k), lo, hi), ap("AS%d%d" % (t, k), lo, hi)), (bank, T[bank][:, c0 + lo:c0 + hi]))
-
-        def addend(w, src, h):
-            lo, hi = PART[h]
-            fin = w == [x for x in words if x in ("an0%d" % h, "an1%d" % h)][-1]
-            mms(Z[h][0], [(Z[h][1], T.IDB[:], ap(src, lo, hi), w[0] == "r", fin)], ["IDB"] + cells(src, lo, hi))
-
-        def part_steps(h):
-            lo, hi = PART[h]
-            u = b("UV", lo, hi, "U.%d" % h)
-            return {"rce%d" % h: lambda: act((cells("RCE", lo, hi), ap("RCE", lo, hi)), by("R", ap(cl, lo // 16, hi // 16), W), Fn.Relu, rd=[cl], bias=EPS - (5 + t)),
-                    "rcm%d" % h: lambda: addend("rcm", "RCE", h),
-                    "an0%d" % h: lambda: addend("an0%d" % h, "RS%d0" % t, h),
-                    "an1%d" % h: lambda: addend("an1%d" % h, "RS%d1" % t, h),
-                    "u%d" % h: lambda: act(u, Z[h], Fn.Relu, scale=-1.0 / 16.0, bias=(1.0 - BIG) / 16.0),
-                    "w%d" % h: lambda: ts(u, Z[h], 0.7 - BIG, 1.0 / 16.0, Op.is_lt, Op.mult),
-                    "v%d" % h: lambda: tt(b("UV", L + lo, L + hi, "V.%d" % h), Z[h], b("BM", lo, hi), Op.is_gt)}
+            sums = "AS%d%d" % (t, min(k, 1))
+            copy(q)((cells(sums, lo, hi), ap(sums, lo, hi)), (bank, T[bank][:, c0 + lo:c0 + hi]))
 
         def citizens():
-            mms("pM", [(T.pM[:, 16:32], T.IDH[:], T.CH[:, 2:18], True, False)], ["IDH", "CH"])
-            if not last:
-                mms("pD", [(T.pD[:, L:L + 2], T.IDB[:], T.CST[:, 2 * t:2 * t + 2], True, False), (T.pD[:, L:L + 2], T.IDB[:], T.C2[:], False, False)],
-                    ["IDB", "CST", "C2"])
+            c, before = T.CH[:, 2:18], T.CH[:, 1:17]
+            mms("pS", [(T.pS[:, 0:128], T.IDH[:], T.SZ[:, 0:128], True, False), (T.pS[:, 0:64:4], T.IDH[:], before, False, False),
+                       (T.pS[:, 2:64:4], T.IDM[:], c, False, False), (T.pS[:, 3:64:4], T.IDH[:], c, False, False), (T.pS[:, 64:128:4], T.IDM[:], c, False, False)],
+                ["IDH", "IDM", "CH", "CH0", "SZ.0"])
+            mms("pM", [(T.pM[:, 0:32:2], T.IDH[:], T.LWB[:], True, False), (T.pM[:, 0:32:2], T.IDM[:], c, False, False), (T.pM[:, 1:32:2], T.IDH[:], c, False, True)],
+                ["IDH", "IDM", "CH", "LWB"])
+
+        def place_addends():
+            mms("pD", [(T.pD[:, L:L + 2], T.IDB[:], T.CST[:, 2 * t:2 * t + 2], True, False), (T.pD[:, L:L + 2], T.IDB[:], T.C2[:], False, False)],
+                ["IDB", "CST", "C2"])
+
+        def best_wrapped():
+            parts = []
+            for z, lo in (("ZG", 0), ("ZP", 2), ("ZP", 64)):
+                parts += [(T.pS[32 * (x // 2):32 * (x // 2) + 32, lo:lo + 62:4], T[z][:, 16 - 16 * (x % 2):48 - 16 * (x % 2)], T.LH[:, 16 * x:16 * x + 16],
+                           False, lo == 64 and x % 2 == 1) for x in range(8)]
+            mms("pS", parts, ["LH", "ZG", "ZP"])
+
+        def permutation():
+            if t == RO - 2:
+                mms("pM", [(T.pM[:, 384:512], rot(0), T.IDH[:], True, True)], ROT + ["IDH"])
+                act(b("PERM"), ("pM", T.pM[:, 384:512]))
 
         def store_records():
             deps("a", ["R"], [])
             A.dma_start(T.yr[:], T.R[:, 0:W]).then_inc(T.sem.stR, 16)
 
+        P1, P2 = b("SC", 3, 64, "SC.1", 4), b("SC", 67, 128, "SC.2", 4)
+
         def finish():
-            tt(b("NEW"), b("QQ"), b("PP"), Op.subtract)
+            tt(b("NEW"), P1, P2, Op.add)
             cp(b("NU"), b("NEW"))
             tt(b("GN"), by("IDX", T.NU[:]), b("HI"), Op.min, rd=["NU"])
             tt(b("XS"), b("GN"), H, Op.max)
             deps("s", ["XS"], [])
             g.sync.dma_start(T.ys[:], T.XS[:]).then_inc(T.sem.stS, 16)
 
-        def next_list():
-            cp(b("CL%d" % (t + 1)), by("SP", ap("OFF%d" % (t + 1), 0, 1)), rd=["OFF%d" % (t + 1)])
-            send_list(t + 1)
-
-        def permutation():
-            if t == RO - 2:
-                mms("pZ2", [(T.pZ2[:, L:L + 128], rot(0), T.IDH[:], True, True)], ROT + ["IDH"])
-                act(b("PERM"), ("pZ2", T.pZ2[:, L:L + 128]))
-
-        best_list = ["EXP", "BK.0", "BK.1"]
+        best_list = ["EXP", "BK.0", "BK.1", "BK"]
         either = {
-            "kl": lambda q: kin_gather(q, "KL", cl, t),
-            "ak0": lambda q: kin_gather(q, "AK0", "RQ%d0" % t, t),
-            "ak1": lambda q: kin_gather(q, "AK1", "RQ%d1" % t, t),
-            "kcf": lambda q: copy(q)(b("KCF"), b("KL")),
+            "kcf": lambda q: copy(q)(b("KCF"), (cells("KL", 0, L), T.KL[:])),
             "crep": lambda q: copy(q)(b("CREP"), by("IDX", ap(cl)), rd=[cl]),
             "xr": lambda q: copy(q)((cells("XR", 0, L), T.XR[:, 0::16]), by("X", ap(cl)), rd=[cl]),
+            "rce": lambda q: over_bar(q, b("RCE"), ap(cl), [cl], t),
+            "k0": lambda q: act(b("K", 0, W // 2), b("KI", 0, W // 2, "KI.0"), Fn.Identity, bias=KOFF),
+            "k1": lambda q: act(b("K", W // 2, W), b("KI", W // 2, W, "KI.1"), Fn.Identity, bias=KOFF),
+            "sz": lambda q: copy(q)(b("SZ", L, 2 * L), b("SP")),
+            "sl": lambda q: copy(q)(b("SL"), b("SLF", 1, 32, None, 2)),
+            "lh": lambda q: copy(q)(b("LH"), by("BK", T.EXP[:, 0:8]), rd=best_list),
         }
         step = {
-            "mc": more_constants,
-            "lc": last_constants,
-            "idx": lambda: iota("IDX", [[1, W]], 0, 0),
-            "spc": lambda: cp(b("SP"), H),
-            "k0": lambda: act(b("K", 0, W // 2), b("KI", 0, W // 2, "KI.0"), Fn.Identity, bias=KOFF),
-            "k1": lambda: act(b("K", W // 2, W), b("KI", W // 2, W, "KI.1"), Fn.Identity, bias=KOFF),
+            "cC": vector_constants,
+            "cD": late_constants,
+            "aC": scalar_constants,
+            "aC0": first_scalar_constants,
             "rcs": lambda: round_constants(t + 1),
             "perm": permutation,
-            "sr": lambda: new_records(t - 1),
+            "idx": lambda: iota(b("IDX"), [[1, W]], 0, 0),
+            "spc": lambda: act(b("SP"), H),
+            "sr": new_records,
             "cw": lambda: act(CW, by("SP", off), rd=["OFF%d" % t]),
             "ch": lambda: act(b("CH", 2, 18), CW),
             "+kcf": kin_moves,
             "cmp": compare_lanes,
             "+cmp": count_lanes,
-            "nt": lambda: act(b("NT"), ("pD", T.pD[:, 0:L]), Fn.Sign, scale=-1.0),
-            "+nt": lambda: [mms(Z[h][0], [(Z[h][1], T.IDK[:], ap("NT", *PART[h]), False, False)], ["IDK", "NT"]) for h in range(2)],
+            "+ob": own_bags,
+            "cmd": lambda: tt(b("EQ", 15 * L, 16 * L, "EQ.15"), b("CREP"), ("pD", T.pD[:, 0:L]), Op.is_equal),
+            "+cmd": lambda: into_sums(0, L, lambda p, a, z: [(p[:, a:z], T.BDS[:], T.EQ[:, 15 * L + a:15 * L + z])], ["EQ.15", "BDS"]),
+            "+rce": lambda: into_sums(0, L, lambda p, a, z: [(p[:, a:z], T.IDB[:], T.RCE[:, a:z])], ["IDB", "RCE"], start=True),
             "bm": lambda: mms("pF", [(T.pF[:, 0:32], T.IDB[:], T.C32[:], True, False)] + wrapped(T.pF[:, 0:32], "ZB", "UV", 32, False, True),
-                              ["IDB", "C32", "ZB", "U.0", "U.1", "V.0", "V.1"]),
+                              ["IDB", "C32", "C32.1", "ZB", "U.0", "V.0", "U.1", "V.1"]),
             "neg": lambda: op("v", ["NEG", "OFF%d" % t], ["SP"], lambda: V.tensor_copy(T.SP[:].indirect(off), T.NEG[:])),
-            "sz": lambda: act(b("SZ", L, 2 * L), b("SP")),
             "+sz": lambda: turn(lambda q: T.IDH[:, 16 * q:16 * q + 16]),
             "tr": lambda: act(b("TR"), H),
             "+tr": lambda: mms("pS", [(T.pS[:, L + j:2 * L:16], rot(-j), T.TR[:, 16 * j:16 * j + 16], True, True) for j in range(16)], ROT + ["TR"]),
             "sf": lambda: act(b("SF"), H),
             "+sf": lambda: mms("pS", [(H[1], T.PERM[:], T.SF[:], True, True)], ["PERM", "SF"]),
             "hi": lambda: act(b("HI"), H, Fn.Relu, scale=-4096.0),
-            "+hi": kin_numbers,
             "kv": lambda: act(b("KV"), ("pM", T.pM[:, 128:128 + L]), Fn.Identity, bias=KOFF),
-            "rc": lambda: act(b("RC"), by("R", ap(cl), W), rd=[cl]),
-            "nvm": lambda: mms(kept[0], [(kept[1], T.IDB[:], T.RC[:], True, False), (kept[1], T.IDN[:], ap("TB%d" % t), False, True)], ["IDB", "IDN", "RC", "TB%d" % t]),
-            "nv": lambda: act(b("NV"), kept, Fn.Relu),
             "nvr": lambda: tt(b("NV"), by("R", ap(cl), W), b("TB%d" % t), Op.max, rd=[cl]),
+            "rc": lambda: act(b("RC"), by("R", ap(cl), W), rd=[cl]),
+            "+nv": lambda: mms("pM", [(T.pM[:, 128:128 + L], T.IDB[:], T.RC[:], True, False), (T.pM[:, 128:128 + L], T.IDN[:], ap("TB%d" % t), False, True)],
+                               ["IDB", "IDN", "RC", "TB%d" % t]),
+            "nv": lambda: act(b("NV"), ("pM", T.pM[:, 128:128 + L]), Fn.Relu),
             "cm": citizens,
-            "lh": lambda: act(b("LH"), by("BK", T.EXP[:, 0:8]), rd=best_list),
-            "lhv": lambda: cp(b("LH"), by("BK", T.EXP[:, 0:8]), rd=best_list),
-            "lhm": lambda: mms("pM", [(T.pM[32 * (x // 2):32 * (x // 2) + 32, 16:32], T.ZG[:, 16 - 16 * (x % 2):48 - 16 * (x % 2)], T.LH[:, 16 * x:16 * x + 16],
-                                       False, x % 2 == 1) for x in range(8)], ["LH", "ZG"]),
+            "cn": place_addends,
+            "lhm": best_wrapped,
             "rnd": lambda: ts(b("RND"), F0, EVEN, -EVEN, Op.add, Op.add),
             "na": lambda: tt(NA, b("RND"), F1, Op.is_ge),
-            "odd": lambda: tt(b("ODD"), F0, b("RND"), Op.is_gt),
-            "fs": lambda: ts(b("FS"), F1, 1.0 / 32.0, 0.012, Op.mult, Op.add),
-            "rn2": lambda: tt(b("RN2"), b("RND"), b("FS"), Op.add),
-            "torn": lambda: tt(b("TORN"), b("RN2"), NA, Op.is_ge),
-            "wn": lambda: tt(b("MB", 34, 49, "MB.2"), b("ODD", 0, 15), b("TORN", 1, 16), Op.mult, rd=["MB"]),
-            "mv": lambda: tt(b("MB", 17, 33, "MB.1"), b("MB", 34, 50, "MB.2"), b("TORN"), Op.is_gt),
-            "tw": lambda: tt(b("MB", 0, 16, "MB.0"), b("MB", 34, 50, "MB.2"), b("TORN"), Op.max),
-            "nl": lambda: tt(b("NL"), NA, b("LWB"), Op.mult),
-            "slm": lambda: tt(b("SLF"), b("NL"), CW, Op.max),
-            "sl": lambda: act(b("SL"), b("SLF")),
-            "slv": lambda: cp(b("SL"), b("SLF")),
+            "odd": lambda: tt(b("WF", 5, 69, "WF.o", 4), F0, b("RND"), Op.is_gt, rd=["WF"]),
+            "torn": lambda: tt(b("WF", 3, 64, "WF.t", 4), b("RND"), NA, Op.is_ge, rd=["WF"]),
+            "ntorn": lambda: tt(b("WF", 6, 70, "WF.n", 4), b("RND"), NA, Op.is_lt, rd=["WF"]),
+            "sls": lambda: scan(b("SLF"), b("XZ", 32, 64), ("pM", T.pM[:, 0:32]), Op.mult, Op.add),
             "ks": lambda: op("a", ["KV", "SL"], ["K"], lambda: A.activation(T.K[:].indirect(T.SL[:]), T.KV[:], Fn.Silu)),
-            "srl": lambda: new_records(t),
+            "srl": new_records,
             "st": store_records,
-            "naa": lambda: mms("pD", [(T.pD[32 * p:32 * p + 32, L:L + 2], T.XZ[:, 16 - 16 * e:48 - 16 * e], T.N16[:], False, e == 1) for p in range(4) for e in range(2)],
+            "naa": lambda: mms("pD", [(T.pD[32 * p:32 * p + 32, L:L + 2], ap("XZ", 33 - 32 * e, 96 - 32 * e, 2), T.N16[:], False, e == 1) for p in range(4) for e in range(2)],
                                ["XZ", "N16"]),
             "rrv": lambda: ts(b("RR", 0, 1), ("pD", T.pD[:, L:L + 1]), -1.0, 127.5, Op.mult, Op.add),
             "offv": lambda: ts(b("OFF%d" % (t + 1), 0, 1), ("pD", T.pD[:, L + 1:L + 2]), col("RR"), None, Op.add, rd=["RR"]),
             "off": lambda: [act(b("RR", 0, 1), ("pD", T.pD[:, L:L + 1]), Fn.Identity, scale=-1.0, bias=127.5),
                             act(b("OFF%d" % (t + 1), 0, 1), ("pD", T.pD[:, L + 1:L + 2]), Fn.Identity, rd=["RR"], bias=col("RR"))],
-            "dc": lambda: tt(b("DC"), b("CH", 1, 17), b("CH", 2, 18), Op.subtract, rd=["CH0"]),
-            "pm": lambda: tt(b("PM1"), b("MB", 16, 32, "MB.1"), b("DC"), Op.mult),
-            "tb": lambda: tt(b("TB"), b("MB", 0, 16, "MB.0"), b("MB", 16, 32, "MB.1"), Op.subtract),
-            "qq": lambda: tt(b("QQ"), b("PM1"), CW, Op.add),
-            "pp": lambda: tt(b("PP"), b("TB"), ("pM", T.pM[:, 16:32]), Op.mult),
-            "sp": lambda: op("v", ["QQ", "PP", "OFF%d" % t], ["SP"], lambda: V.tensor_tensor(T.SP[:].indirect(off), T.QQ[:], T.PP[:], Op.subtract)),
-            "cl": next_list,
+            "c1": lambda: scan(b("SC", 0, 64, "SC.1"), (WF, ap("WF", 0, 64)), ("pS", T.pS[:, 0:64]), Op.mult, Op.add),
+            "c2": lambda: scan(b("SC", 64, 128, "SC.2"), (WF, ap("WF", 4, 68)), ("pS", T.pS[:, 64:128]), Op.mult, Op.add),
+            "sp": lambda: op("v", ["SC.1", "SC.2", "OFF%d" % t], ["SP"], lambda: V.tensor_tensor(T.SP[:].indirect(off), P1[1], P2[1], Op.add)),
+            "cl": lambda: cp(b("CL%d" % (t + 1)), by("SP", ap("OFF%d" % (t + 1), 0, 1)), rd=["OFF%d" % (t + 1)]),
+            "cla": lambda: act(b("CL%d" % (t + 1)), by("SP", ap("OFF%d" % (t + 1), 0, 1)), rd=["OFF%d" % (t + 1)]),
+            "l0": lambda: send_list(t + 1, 0),
+            "l1": lambda: send_list(t + 1, 1),
+            "lf": lambda: send_lists(t + 1),
             "fin": finish,
         }
         for h in range(2):
-            step.update(part_steps(h))
             step.update(best_steps(h))
+            if PART[h][0] < L:
+                step.update(part_steps(h))
 
         for word in words:
+            done.append(word)
             q = {"V": "v", "A": "a", "G": "q", "+": "p"}.get(word[0])
             kind, _x, span = (word[1:] if q else word).partition(":")
             if not span:
@@ -623,6 +665,10 @@ def rank_program(g, core, T, topo):
                 best_piece(lo, hi)
             elif kind in BUF:
                 rec_piece(q, kind, lo, hi, t)
+            elif kind == "kl":
+                kin_gather(q, "KL", cl, lo, hi, t)
+            elif kind[0] == "a":
+                kin_gather(q, "AK" + kind[2], "RQ%d%s" % (t, kind[2]), lo, hi, t)
             elif kind[0] == "e":
                 evacuate(q, int(kind[1]), lo, hi)
             elif kind[0] == "s":

from concourse.bass import DstId, RemoteDMATransfer
from concourse.mybir import dt, AluOpType as Op, ActivationFunctionType as Fn

NR, RO, W, L = 8, 4, 2048, 256
WX = W + 3 * L
KOFF = 64.0
EPS = 1.0 / 2048.0
BIG = 1024.0
CELL = 8
MOD = 129 * 256
ZS = 192

S0 = """
idx aT cmp Akl:0-256 cC aC Arce +rce +cmp Ao:0-64 Axr Ax0:0-256 Gx1:0-256 Gx2:0-256 Gx3:0-128 Vak0:0-256 ch Ao:64-128 Vak1:0-256 Ag0:0-64
+o:0-64 +o:64-128 Vg0:128-192 +g0:128-192 +g0:0-64 Ag0:64-128 Vg0:192-256 +g0:192-256 +g0:64-128 Vg1:192-256 Ag1:0-64 Ae0:0-256 s0:0-256 Gx3:128-256
+g1:192-256 +g1:0-64 Ag1:64-128 Vy:0-128 +g1:64-128 Ag2:128-192 +g2:128-192 Ae1:0-128 Ae1:192-256 Ae2:128-192 s1:0-256 +y:0-128 Akcf spc cm +kcf
Ao:128-192 +o:128-192 an0 Vy:128-256 rm0 cD Ao:192-256 ni0 +y:128-256 +kx0 +o:192-256 an1 nvr bp0 rm1 Ak0 Ak1 kv ni1 +kx1 w v bm bp1 lh lhm rnd na odd naa
sls torn ntorn off c1 c2 sl ks sp cl l0 l1 rcs
"""
S1 = """
sr cw Axr Acrep Akl:0-256 Gx0:0-256 Gx1:0-256 Gx2:0-256 Gx3:0-128 Arce +rce cmp +cmp Ao:0-64 +o:0-64 Vak0:128-256 Aak0:0-128 Vg0:128-192
ch Ag0:0-64 +g0:128-192 +g0:0-64 Aak1:0-256 Vg0:192-256 Ag0:64-128 +g0:192-256 +g0:64-128 Vg1:192-256 Ag1:0-64 Ae0:0-256 s0:0-256 Gx3:128-256
+g1:192-256 +g1:0-64 Ag1:64-128 Vy:0-128 +g1:64-128 Ag2:128-192 +g2:128-192 Ae1:0-128 Ae1:192-256 Ae2:128-192 s1:0-256 +y:0-128 Vkcf cm +kcf
Ao:64-128 +o:64-128 an0 Vy:128-256 rm0 Ao:128-192 ni0 +y:128-256 +kx0 +o:128-192 Vo:224-256 Ao:192-224 nvr bp0 rm1 +o:192-256 an1 kv ni1 +kx1 w v bm bp1 lh lhm
rnd na odd naa sls torn ntorn off c1 c2 sl ks sp cl l0 l1 perm rcs
"""
S3 = """
cw sr neg Asz +sz Axr Acrep Akl:0-256 Gx0:0-256 Gx1:0-256 Gx2:0-256 Gx3:0-128 Arce +rce cmp +cmp tr +tr Ao:0-64 +o:0-64 Vak0:128-256 Aak0:0-128 Vg0:128-192
ch Ag0:0-64 +g0:128-192 +g0:0-64 Aak1:0-256 Vg0:192-256 Ag0:64-128 +g0:192-256 +g0:64-128 Vg1:192-256 Ag1:0-64 Ae0:0-256 s0:0-256 Gx3:128-256
+g1:192-256 +g1:0-64 Ag1:64-128 Vo:192-256 +g1:64-128 Ag2:128-192 +g2:128-192 Ae1:0-128 Ae1:192-256 Ae2:128-192 s1:0-256 Vy:0-128 Vkcf cm
Ao:64-128 +o:64-128 +o:192-256 +y:0-128 an0 Ao:128-192 +o:128-192 an1 nvr rm0 sf +sf w v bm ni0 Vy:128-192 +kx0 hi rnd na sls sl srl st Vy:192-256
+y:128-256 bp0 odd torn ntorn rm1 ni1 +kx1 bp1 lh lhm c1 c2 fin
"""
S0 = """
idx ch Akl:0-256 +ob cC cmp Ao:0-64 Arce +rce Axr Ax0:0-256 Vak0:0-256 aC0 aC Gx1:0-256 Gx2:0-256 Gx3:0-128 Ag0:0-72 Vak1:0-256 Vg0:128-192 +o:0-64
+cmp +g0:128-192 +g0:0-64 Ag0:72-128 Vg0:192-256 Vkcf +g0:192-256 +g0:64-128 Ag1:0-72 Vg1:128-192 Ae0:0-256 Gx3:128-256 s0:0-256 +g1:128-192 +g1:0-72
spc Ag1:72-128 Vg1:192-256 cmd Vo:64-96 +g1:192-256 +g1:72-128 Ao:96-144 Vy:0-128 Ae1:0-256 s1:0-256 Ao:144-192 rc Ao:192-256 +cmd +kcf cm +y:0-128
+kn0 +o:64-192 an00 Vy:128-224 +y:128-224 an10 cn Vy:224-256 rm0 ni0 v0 w0 +y:224-256 an01 +o:192-256 an11 Ak0 kv rm1 kx0 ni1 +kx1 +nv v1 w1 bm cD bp1
bp0 Ak1 rcs nv Vlh rnd na lhm naa ntorn sls odd torn c1 c2 sp Asl off ks cl l0 l1
"""
S1 = """
Acrep cw sr Axr ch Arce Vkl:0-256 Gx0:0-256 Gx1:0-256 Gx2:0-256 Gx3:0-128 +rce +ob cmp Vak0:0-256 cmd Ao:0-96 Ag0:0-56 Aak1:0-256 Vg0:136-200
Vg0:200-256 Vg1:176-256 Ag0:56-136 cn +cmp +g0:136-200 +g0:0-56 +g0:200-256 +cmd +g0:56-136 +o:0-64 Ag1:0-72 Ae0:0-256 Gx3:128-256 s0:0-256
Vg1:144-176 Ag1:72-144 +g1:144-192 +g1:0-72 +g1:192-256 +g1:72-144 Ao:96-136 Vkcf Vy:0-128 Ae1:0-256 s1:0-256 Ao:136-192 +y:0-128 +kn0 +kcf cm
Vy:128-224 Ao:192-256 +o:64-192 an00 an01 +y:128-224 an10 Vy:224-256 rm0 ni0 kx0 w0 v0 +y:224-256 +o:192-256 an11 kv rc +nv rm1 ni1 +kx1 w1 v1 bm bp0
bp1 nv rcs Vlh rnd na lhm naa odd sls torn ntorn Asl off c2 c1 sp perm ks cl l0 l1
"""
S3 = """
cw Acrep ch +ob sr neg Asz Arce Vkl:0-256 Vxr Gx0:0-256 Gx1:0-256 Gx2:0-256 Gx3:0-128 Gx3:128-256 +sz +rce Vkcf cmp cmd +cmd +cmp Ao:0-88 Aak1:0-256
Vak0:0-256 Vg0:176-256 Vg0:112-176 Ag0:0-48 Ag0:48-112 +g0:184-256 +g0:112-184 +g0:0-72 +g0:72-112 Ag1:0-88 Ae0:0-256 s0:0-256 Vg1:168-256 Ag1:88-136
+g1:168-256 +g1:0-88 Ag1:136-168 tr +g1:88-168 +o:0-88 Vy:0-128 Ao:88-128 Ae1:0-256 s1:0-256 Ao:128-192 +y:0-128 +kn0 +tr Vy:128-224 +o:88-192 an00 sf
Ao:192-256 +sf +y:128-224 an10 rm0 Vy:224-256 ni0 kx0 w0 +y:224-256 an01 +o:192-256 an11 rc +nv hi cm rm1 v0 ni1 +kx1 v1 w1 bm bp0 bp1 rnd nv Alh na
lhm sls odd torn ntorn Asl c1 c2 srl st fin
"""
SEQ = [S0, S1, S1, S3]

SCRATCH = {}


def _s(name, cols, dtype="float32", where="sbuf"):
    SCRATCH[name] = (where, [128, cols], dtype)


_s("R", WX, "bfloat16")
_s("X", W, "bfloat16")
_s("KI", W, "int32")
_s("K", WX)
_s("SN", L, "int32")
_s("IDX", W)
for _n in ("GO", "GA0", "GA1", "Y", "XR", "EQ"):
    _s(_n, 16 * L, "bfloat16")
for _n in ("KL", "AK0", "AK1"):
    _s(_n, L, "uint16")
_s("SZ", 3 * L, "float16")
LOG = {}


def _many(base, names, cols, dtype="float32"):
    _s(base, cols * len(names), dtype)
    for i, n in enumerate(names):
        LOG[n] = (base, cols * i, cols)


_TT = range(RO)
_TK = [(t, k) for t in range(RO) for k in range(2)]
_many("CLB", ["CL%d" % t for t in _TT], 16, "uint16")
_many("RQB", ["RQ%d%d" % x for x in _TK], 16, "uint16")
_many("RSB", ["RS%d%d" % x for x in _TK], L, "bfloat16")
_many("ASB", ["AS%d%d" % x for x in _TK], L, "bfloat16")
_many("TBF", ["TB%d" % t for t in _TT], L, "bfloat16")
_many("DGB", ["DN%d" % t for t in range(3)], 128, "float16")
_many("OFB", ["OFF%d" % t for t in _TT], 2, "uint16")
_many("ZER", ["XZ", "WF"], 96, "bfloat16")
for _n in ("CREP", "KCF", "SF", "SM", "TR", "ROT"):
    _s(_n, L, "float16")
for _n in ("KV", "RM", "XS", "SP", "HI", "GN"):
    _s(_n, L)
for _n in ("RCE", "RC", "UP", "NV", "MK0", "BM", "JF", "BF", "D", "NI"):
    _s(_n, L, "bfloat16")
_s("UV", 2 * L, "bfloat16")
for _n in ("IDH", "IDM", "IDS", "LH", "BDH", "PERM"):
    _s(_n, 128, "float16")
for _n in ("IDB", "BDS", "IDN", "SG1", "SGN", "RST"):
    _s(_n, 128, "bfloat16")
for _n in ("ZH", "Z16"):
    _s(_n, 144, "float16")
_s("ZB", 144, "bfloat16")
for _n in ("ZG", "ZP"):
    _s(_n, 48, "float16")
_s("C32", 32, "bfloat16")
_s("CH", 34, "float16")
_s("LWB", 16, "float16")
_s("BK", L + 8)
_s("SC", 128)
_s("SLF", 32)
for _n in ("ISN", "CSI"):
    _s(_n, 8)
for _n in ("GB16", "CST"):
    _s(_n, 8, "bfloat16")
for _n in ("PC", "PM"):
    _s(_n, 2, "int32")
for _n in ("PG", "PH", "PH2"):
    _s(_n, 1, "int32")
_s("PMF", 2)
for _n in ("PGF", "ZC", "RTC", "PHF", "PHG", "ZGC", "OBC"):
    _s(_n, 1)
for _n in ("N16", "C2", "RR"):
    _s(_n, 2, "bfloat16")
for _n in ("EXP", "SL", "NU"):
    _s(_n, 16, "uint16")
for _n in ("CW", "RND", "NEG", "NEW", "LT"):
    _s(_n, 16)
for _n in ("pZ", "pZ2", "pA", "pK", "pS", "pD", "pF", "pM"):
    _s(_n, 512, "float32", "psum")

SEMAPHORES = ["sv", "sa", "sp", "sq", "loc", "ldS", "ldK0", "ldK1", "ldR", "ldX", "stR", "stS"]
SEMAPHORES += ["rq%d%d" % x for x in _TK]
SEMAPHORES += ["rs%d%s_%s" % (t, w[1], w[3:].split("-")[0]) for t in _TT for w in SEQ[t].split() if w[:3] in ("s0:", "s1:")]


def rank_program(g, core, T, topo):
    rank = T.rank_of(core)
    if rank is None:
        return
    V, A, PE = g.vector, g.scalar, g.tensor
    eng = {"v": V, "a": A, "p": PE, "q": g, "s": g.sync}
    own = {"v": "sv", "a": "sa", "p": "sp", "q": "sq"}
    cnt = {"v": 0, "a": 0, "p": 0, "q": 0}
    known = {q: {} for q in eng}
    snap = {}
    res = {}

    def need(q, tok):
        s, n = tok
        if known[q].get(s, 0) >= n:
            return
        eng[q].wait_ge(T.sem[s], n)
        known[q][s] = n
        for s2, n2 in snap.get(tok, {}).items():
            if known[q].get(s2, 0) < n2:
                known[q][s2] = n2

    def entry(k):
        if k not in res:
            res[k] = {"w": None, "r": {}, "lw": {}}
        return res[k]

    def flat(keys):
        out = []
        for k in keys:
            out += k if isinstance(k, list) else [k]
        return out

    def deps(q, reads, writes):
        d = []
        for k in flat(reads):
            e = entry(k)
            if k[0] == "p":
                d += [tok for q2, tok in e["lw"].items() if not (q2 == q == "p")]
                d += [tok for q2, tok in e["r"].items() if q2 != q]
            elif e["w"]:
                d.append(e["w"])
        for k in flat(writes):
            e = entry(k)
            if k[0] == "p":
                for m in ("lw", "r"):
                    d += [tok for q2, tok in e[m].items() if not (q2 == q == "p")]
            else:
                if e["w"]:
                    d.append(e["w"])
                d += list(e["r"].values())
        best = {}
        for s, n in d:
            best[s] = max(best.get(s, 0), n)
        for s in best:
            need(q, (s, best[s]))

    def op(q, reads, writes, fn):
        deps(q, reads, writes)
        ins = fn()
        cnt[q] += 1
        tok = (own[q], cnt[q])
        ins.then_inc(T.sem[own[q]], 1)
        snap[tok] = dict(known[q])
        for k in flat(reads):
            entry(k)["r"][q] = tok
        for k in flat(writes):
            e = entry(k)
            if k[0] == "p":
                e["lw"][q] = tok
            else:
                e["w"] = tok
                e["r"] = {}
        return tok

    def landed(k, sem, n):
        entry(k)["w"] = (sem, n)

    def ts(o, i, s1, s2, op0, op1=None, rd=()):
        (on, oa), (inn, ia) = o, i
        if op1 is None:
            f = lambda: V.tensor_scalar(oa, ia, s1, None, op0)
        else:
            f = lambda: V.tensor_scalar(oa, ia, s1, s2, op0, op1)
        return op("v", [inn] + list(rd), [on], f)

    def tt(o, i0, i1, o0, rd=()):
        return op("v", [i0[0], i1[0]] + list(rd), [o[0]], lambda: V.tensor_tensor(o[1], i0[1], i1[1], o0))

    def cp(o, i, rd=()):
        return op("v", [i[0]] + list(rd), [o[0]], lambda: V.tensor_copy(o[1], i[1]))

    def scan(o, d0, d1, op0, op1):
        return op("v", [d0[0], d1[0]], [o[0]], lambda: V.tensor_tensor_scan(o[1], d0[1], d1[1], 0.0, op0, op1))

    def act(o, i, fn=Fn.Copy, rd=(), **kw):
        return op("a", [i[0]] + list(rd), [o[0]], lambda: A.activation(o[1], i[1], fn, **kw))

    def mms(bank, parts, rd):
        def f():
            last = None
            for (oa, l, r, st, sp) in parts:
                last = PE.matmul(oa, l, r, st, sp)
            return last
        return op("p", rd, [bank], f)

    def ap(name, lo=0, hi=None, step=None):
        base, o, n = LOG.get(name, (name, 0, SCRATCH[name][1][1] if name in SCRATCH else 0))
        return T[base][:, o + lo:o + (n if hi is None else hi):step]

    def b(name, lo=0, hi=None, key=None, step=None):
        return (key or name, ap(name, lo, hi, step))

    def by(name, lst, hi=None):
        return (name, ap(name, 0, hi).indirect(lst))

    def col(name, k=0):
        return T[name][:, k:k + 1]

    def cells(name, lo, hi):
        return ["%s.%d" % (name, c) for c in range(lo // CELL, (hi + CELL - 1) // CELL)]

    def iota(o, pattern, base, cm):
        kw = {} if SCRATCH[o[0].split(".")[0]][2] == "int32" else {"allow_small_or_imprecise_dtypes": True}
        return op("q", [], [o[0]], lambda: g.iota(o[1], pattern, base, cm, **kw))

    def fill(o, val):
        return op("v", [], [o[0]], lambda: V.memset(o[1], val))

    def copy(q):
        return cp if q == "v" else act

    g.sync.dma_start(T.SN[:], T.slips[:]).then_inc(T.sem.ldS, 16)
    for h in range(2):
        g.sync.dma_start(T.KI[:, W // 2 * h:W // 2 * (h + 1)], T.kin[:, W // 2 * h:W // 2 * (h + 1)]).then_inc(T.sem["ldK%d" % h], 16)
        landed("KI.%d" % h, "ldK%d" % h, 16)
    g.sync.dma_start(T.R[:, 0:W], T.rec[:]).then_inc(T.sem.ldR, 16)
    g.sync.dma_start(T.X[:], T.wealth[:]).then_inc(T.sem.ldX, 16)
    landed("SN", "ldS", 16)
    landed("R", "ldR", 16)
    landed("X", "ldX", 16)

    left = [0]

    def send(t, k, way, out, src, keys, sem, lands):
        dst, frm = (T.cores[(rank + w * (1 + (2 * t + k) % 7)) % NR] for w in (way, -way))
        rid, pid, _x = topo.addr(dst)
        deps("q", keys, [])
        g.remote_dma(out, src, T.sem[sem], T.sem.loc, pid, rid, topo.mask(core, dst))
        left[0] += len(topo.engines(core, dst))
        for c in lands:
            landed(c, sem, len(topo.engines(frm, core)))

    def send_list(t, k):
        send(t, k, 1, ap("RQ%d%d" % (t, k)), ap("CL%d" % t), ["CL%d" % t], "rq%d%d" % (t, k), ["RQ%d%d" % (t, k)])

    def send_lists(t):
        trs = []
        for k in range(2):
            dst, frm = (T.cores[(rank + w * (1 + (2 * t + k) % 7)) % NR] for w in (1, -1))
            es = topo.engines(core, dst)
            half = len(es) // 2
            rid, pid, _x = topo.addr(dst)
            trs.append(RemoteDMATransfer(dst_ids=[DstId(rid=rid, pnc=pid)], dma_engine_mask=sum(1 << e for e in es[k * half:(k + 1) * half]),
                                         remote_sem=T.sem["rq%d%d" % (t, k)], src=ap("CL%d" % t), dst=ap("RQ%d%d" % (t, k))))
            landed("RQ%d%d" % (t, k), "rq%d%d" % (t, k), len(topo.engines(frm, core)) // 2)
            left[0] += half
        deps("q", ["CL%d" % t], [])
        g.remote_dma_fused(trs, local_sem=T.sem.loc)

    def send_sums(t, k, lo, hi):
        rs, sums = "RS%d%d" % (t, k), "AS%d%d" % (t, k)
        send(t, k, -1, ap(rs, lo, hi), ap(sums, lo, hi), cells(sums, lo, hi), "rs%d%d_%d" % (t, k, lo), cells(rs, lo, hi))

    H = ("pS", T.pS[:, L:2 * L])
    CW = b("CW")

    def wrapped(out, z, src, n, start, fin):
        return [(out, T[z][:, 15 - j:143 - j], T[src][:, j:16 * n:16], start and j == 0, fin and j == 15) for j in range(16)]

    def turn(rows):
        parts = []
        for p in range(4):
            for x in range(16):
                for e in range(2):
                    lo = L - L * e + x
                    parts.append((T.pS[32 * p:32 * p + 32, L + x:2 * L:16], T.SZ[:, lo:lo + 2 * L - x:16], rows(2 * p + e), e == 0, e == 1))
        mms("pS", parts, ["SZ", "SZ.0", "SZ.2", "IDH"])

    def rot(j):
        return T.ROT[:, 8 * (5 * j % 16):8 * (5 * j % 16) + 128]

    ROT = ["ROT.0", "ROT.128"]

    def scaled(names):
        for nm, src, f in names:
            act(b(nm), b(src), Fn.Identity, scale=f)

    iota(b("PC", 0, 1, "PC.0"), [[0, 1]], 0, 1)
    iota(b("PC", 1, 2, "PC.1"), [[0, 1]], 0, 13)
    iota(b("D"), [[1, L]], 0, -1)
    iota(b("JF"), [[0, 16], [1, 16]], 0, 0)
    iota(b("CSI"), [[16, 4], [0, 2]], 16, 0)
    op("v", [], ["XZ", "WF"], lambda: V.memset(T.ZER[:], 0.0))
    fill(b("C32", 0, 16), 1.0 + 3.25 / 16.0)
    ts(b("PM"), b("PC", 0, 2, "PC.0"), 15, None, Op.bitwise_and, rd=["PC.1"])
    ts(b("PG"), b("PC", 0, 1, "PC.0"), 4, None, Op.arith_shift_right)
    fill(b("C32", 16, 32, "C32.1"), 0.7421875)
    ts(b("ZC"), b("PM", 0, 1), -1.0, 15.0, Op.mult, Op.add)
    cp(b("PMF"), b("PM"))
    ts(b("RTC"), b("PG"), -15.0, None, Op.mult)
    act(b("LWB"), b("D", 0, L, None, 16), Fn.Silu, scale=2.0, bias=float(W + L))
    ts(b("IDH"), b("D", 0, 128), 0.0, None, Op.is_equal)
    ts(b("ZH"), b("D", 0, 144), col("ZC"), None, Op.is_equal, rd=["ZC"])
    ts(b("RTC"), b("PMF", 0, 1), 7.0, col("RTC"), Op.mult, Op.add, rd=["RTC"])
    ts(b("MK0"), b("JF"), col("PMF", 1), None, Op.is_equal, rd=["PMF"])
    for lo in (0, 128):
        ts(b("ROT", lo, lo + 128, "ROT.%d" % lo), b("D", 0, 128), col("RTC"), None, Op.is_equal, rd=["RTC"])
    tt(b("SM"), b("SN"), b("MK0"), Op.mult)
    mms("pM", wrapped(T.pM[:, 0:16], "ZH", "SM", 16, True, True), ["ZH", "SM"])
    tt(b("BF"), b("JF"), b("D"), Op.subtract)
    act(b("SF"), b("SN"))
    act(b("SG1"), b("JF", 0, 128), Fn.Sign, scale=-1.0, bias=7.5)
    scaled((("SGN", "SG1", BIG),))
    ts(b("BDH"), b("BF", 0, 128), col("PMF"), None, Op.is_equal, rd=["PMF"])
    ts(b("UP"), b("JF"), col("PMF"), 4096.0, Op.is_le, Op.mult, rd=["PMF"])
    cp(b("CL0"), ("pM", T.pM[:, 0:16]))
    send_lists(0)

    mms("pK", [(T.pK[:, 0:L], T.BDH[:], T.SM[:], True, True)], ["BDH", "SM"])
    mms("pS", [(T.pS[:, L + 16 * j:L + 16 * j + 16], rot(j), T.SF[:, j::16], True, True) for j in range(16)], ROT + ["SF"])
    tt(b("BDS"), b("BDH"), b("SGN"), Op.mult)
    for x in (0, 2):
        ts(b("SZ", x * L, x * L + L, "SZ.%d" % x), b("MK0"), 0.0, None, Op.mult)
    scaled((("IDB", "IDH", 1.0), ("IDM", "IDH", -1.0), ("IDN", "IDH", -1.0)))
    act(CW, ("pM", T.pM[:, 0:16]))
    act(b("CREP"), ("pK", T.pK[:, 0:L]))
    act(b("SZ", L, 2 * L), H)
    turn(lambda q: T.IDH[:, q::8])

    def vector_constants():
        ts(b("OBC"), b("PMF", 0, 1), -16.0, col("D"), Op.mult, Op.subtract, rd=["D"])
        ts(b("ISN", 0, 4), b("JF", 0, 4), col("PMF"), None, Op.not_equal, rd=["PMF"])
        cp(b("PGF"), b("PG"))
        ts(b("ZGC"), b("PG"), -16.0, 16.0, Op.mult, Op.add)
        ts(b("TB0"), b("BF"), col("OBC"), 8.0, Op.is_equal, Op.mult, rd=["OBC"])
        ts(b("BM"), b("BF"), col("OBC"), BIG * BIG, Op.not_equal, Op.mult, rd=["OBC"])
        ts(b("GB16"), b("JF", 0, 8), col("PGF"), 16.0, Op.is_equal, Op.mult, rd=["PGF"])
        ts(b("ZP"), b("D", 0, 48), col("ZGC"), 4096.0, Op.is_equal, Op.mult, rd=["ZGC"])

    def late_constants():
        ts(b("PH"), b("PM", 0, 1), 8, None, Op.bitwise_and)
        ts(b("PH2"), b("PM", 0, 1), 7, None, Op.bitwise_and)
        ts(b("PHF"), b("PH"), 16.0, col("D"), Op.mult, Op.subtract, rd=["D"])
        ts(b("PHG"), b("PH2"), col("PGF"), None, Op.is_equal, rd=["PGF"])
        ts(b("EXP", 0, 8), ("D", T.D[:, 23:151:16]), col("PHF"), col("PHG"), Op.add, Op.mult, rd=["PHF", "PHG"])

    def scalar_constants():
        scaled((("ZG", "ZP", -1.0),))
        act(b("DN0"), b("IDH"), Fn.Identity, rd=["ISN"], scale=col("ISN", 0))

    def first_scalar_constants():
        scaled((("IDS", "IDH", 1.0 / 4096.0), ("ZB", "ZH", -1.0), ("Z16", "ZH", 1.0 / 16.0)))
        act(b("RST"), b("JF", 0, 128), Fn.Sign)
        act(b("CST"), b("CSI"), Fn.Identity, rd=["PMF"], bias=col("PMF"))
        act(b("OFF0"), b("PMF"))
        for o, n, x in ((b("N16"), 2, -16.0), (b("C2"), 2, -float(MOD)), (b("NEG"), 16, -1.0), (b("BK", 0, 8), 8, 0.0), (b("CH", 0, 2, "CH0"), 2, 0.0)):
            act(o, b("JF", 0, n), Fn.Identity, scale=0.0, bias=x)

    def round_constants(t):
        act(b("TB%d" % t), b("TB0"), Fn.Identity, scale=(8 + t) / 8.0)
        if t < RO - 1:
            act(b("DN%d" % t), b("IDH"), Fn.Identity, rd=["ISN"], scale=col("ISN", t))

    EVEN = 1.5 * 2.0 ** 20
    NA = b("XZ", 33, 64, None, 2)
    F0, F1 = ("pF", T.pF[:, 0:16]), ("pF", T.pF[:, 16:32])
    BUF = {"g0": ("GA0", "AK0"), "g1": ("GA1", "AK1"), "g2": ("GA1", "AK1"), "o": ("GO", "KL")}
    ABANK = (("pA", 0), ("pF", L), ("pD", 0))
    KEY = ("pK", "pA")
    ZBANK, PART = ("pZ", "pZ2"), ((0, ZS), (ZS, L))
    WF = ["WF", "WF.o", "WF.n", "WF.t"]

    def kin_gather(q, out, lst, lo, hi, t):
        l = ap(lst, lo // 16, hi // 16)
        src, x = ((["KI.0", "KI.1"], T.KI[:].indirect(l)), 0.25) if t == 0 else (by("K", l, W), 0.25 - KOFF)
        o = (cells(out, lo, hi), ap(out, lo, hi))
        if q == "a":
            act(o, src, Fn.Identity, rd=[lst], bias=x)
        else:
            ts(o, src, x, None, Op.add, rd=[lst])

    def over_bar(q, o, lst, keys, t):
        if q == "a":
            act(o, by("R", lst, W), Fn.Relu, rd=keys, bias=EPS - (5 + t))
        else:
            ts(o, by("R", lst, W), EPS - (5 + t), 0.0, Op.add, Op.max, rd=keys)

    def rec_piece(q, kind, lo, hi, t):
        G, lst = BUF[kind]
        over_bar(q, (cells(G, lo, hi), T[G][:, 16 * lo:16 * hi]), T[lst][:, lo:hi], cells(lst, lo, hi), t)

    def compare_lanes():
        for bb in range(15):
            ts(("EQ.%d" % bb, T.EQ[:, L * bb + 16 * bb + 16:L * bb + L]), ("CREP", T.CREP[:, 16 * bb + 16:L]), col("CW", bb), None, Op.is_equal, rd=["CW"])

    def best_piece(lo, hi):
        sl = slice(16 * lo, 16 * hi)
        tt((cells("Y", lo, hi), T.Y[:, sl]), by("X", T.KL[:, lo:hi]), (cells("XR", lo, hi), T.XR[:, sl]), Op.max, rd=cells("KL", lo, hi))

    def best_sum(lo, hi):
        bank, p0 = KEY[lo // 128], lo % 128
        parts = [(T[bank][:, 0:128], T.IDN[:], T.JF[:, 0:128], True, False)] if p0 == 0 else []
        for m in range(16):
            parts.append((T[bank][p0:p0 + hi - lo, m:128:16], T.Y[:, 16 * lo + m:16 * hi:16], T.GB16[:], False, m == 15))
        mms(bank, parts, cells("Y", lo, hi) + ["GB16", "IDN", "JF"])

    def best_steps(h):
        lo, hi = 128 * h, 128 * h + 128
        rm, ni = (b(n, lo, hi, "%s.%d" % (n, h)) for n in ("RM", "NI"))
        key, kin = (KEY[h], T[KEY[h]][:, 0:128]), (KEY[h], T[KEY[h]][:, 128:L])
        return {"rm%d" % h: lambda: scan(rm, b("RST"), key, Op.mult, Op.max),
                "ni%d" % h: lambda: tt(ni, rm, key, Op.subtract),
                "+kx%d" % h: lambda: mms(KEY[h], [(kin[1], T.KCF[:, lo:hi], T.IDS[:], True, False), (kin[1], T.IDN[:], ni[1], False, True)], ["KCF", "IDS", "IDN", ni[0]]),
                "bp%d" % h: lambda: scan(b("BK", 8 + lo, 8 + hi, "BK.%d" % h), ni, kin, Op.min, Op.max),
                "+kn%d" % h: lambda: mms(KEY[h], [(kin[1], T.KCF[:, lo:hi], T.IDS[:], True, True)], ["KCF", "IDS"]),
                "kx%d" % h: lambda: tt(kin, kin, ni, Op.subtract)}

    def double(q, s, lo, hi):
        st, keys = 8 >> s, cells("XR", lo, hi)
        o, i = T.XR[:, 16 * lo + st:16 * hi:2 * st], T.XR[:, 16 * lo:16 * hi:2 * st]
        if q == "q":
            op("q", [], keys, lambda: g.affine_select(o, i, [[0, (hi - lo) << s]], Op.is_ge, 0.0, 0, 0))
        else:
            copy(q)((keys, o), (keys, i))

    def one_round(t):
        last = t == RO - 1
        cl = "CL%d" % t
        off = ap("OFF%d" % t, 0, 1)
        words = SEQ[t].split()
        done = []

        def into_sums(lo, hi, parts, rd, start=False, fin=False):
            for bank, (a, z) in zip(ZBANK, PART):
                a, z = max(a, lo), min(z, hi)
                if a < z:
                    ps = parts(T[bank], a, z)
                    mms(bank, [(o, l, r, start, fin) for o, l, r in ps], rd)

        def rec_sum(kind, lo, hi):
            G = BUF[kind][0]
            if kind == "o":
                into_sums(lo, hi, lambda p, a, z: [(p[:, a:z], T.IDB[:], T.GO[:, 16 * a + m:16 * z:16]) for m in range(16)], cells(G, lo, hi) + ["IDB"])
            else:
                bank, c0 = ABANK[int(kind[1])]
                mms(bank, [(T[bank][:, c0 + lo:c0 + hi], T.IDB[:], T[G][:, 16 * lo + m:16 * hi:16], m == 0, m == 15) for m in range(16)], cells(G, lo, hi) + ["IDB"])

        def count_lanes():
            for bb in range(15):
                into_sums(16 * bb + 16, L, lambda p, a, z: [(p[:, a:z], T.BDS[:], T.EQ[:, L * bb + a:L * bb + z])], ["EQ.%d" % bb, "BDS"])

        def own_bags():
            parts = [(T.pD[:, 0:L], T.IDB[:], T.UP[:], True, False)] + [(T.pD[:, j:L:16], T.IDH[:], T.CH[:, 2:18], False, j == 15) for j in range(16)]
            mms("pD", parts, ["IDB", "UP", "IDH", "CH"])

        def part_steps(h):
            lo, hi = PART[h]
            z = (ZBANK[h], T[ZBANK[h]][:, lo:hi])
            fin = max(words.index("an%d%d" % (k, h)) for k in range(2))

            def answer(k):
                rs = "RS%d%d" % (t, k)
                into_sums(lo, hi, lambda p, a, z: [(p[:, a:z], T.IDB[:], ap(rs, a, z))], ["IDB"] + cells(rs, lo, hi), fin=words[fin] == "an%d%d" % (k, h))

            return {"an0%d" % h: lambda: answer(0), "an1%d" % h: lambda: answer(1),
                    "w%d" % h: lambda: ts(b("UV", lo, hi, "U.%d" % h), z, 0.7, 1.0 / 16.0, Op.is_lt, Op.mult),
                    "v%d" % h: lambda: tt(b("UV", L + lo, L + hi, "V.%d" % h), z, b("BM", lo, hi), Op.is_gt)}

        def kin_moves():
            parts = [(T.pM[:, 128:128 + L], ap("DN%d" % t), T.KCF[:], True, False)]
            parts += [(T.pM[:, 128 + e:128 + L:2], T.Z16[:, 15 - t:143 - t], T.CREP[:, 1 - e::2], False, e == 1) for e in range(2)]
            mms("pM", parts, ["DN%d" % t, "Z16", "KCF", "CREP"])

        def new_records():
            u = t if done[-1] == "srl" else t - 1
            if "nvr" in SEQ[u].split():
                op("v", ["NV", "SL"], ["R"], lambda: V.tensor_copy(T.R[:].indirect(T.SL[:]), T.NV[:]))
            else:
                op("v", ["NV", "TB%d" % u, "SL"], ["R"], lambda: V.tensor_tensor(T.R[:].indirect(T.SL[:]), T.NV[:], ap("TB%d" % u), Op.add))

        def evacuate(q, k, lo, hi):
            bank, c0 = ABANK[k]
            sums = "AS%d%d" % (t, min(k, 1))
            copy(q)((cells(sums, lo, hi), ap(sums, lo, hi)), (bank, T[bank][:, c0 + lo:c0 + hi]))

        def citizens():
            c, before = T.CH[:, 2:18], T.CH[:, 1:17]
            mms("pS", [(T.pS[:, 0:128], T.IDH[:], T.SZ[:, 0:128], True, False), (T.pS[:, 0:64:4], T.IDH[:], before, False, False),
                       (T.pS[:, 2:64:4], T.IDM[:], c, False, False), (T.pS[:, 3:64:4], T.IDH[:], c, False, False), (T.pS[:, 64:128:4], T.IDM[:], c, False, False)],
                ["IDH", "IDM", "CH", "CH0", "SZ.0"])
            mms("pM", [(T.pM[:, 0:32:2], T.IDH[:], T.LWB[:], True, False), (T.pM[:, 0:32:2], T.IDM[:], c, False, False), (T.pM[:, 1:32:2], T.IDH[:], c, False, True)],
                ["IDH", "IDM", "CH", "LWB"])

        def place_addends():
            mms("pD", [(T.pD[:, L:L + 2], T.IDB[:], T.CST[:, 2 * t:2 * t + 2], True, False), (T.pD[:, L:L + 2], T.IDB[:], T.C2[:], False, False)],
                ["IDB", "CST", "C2"])

        def best_wrapped():
            parts = []
            for z, lo in (("ZG", 0), ("ZP", 2), ("ZP", 64)):
                parts += [(T.pS[32 * (x // 2):32 * (x // 2) + 32, lo:lo + 62:4], T[z][:, 16 - 16 * (x % 2):48 - 16 * (x % 2)], T.LH[:, 16 * x:16 * x + 16],
                           False, lo == 64 and x % 2 == 1) for x in range(8)]
            mms("pS", parts, ["LH", "ZG", "ZP"])

        def permutation():
            if t == RO - 2:
                mms("pM", [(T.pM[:, 384:512], rot(0), T.IDH[:], True, True)], ROT + ["IDH"])
                act(b("PERM"), ("pM", T.pM[:, 384:512]))

        def store_records():
            deps("a", ["R"], [])
            A.dma_start(T.yr[:], T.R[:, 0:W]).then_inc(T.sem.stR, 16)

        P1, P2 = b("SC", 3, 64, "SC.1", 4), b("SC", 67, 128, "SC.2", 4)

        def finish():
            tt(b("NEW"), P1, P2, Op.add)
            cp(b("NU"), b("NEW"))
            tt(b("GN"), by("IDX", T.NU[:]), b("HI"), Op.min, rd=["NU"])
            tt(b("XS"), b("GN"), H, Op.max)
            deps("s", ["XS"], [])
            g.sync.dma_start(T.ys[:], T.XS[:]).then_inc(T.sem.stS, 16)

        best_list = ["EXP", "BK.0", "BK.1", "BK"]
        either = {
            "kcf": lambda q: copy(q)(b("KCF"), (cells("KL", 0, L), T.KL[:])),
            "crep": lambda q: copy(q)(b("CREP"), by("IDX", ap(cl)), rd=[cl]),
            "xr": lambda q: copy(q)((cells("XR", 0, L), T.XR[:, 0::16]), by("X", ap(cl)), rd=[cl]),
            "rce": lambda q: over_bar(q, b("RCE"), ap(cl), [cl], t),
            "k0": lambda q: act(b("K", 0, W // 2), b("KI", 0, W // 2, "KI.0"), Fn.Identity, bias=KOFF),
            "k1": lambda q: act(b("K", W // 2, W), b("KI", W // 2, W, "KI.1"), Fn.Identity, bias=KOFF),
            "sz": lambda q: copy(q)(b("SZ", L, 2 * L), b("SP")),
            "sl": lambda q: copy(q)(b("SL"), b("SLF", 1, 32, None, 2)),
            "lh": lambda q: copy(q)(b("LH"), by("BK", T.EXP[:, 0:8]), rd=best_list),
        }
        step = {
            "cC": vector_constants,
            "cD": late_constants,
            "aC": scalar_constants,
            "aC0": first_scalar_constants,
            "rcs": lambda: round_constants(t + 1),
            "perm": permutation,
            "idx": lambda: iota(b("IDX"), [[1, W]], 0, 0),
            "spc": lambda: act(b("SP"), H),
            "sr": new_records,
            "cw": lambda: act(CW, by("SP", off), rd=["OFF%d" % t]),
            "ch": lambda: act(b("CH", 2, 18), CW),
            "+kcf": kin_moves,
            "cmp": compare_lanes,
            "+cmp": count_lanes,
            "+ob": own_bags,
            "cmd": lambda: tt(b("EQ", 15 * L, 16 * L, "EQ.15"), b("CREP"), ("pD", T.pD[:, 0:L]), Op.is_equal),
            "+cmd": lambda: into_sums(0, L, lambda p, a, z: [(p[:, a:z], T.BDS[:], T.EQ[:, 15 * L + a:15 * L + z])], ["EQ.15", "BDS"]),
            "+rce": lambda: into_sums(0, L, lambda p, a, z: [(p[:, a:z], T.IDB[:], T.RCE[:, a:z])], ["IDB", "RCE"], start=True),
            "bm": lambda: mms("pF", [(T.pF[:, 0:32], T.IDB[:], T.C32[:], True, False)] + wrapped(T.pF[:, 0:32], "ZB", "UV", 32, False, True),
                              ["IDB", "C32", "C32.1", "ZB", "U.0", "V.0", "U.1", "V.1"]),
            "neg": lambda: op("v", ["NEG", "OFF%d" % t], ["SP"], lambda: V.tensor_copy(T.SP[:].indirect(off), T.NEG[:])),
            "+sz": lambda: turn(lambda q: T.IDH[:, 16 * q:16 * q + 16]),
            "tr": lambda: act(b("TR"), H),
            "+tr": lambda: mms("pS", [(T.pS[:, L + j:2 * L:16], rot(-j), T.TR[:, 16 * j:16 * j + 16], True, True) for j in range(16)], ROT + ["TR"]),
            "sf": lambda: act(b("SF"), H),
            "+sf": lambda: mms("pS", [(H[1], T.PERM[:], T.SF[:], True, True)], ["PERM", "SF"]),
            "hi": lambda: act(b("HI"), H, Fn.Relu, scale=-4096.0),
            "kv": lambda: act(b("KV"), ("pM", T.pM[:, 128:128 + L]), Fn.Identity, bias=KOFF),
            "nvr": lambda: tt(b("NV"), by("R", ap(cl), W), b("TB%d" % t), Op.max, rd=[cl]),
            "rc": lambda: act(b("RC"), by("R", ap(cl), W), rd=[cl]),
            "+nv": lambda: mms("pM", [(T.pM[:, 128:128 + L], T.IDB[:], T.RC[:], True, False), (T.pM[:, 128:128 + L], T.IDN[:], ap("TB%d" % t), False, True)],
                               ["IDB", "IDN", "RC", "TB%d" % t]),
            "nv": lambda: act(b("NV"), ("pM", T.pM[:, 128:128 + L]), Fn.Relu),
            "cm": citizens,
            "cn": place_addends,
            "lhm": best_wrapped,
            "rnd": lambda: ts(b("RND"), F0, EVEN, -EVEN, Op.add, Op.add),
            "na": lambda: tt(NA, b("RND"), F1, Op.is_ge),
            "odd": lambda: tt(b("WF", 5, 69, "WF.o", 4), F0, b("RND"), Op.is_gt, rd=["WF"]),
            "torn": lambda: tt(b("WF", 3, 64, "WF.t", 4), b("RND"), NA, Op.is_ge, rd=["WF"]),
            "ntorn": lambda: tt(b("WF", 6, 70, "WF.n", 4), b("RND"), NA, Op.is_lt, rd=["WF"]),
            "sls": lambda: scan(b("SLF"), b("XZ", 32, 64), ("pM", T.pM[:, 0:32]), Op.mult, Op.add),
            "ks": lambda: op("a", ["KV", "SL"], ["K"], lambda: A.activation(T.K[:].indirect(T.SL[:]), T.KV[:], Fn.Silu)),
            "srl": new_records,
            "st": store_records,
            "naa": lambda: mms("pD", [(T.pD[32 * p:32 * p + 32, L:L + 2], ap("XZ", 33 - 32 * e, 96 - 32 * e, 2), T.N16[:], False, e == 1) for p in range(4) for e in range(2)],
                               ["XZ", "N16"]),
            "rrv": lambda: ts(b("RR", 0, 1), ("pD", T.pD[:, L:L + 1]), -1.0, 127.5, Op.mult, Op.add),
            "offv": lambda: ts(b("OFF%d" % (t + 1), 0, 1), ("pD", T.pD[:, L + 1:L + 2]), col("RR"), None, Op.add, rd=["RR"]),
            "off": lambda: [act(b("RR", 0, 1), ("pD", T.pD[:, L:L + 1]), Fn.Identity, scale=-1.0, bias=127.5),
                            act(b("OFF%d" % (t + 1), 0, 1), ("pD", T.pD[:, L + 1:L + 2]), Fn.Identity, rd=["RR"], bias=col("RR"))],
            "c1": lambda: scan(b("SC", 0, 64, "SC.1"), (WF, ap("WF", 0, 64)), ("pS", T.pS[:, 0:64]), Op.mult, Op.add),
            "c2": lambda: scan(b("SC", 64, 128, "SC.2"), (WF, ap("WF", 4, 68)), ("pS", T.pS[:, 64:128]), Op.mult, Op.add),
            "sp": lambda: op("v", ["SC.1", "SC.2", "OFF%d" % t], ["SP"], lambda: V.tensor_tensor(T.SP[:].indirect(off), P1[1], P2[1], Op.add)),
            "cl": lambda: cp(b("CL%d" % (t + 1)), by("SP", ap("OFF%d" % (t + 1), 0, 1)), rd=["OFF%d" % (t + 1)]),
            "cla": lambda: act(b("CL%d" % (t + 1)), by("SP", ap("OFF%d" % (t + 1), 0, 1)), rd=["OFF%d" % (t + 1)]),
            "l0": lambda: send_list(t + 1, 0),
            "l1": lambda: send_list(t + 1, 1),
            "lf": lambda: send_lists(t + 1),
            "fin": finish,
        }
        for h in range(2):
            step.update(best_steps(h))
            if PART[h][0] < L:
                step.update(part_steps(h))

        for word in words:
            done.append(word)
            q = {"V": "v", "A": "a", "G": "q", "+": "p"}.get(word[0])
            kind, _x, span = (word[1:] if q else word).partition(":")
            if not span:
                either[kind](q) if q in ("v", "a") else step[word]()
                continue
            lo, hi = (int(x) for x in span.split("-"))
            if q == "p":
                best_sum(lo, hi) if kind == "y" else rec_sum(kind, lo, hi)
            elif kind == "y":
                best_piece(lo, hi)
            elif kind in BUF:
                rec_piece(q, kind, lo, hi, t)
            elif kind == "kl":
                kin_gather(q, "KL", cl, lo, hi, t)
            elif kind[0] == "a":
                kin_gather(q, "AK" + kind[2], "RQ%d%s" % (t, kind[2]), lo, hi, t)
            elif kind[0] == "e":
                evacuate(q, int(kind[1]), lo, hi)
            elif kind[0] == "s":
                send_sums(t, int(kind[1]), lo, hi)
            else:
                double(q, int(kind[1]), lo, hi)

    for t in range(RO):
        one_round(t)

    g.wait_ge(T.sem.loc, left[0])
    A.wait_ge(T.sem.stR, 16)
    g.sync.wait_ge(T.sem.stS, 16)
    for q in ("v", "a", "p", "q"):
        g.wait_ge(T.sem[own[q]], cnt[q])
